import numpy as np
import ml_dtypes


def mxq(x, axis, fmt="e4m3"):
    dtype, down = {"e4m3": (ml_dtypes.float8_e4m3fn, 7), "e5m2": (ml_dtypes.float8_e5m2, 14)}[fmt]
    v = np.moveaxis(np.asarray(x, np.float32).astype(ml_dtypes.bfloat16).astype(np.float64), axis, -1)
    blocks = v.reshape(v.shape[:-1] + (-1, 32))
    amax = np.abs(blocks).max(-1, keepdims=True)
    byte = np.maximum(np.where(amax > 0, np.frexp(amax)[1] - 1 + 127, 0) - down, 1)
    scale = np.exp2(byte - 127.0)
    codes = (blocks / scale).astype(np.float32).astype(dtype).astype(np.float64)
    return np.moveaxis((codes * scale).reshape(v.shape), -1, axis)


WIDE = False


def mx_kscale(k):
    if not WIDE:
        return np.ones(k)
    levels = np.array([18, -18])
    if k % 512:
        return np.exp2(np.random.permutation(np.resize(levels, k // 32))).repeat(32)
    a = np.empty((k // 512, 16))
    for p in range(k // 512):
        a[p, :8] = np.random.permutation(np.resize(levels, 8))
        for g in range(8):
            far = levels[np.abs(levels - a[p, g]) >= 10]
            a[p, g + 8] = far[np.random.randint(len(far))]
    return np.exp2(a.ravel()).repeat(32)


def f64(x):
    return np.asarray(x).astype(np.float64)


def striped(idx):
    return np.tile(np.asarray(idx).reshape(-1, 16).T, (8, 1)).astype(np.uint16)


def unstriped(offs):
    return offs[:16].T.reshape(-1).astype(np.int64)


B, N, T, D, R = 2, 512, 2048, 512, 512


def setup_inputs():
    n = np.random.standard_normal
    idx = np.random.permutation(T)[:B * N]
    s = mx_kscale(D)[:, None]
    z = mx_kscale(R)[:, None]
    x = n((B, D, R))
    return {
        "xT": (x * s).astype(np.float32),
        "wT": (n((D, T)) * (1.00 / np.sqrt(D)) / s).astype(np.float32),
        "y": np.random.randint(0, 2, (B, R, N)).astype(np.float32),
        "wt": (np.random.uniform(0.5, 1.5, (B, R, 1)) * 1.0 / np.sqrt(R) * z).astype(np.float32),
        "kb": np.tile(0.5 * n(T), (128, 1)).astype(np.float32),
        "xm": (x.transpose(0, 2, 1) / z).astype(np.float32),
        "offs": striped(idx),
    }


def reference(xT, wT, y, wt, kb, xm, offs):
    idx = unstriped(offs)
    pick = lambda x: x[:, idx].reshape(x.shape[0], B, N).transpose(1, 0, 2)
    a = mxq(f64(xT), 1, "e4m3").transpose(0, 2, 1) @ mxq(pick(f64(wT)), 1, "e4m3")
    a = a + pick(f64(kb))[:, :1, :]
    g = f64(wt) * (1.0 / (1.0 + np.exp(-a)) - f64(y))
    dw = mxq(f64(xm), 1, "e4m3").transpose(0, 2, 1) @ mxq(g, 1, "e5m2")
    gw = np.zeros((D, T))
    gw[:, idx] = dw.transpose(1, 0, 2).reshape(D, B * N)
    return gw

@@ -1,0 +1,216 @@
+from contextlib import ExitStack
+
+import concourse.mybir as mybir
+from concourse.masks import make_identity
+
+B, N, T, D, R = 2, 512, 2048, 512, 512
+FLOPS = 2 * 2 * B * N * D * R
+
+F32 = mybir.dt.float32
+BF16 = mybir.dt.bfloat16
+U32 = mybir.dt.uint32
+U16 = mybir.dt.uint16
+U8 = mybir.dt.uint8
+E4M3 = mybir.dt.float8_e4m3fn_x4
+E5M2 = mybir.dt.float8_e5m2_x4
+SIGMOID = mybir.ActivationFunctionType.Sigmoid
+COPY = mybir.ActivationFunctionType.Copy
+MULT = mybir.AluOpType.mult
+SUB = mybir.AluOpType.subtract
+
+P = 128
+PACK = 4
+BLK = 128
+LANES = 16
+
+
+def tile_attend_gnce_w_kb_kernel(tc, xT, wT, y, wt, kb, xm, offs, out):
+    nc = tc.nc
+    with ExitStack() as ctx:
+        keep = ctx.enter_context(tc.tile_pool(name="keep", bufs=1))
+        ring = ctx.enter_context(tc.tile_pool(name="ring", bufs=4))
+        psum = ctx.enter_context(tc.psum_pool(name="psum", bufs=4))
+
+        offsets = keep.tile([P, B * N // LANES], U16, name="offsets")
+        nc.sync.dma_start(offsets[:], offs)
+
+        def listed(first, count):
+            return offsets[:, first // LANES : (first + count) // LANES]
+
+        kb_row = keep.tile([P, T], F32, name="kb_row")
+        nc.vector.memset(kb_row[:], 0.0)
+        warm = keep.tile([P, 1], F32, name="warm")
+        nc.scalar.activation(warm[:], kb_row[:, 0:1], SIGMOID)
+        nc.scalar.dma_start(kb_row[0:1, :], kb[0:1, :])
+        weight = []
+        for b in range(B):
+            w_b = keep.tile([P, PACK], F32, name=f"weight{b}")
+            nc.scalar.dma_start(w_b[:], wt[b].rearrange("(p t) o -> p (t o)", t=PACK))
+            weight.append(w_b)
+        ident = keep.tile([P, P], F32, name="ident")
+        make_identity(nc, ident[:])
+
+        def load(src, name):
+            raw = keep.tile([P, PACK, src.shape[1]], F32, name=name)
+            nc.sync.dma_start(raw[:], src.rearrange("(p t) c -> p t c", t=PACK))
+            return raw
+
+        planes = []
+        for t in range(PACK):
+            if t == 2:
+                x_raw = [load(xT[0], "x_raw0")]
+            plane = keep.tile([P, T], F32, name=f"plane{t}")
+            width = T // 2 if t < 2 else T
+            for c0 in range(0, T, width):
+                nc.sync.dma_start(
+                    plane[:, c0 : c0 + width], wT.rearrange("(p t) c -> p t c", t=PACK)[:, t, c0 : c0 + width]
+                )
+            planes.append(plane)
+        y_raw = [load(y[0], "y_raw0")]
+        xm_raw = [load(xm[0], "xm_raw0")]
+        x_raw.append(load(xT[1], "x_raw1"))
+        y_raw.append(load(y[1], "y_raw1"))
+        xm_raw.append(load(xm[1], "xm_raw1"))
+
+        out_tiles = []
+        for j in range(D // BLK):
+            o = keep.tile([P, T], F32, name=f"out{j}")
+            nc.vector.memset(o[:], 0.0)
+            out_tiles.append(o)
+
+        w_listed = [keep.tile([P, PACK, N], F32, name=f"w_listed{b}") for b in range(B)]
+
+        def gather(b, t, c0, c1):
+            nc.vector.tensor_copy(w_listed[b][:, t, c0:c1], planes[t][:].indirect(listed(b * N + c0, c1 - c0)))
+
+        for t in range(2):
+            for b in range(B):
+                gather(b, t, 0, N)
+
+        kb_listed = keep.tile([P, B * N], F32, name="kb_listed")
+        nc.vector.tensor_copy(kb_listed[:], kb_row[:].indirect(offsets[:]))
+        bias = keep.tile([P, B * N // BLK], F32, name="bias")
+        for b in range(B):
+            bank = psum.tile([P, N // BLK, BLK], F32, name="bank", tag="turned")
+            for j in range(N // BLK):
+                c0 = b * N + j * BLK
+                nc.tensor.transpose(bank[:, j, :], kb_listed[:, c0 : c0 + BLK], ident[:])
+            nc.scalar.copy(bias[:, b * 4 : (b + 1) * 4], bank[:, :, 0])
+
+        def operand(name):
+            grouped = keep.tile([P, N, PACK], BF16, name=name + "_grouped", align_bytes=64)
+            codes = keep.tile([P, N], U32, name=name + "_codes", align_bytes=64)
+            scales = keep.tile([P, N], U8, name=name + "_scales", align_bytes=64)
+            return grouped, codes, scales
+
+        def by_lines(ap, order):
+            return ap.rearrange(order + " -> p c t i", i=4)
+
+        def interleave(engine_copy, op, raw, c0, c1):
+            engine_copy(by_lines(op[0][:, c0:c1, :], "p (c i) t"), by_lines(raw[:, :, c0:c1], "p t (c i)"))
+
+        def quantize(op, c0, c1, fmt):
+            nc.vector.quantize_mx(
+                out=op[1][:, c0:c1].bitcast(fmt),
+                scales=op[2][:, c0:c1],
+                in_=op[0][:, c0:c1, :].rearrange("p c t -> p (c t)"),
+            )
+
+        def product(bank, lhs, c0, lhs_fmt, rhs, rhs_fmt):
+            nc.tensor.matmul_mx(
+                out=bank[:],
+                lhsT=lhs[1][:, c0 : c0 + BLK].bitcast(lhs_fmt),
+                lhsT_scale=lhs[2][:, c0 : c0 + BLK],
+                rhs=rhs[1][:].bitcast(rhs_fmt),
+                rhs_scale=rhs[2][:],
+                start=True,
+                stop=True,
+            )
+
+        H = N // 2
+        grads = []
+        for b in range(B):
+            x_op, w_op, g_op, xm_op = operand(f"x{b}"), operand(f"w{b}"), operand(f"g{b}"), operand(f"xm{b}")
+            interleave(nc.scalar.copy, x_op, x_raw[b], 0, R)
+            quantize(x_op, 0, R, E4M3)
+            if b == 0:
+                gather(0, 2, 0, N)
+                gather(0, 3, 0, H)
+                gather(0, 3, H, N)
+                interleave(nc.scalar.copy, w_op, w_listed[0], 0, H)
+                interleave(nc.vector.tensor_copy, w_op, w_listed[0], H, N)
+                quantize(w_op, H, N, E4M3)
+                quantize(w_op, 0, H, E4M3)
+                order = [2, 3, 0, 1]
+            else:
+                interleave(nc.scalar.copy, w_op, w_listed[1], 0, N)
+                quantize(w_op, 0, N, E4M3)
+                order = [0, 1, 2, 3]
+            turned = {}
+            if b == 1:
+                by_t = [psum.tile([P, N], F32, name="bank", tag="turned") for t in range(PACK)]
+                for t in range(PACK):
+                    nc.scalar.activation(y_raw[1][:, t, :], y_raw[1][:, t, :], COPY, scale=weight[1][:, t : t + 1])
+            for j in order:
+                scores = psum.tile([P, R], F32, name="scores", tag="products")
+                product(scores, w_op, j * BLK, E4M3, x_op, E4M3)
+                prob = ring.tile([P, PACK, BLK], F32, name="prob")
+                nc.scalar.activation(
+                    prob[:], scores[:].rearrange("p (m t) -> p t m", t=PACK), SIGMOID,
+                    bias=bias[:, b * 4 + j : b * 4 + j + 1],
+                )
+                if b == 1:
+                    for t in range(PACK):
+                        nc.tensor.transpose(by_t[t][:, j * BLK : (j + 1) * BLK], prob[:, t, :], ident[:])
+                    continue
+                bank = psum.tile([P, PACK, BLK], F32, name="bank", tag="turned")
+                for t in range(PACK):
+                    nc.tensor.transpose(bank[:, t, :], prob[:, t, :], ident[:])
+                turned[j] = bank
+            if b == 1:
+                weighted = keep.tile([P, PACK, N], F32, name="weighted", tag="w_listed0")
+                for t in range(PACK):
+                    nc.scalar.activation(weighted[:, t, :], by_t[t][:], COPY, scale=weight[1][:, t : t + 1])
+                nc.vector.tensor_tensor(
+                    by_lines(g_op[0][:], "p (c i) t"), by_lines(weighted[:], "p t (c i)"),
+                    by_lines(y_raw[1][:], "p t (c i)"), SUB,
+                )
+                order = []
+            wide = weight[b][:].unsqueeze(1).unsqueeze(3).to_broadcast([P, BLK // 4, PACK, 4])
+            diffs = {}
+            for step in range(len(order) + 1 if order else 0):
+                if step < len(order):
+                    j = order[step]
+                    diff = ring.tile([P, PACK, BLK], F32, name="diff")
+                    nc.vector.tensor_tensor(diff[:], turned[j][:], y_raw[b][:, :, j * BLK : (j + 1) * BLK], SUB)
+                    diffs[j] = diff
+                if step > 0:
+                    j = order[step - 1]
+                    nc.vector.tensor_tensor(
+                        by_lines(g_op[0][:, j * BLK : (j + 1) * BLK, :], "p (c i) t"),
+                        by_lines(diffs[j][:], "p t (c i)"), wide, MULT,
+                    )
+            for j in range(D // BLK):
+                interleave(nc.scalar.copy, xm_op, xm_raw[b], j * BLK, (j + 1) * BLK)
+            first = order[0] * BLK if order else 0
+            quantize(g_op, first, first + H, E5M2)
+            quantize(xm_op, 0, H, E4M3)
+            quantize(g_op, H - first, N - first, E5M2)
+            quantize(xm_op, H, D, E4M3)
+            grad = []
+            for j in range(D // BLK):
+                bank = psum.tile([P, N], F32, name="dw", tag="products")
+                product(bank, xm_op, j * BLK, E4M3, g_op, E5M2)
+                dw = keep.tile([P, N], F32, name=f"dw{b}_{j}")
+                nc.scalar.copy(dw[:], bank[:])
+                grad.append(dw)
+            grads.append(grad)
+            if b == 0:
+                for t in range(2, PACK):
+                    gather(1, t, 0, N)
+
+        for b in range(B):
+            for j in range(D // BLK):
+                nc.vector.tensor_copy(out_tiles[j][:].indirect(listed(b * N, N)), grads[b][j][:])
+                if b == B - 1:
+                    nc.sync.dma_start(out[j * BLK : (j + 1) * BLK, :], out_tiles[j][:])

@@ -22,6 +22,7 @@ P = 128
 PACK = 4
 BLK = 128
 LANES = 16
+KB_ROW = 96
 
 
 def tile_attend_gnce_w_kb_kernel(tc, xT, wT, y, wt, kb, xm, offs, out):
@@ -38,36 +39,34 @@ def tile_attend_gnce_w_kb_kernel(tc, xT, wT, y, wt, kb, xm, offs, out):
             return offsets[:, first // LANES : (first + count) // LANES]
 
         kb_row = keep.tile([P, T], F32, name="kb_row")
-        nc.vector.memset(kb_row[:], 0.0)
-        warm = keep.tile([P, 1], F32, name="warm")
-        nc.scalar.activation(warm[:], kb_row[:, 0:1], SIGMOID)
-        nc.scalar.dma_start(kb_row[0:1, :], kb[0:1, :])
+        nc.gpsimd.memset(kb_row[0:KB_ROW, :], 0.0)
+        nc.sync.dma_start(kb_row[KB_ROW:P, :], kb[KB_ROW:P, :])
         weight = []
         for b in range(B):
             w_b = keep.tile([P, PACK], F32, name=f"weight{b}")
             nc.scalar.dma_start(w_b[:], wt[b].rearrange("(p t) o -> p (t o)", t=PACK))
             weight.append(w_b)
+        warm = keep.tile([P, 1], F32, name="warm")
+        nc.scalar.activation(warm[:], weight[0][:, 0:1], SIGMOID)
         ident = keep.tile([P, P], F32, name="ident")
         make_identity(nc, ident[:])
 
-        def load(src, name):
+        def load(src, name, pieces=1):
             raw = keep.tile([P, PACK, src.shape[1]], F32, name=name)
-            nc.sync.dma_start(raw[:], src.rearrange("(p t) c -> p t c", t=PACK))
+            rows = src.rearrange("(p t) c -> p t c", t=PACK)
+            width = src.shape[1] // pieces
+            for c0 in range(0, src.shape[1], width):
+                nc.sync.dma_start(raw[:, :, c0 : c0 + width], rows[:, :, c0 : c0 + width])
             return raw
 
         planes = []
         for t in range(PACK):
-            if t == 2:
-                x_raw = [load(xT[0], "x_raw0")]
             plane = keep.tile([P, T], F32, name=f"plane{t}")
-            width = T // 2 if t < 2 else T
-            for c0 in range(0, T, width):
-                nc.sync.dma_start(
-                    plane[:, c0 : c0 + width], wT.rearrange("(p t) c -> p t c", t=PACK)[:, t, c0 : c0 + width]
-                )
+            nc.sync.dma_start(plane[:], wT.rearrange("(p t) c -> p t c", t=PACK)[:, t, :])
             planes.append(plane)
-        y_raw = [load(y[0], "y_raw0")]
+        x_raw = [load(xT[0], "x_raw0", 2)]
         xm_raw = [load(xm[0], "xm_raw0")]
+        y_raw = [load(y[0], "y_raw0", 2)]
         x_raw.append(load(xT[1], "x_raw1"))
         y_raw.append(load(y[1], "y_raw1"))
         xm_raw.append(load(xm[1], "xm_raw1"))
@@ -75,17 +74,19 @@ def tile_attend_gnce_w_kb_kernel(tc, xT, wT, y, wt, kb, xm, offs, out):
         out_tiles = []
         for j in range(D // BLK):
             o = keep.tile([P, T], F32, name=f"out{j}")
-            nc.vector.memset(o[:], 0.0)
+            nc.gpsimd.memset(o[:], 0.0)
             out_tiles.append(o)
 
-        w_listed = [keep.tile([P, PACK, N], F32, name=f"w_listed{b}") for b in range(B)]
+        w_pairs = keep.tile([P, 2, B * N, 2], BF16, name="w_pairs")
 
-        def gather(b, t, c0, c1):
-            nc.vector.tensor_copy(w_listed[b][:, t, c0:c1], planes[t][:].indirect(listed(b * N + c0, c1 - c0)))
+        def gather(t, c0, c1):
+            nc.vector.tensor_copy(w_pairs[:, t // 2, c0:c1, t % 2], planes[t][:].indirect(listed(c0, c1 - c0)))
 
-        for t in range(2):
-            for b in range(B):
-                gather(b, t, 0, N)
+        def join_pairs(engine_copy, op, b, c0, c1):
+            engine_copy(
+                op[0][:, c0:c1, :].rearrange("p c (u e) -> p c u e", e=2),
+                w_pairs[:, :, b * N + c0 : b * N + c1, :].rearrange("p u c e -> p c u e"),
+            )
 
         kb_listed = keep.tile([P, B * N], F32, name="kb_listed")
         nc.vector.tensor_copy(kb_listed[:], kb_row[:].indirect(offsets[:]))
@@ -95,7 +96,7 @@ def tile_attend_gnce_w_kb_kernel(tc, xT, wT, y, wt, kb, xm, offs, out):
             for j in range(N // BLK):
                 c0 = b * N + j * BLK
                 nc.tensor.transpose(bank[:, j, :], kb_listed[:, c0 : c0 + BLK], ident[:])
-            nc.scalar.copy(bias[:, b * 4 : (b + 1) * 4], bank[:, :, 0])
+            nc.scalar.copy(bias[:, b * 4 : (b + 1) * 4], bank[:, :, KB_ROW])
 
         def operand(name):
             grouped = keep.tile([P, N, PACK], BF16, name=name + "_grouped", align_bytes=64)
@@ -131,26 +132,30 @@ def tile_attend_gnce_w_kb_kernel(tc, xT, wT, y, wt, kb, xm, offs, out):
         grads = []
         for b in range(B):
             x_op, w_op, g_op, xm_op = operand(f"x{b}"), operand(f"w{b}"), operand(f"g{b}"), operand(f"xm{b}")
-            interleave(nc.scalar.copy, x_op, x_raw[b], 0, R)
-            quantize(x_op, 0, R, E4M3)
             if b == 0:
-                gather(0, 2, 0, N)
-                gather(0, 3, 0, H)
-                gather(0, 3, H, N)
-                interleave(nc.scalar.copy, w_op, w_listed[0], 0, H)
-                interleave(nc.vector.tensor_copy, w_op, w_listed[0], H, N)
-                quantize(w_op, H, N, E4M3)
+                for t in range(PACK - 1):
+                    gather(t, 0, B * N)
+                interleave(nc.scalar.copy, x_op, x_raw[0], 0, H)
+                interleave(nc.scalar.copy, x_op, x_raw[0], H, R)
+                gather(PACK - 1, 0, H)
+                gather(PACK - 1, H, N)
+                join_pairs(nc.vector.tensor_copy, w_op, 0, 0, H)
+                join_pairs(nc.vector.tensor_copy, w_op, 0, H, N)
+                quantize(x_op, 0, H, E4M3)
                 quantize(w_op, 0, H, E4M3)
-                order = [2, 3, 0, 1]
+                quantize(x_op, H, R, E4M3)
+                quantize(w_op, H, N, E4M3)
             else:
-                interleave(nc.scalar.copy, w_op, w_listed[1], 0, N)
+                for j in range(R // BLK):
+                    interleave(nc.scalar.copy, x_op, x_raw[b], j * BLK, (j + 1) * BLK)
+                join_pairs(nc.vector.tensor_copy, w_op, 1, 0, H)
+                join_pairs(nc.vector.tensor_copy, w_op, 1, H, N)
+                quantize(x_op, 0, R, E4M3)
                 quantize(w_op, 0, N, E4M3)
-                order = [0, 1, 2, 3]
+            order = [0, 1, 2, 3]
             turned = {}
             if b == 1:
                 by_t = [psum.tile([P, N], F32, name="bank", tag="turned") for t in range(PACK)]
-                for t in range(PACK):
-                    nc.scalar.activation(y_raw[1][:, t, :], y_raw[1][:, t, :], COPY, scale=weight[1][:, t : t + 1])
             for j in order:
                 scores = psum.tile([P, R], F32, name="scores", tag="products")
                 product(scores, w_op, j * BLK, E4M3, x_op, E4M3)
@@ -168,13 +173,18 @@ def tile_attend_gnce_w_kb_kernel(tc, xT, wT, y, wt, kb, xm, offs, out):
                     nc.tensor.transpose(bank[:, t, :], prob[:, t, :], ident[:])
                 turned[j] = bank
             if b == 1:
-                weighted = keep.tile([P, PACK, N], F32, name="weighted", tag="w_listed0")
+                weighted = keep.tile([P, PACK, N], F32, name="weighted")
+                for t in range(PACK):
+                    nc.scalar.activation(y_raw[1][:, t, :], y_raw[1][:, t, :], COPY, scale=weight[1][:, t : t + 1])
                 for t in range(PACK):
                     nc.scalar.activation(weighted[:, t, :], by_t[t][:], COPY, scale=weight[1][:, t : t + 1])
-                nc.vector.tensor_tensor(
-                    by_lines(g_op[0][:], "p (c i) t"), by_lines(weighted[:], "p t (c i)"),
-                    by_lines(y_raw[1][:], "p t (c i)"), SUB,
-                )
+                for c0 in range(0, N, H):
+                    nc.vector.tensor_tensor(
+                        by_lines(g_op[0][:, c0 : c0 + H, :], "p (c i) t"),
+                        by_lines(weighted[:, :, c0 : c0 + H], "p t (c i)"),
+                        by_lines(y_raw[1][:, :, c0 : c0 + H], "p t (c i)"),
+                        SUB,
+                    )
                 order = []
             wide = weight[b][:].unsqueeze(1).unsqueeze(3).to_broadcast([P, BLK // 4, PACK, 4])
             diffs = {}
@@ -192,10 +202,10 @@ def tile_attend_gnce_w_kb_kernel(tc, xT, wT, y, wt, kb, xm, offs, out):
                     )
             for j in range(D // BLK):
                 interleave(nc.scalar.copy, xm_op, xm_raw[b], j * BLK, (j + 1) * BLK)
-            first = order[0] * BLK if order else 0
-            quantize(g_op, first, first + H, E5M2)
-            quantize(xm_op, 0, H, E4M3)
-            quantize(g_op, H - first, N - first, E5M2)
+            quantize(g_op, 0, H, E5M2)
+            quantize(xm_op, 0, BLK, E4M3)
+            quantize(g_op, H, N, E5M2)
+            quantize(xm_op, BLK, H, E4M3)
             quantize(xm_op, H, D, E4M3)
             grad = []
             for j in range(D // BLK):
@@ -206,8 +216,7 @@ def tile_attend_gnce_w_kb_kernel(tc, xT, wT, y, wt, kb, xm, offs, out):
                 grad.append(dw)
             grads.append(grad)
             if b == 0:
-                for t in range(2, PACK):
-                    gather(1, t, 0, N)
+                gather(PACK - 1, N, B * N)
 
         for b in range(B):
             for j in range(D // BLK):

@@ -16,210 +16,251 @@ E5M2 = mybir.dt.float8_e5m2_x4
 SIGMOID = mybir.ActivationFunctionType.Sigmoid
 COPY = mybir.ActivationFunctionType.Copy
 MULT = mybir.AluOpType.mult
+ADD = mybir.AluOpType.add
 SUB = mybir.AluOpType.subtract
 
 P = 128
 PACK = 4
 BLK = 128
+BLOCKS = 4
+HALF = 256
+HALVES = ((0, HALF), (HALF, N))
 LANES = 16
+LINE = 4
 KB_ROW = 96
+EARLY = 2
 
 
 def tile_attend_gnce_w_kb_kernel(tc, xT, wT, y, wt, kb, xm, offs, out):
     nc = tc.nc
     with ExitStack() as ctx:
         keep = ctx.enter_context(tc.tile_pool(name="keep", bufs=1))
-        ring = ctx.enter_context(tc.tile_pool(name="ring", bufs=4))
-        psum = ctx.enter_context(tc.psum_pool(name="psum", bufs=4))
+        ring = ctx.enter_context(tc.tile_pool(name="ring", bufs=BLOCKS))
+        psum = ctx.enter_context(tc.psum_pool(name="psum", bufs=1))
 
         offsets = keep.tile([P, B * N // LANES], U16, name="offsets")
         nc.sync.dma_start(offsets[:], offs)
 
-        def listed(first, count):
-            return offsets[:, first // LANES : (first + count) // LANES]
+        def listed(first, last):
+            return offsets[:, first // LANES : last // LANES]
 
-        kb_row = keep.tile([P, T], F32, name="kb_row")
-        nc.gpsimd.memset(kb_row[0:KB_ROW, :], 0.0)
-        nc.sync.dma_start(kb_row[KB_ROW:P, :], kb[KB_ROW:P, :])
-        weight = []
-        for b in range(B):
-            w_b = keep.tile([P, PACK], F32, name=f"weight{b}")
-            nc.scalar.dma_start(w_b[:], wt[b].rearrange("(p t) o -> p (t o)", t=PACK))
-            weight.append(w_b)
-        warm = keep.tile([P, 1], F32, name="warm")
-        nc.scalar.activation(warm[:], weight[0][:, 0:1], SIGMOID)
+        kb_table = keep.tile([P, T], F32, name="kb_table")
+        nc.gpsimd.memset(kb_table[0:KB_ROW, :], 0.0)
+        nc.scalar.dma_start(kb_table[KB_ROW:P, :], kb[KB_ROW:P, :])
+        weights = keep.tile([P, B, PACK], F32, name="weights")
+        nc.scalar.dma_start(weights[:], wt.rearrange("b (p t) o -> p b (t o)", t=PACK))
         ident = keep.tile([P, P], F32, name="ident")
         make_identity(nc, ident[:])
 
-        def load(src, name, pieces=1):
-            raw = keep.tile([P, PACK, src.shape[1]], F32, name=name)
-            rows = src.rearrange("(p t) c -> p t c", t=PACK)
-            width = src.shape[1] // pieces
-            for c0 in range(0, src.shape[1], width):
-                nc.sync.dma_start(raw[:, :, c0 : c0 + width], rows[:, :, c0 : c0 + width])
-            return raw
+        def staged(name):
+            return keep.tile([P, PACK, N], F32, name=name, align_bytes=64)
 
+        def load(raw, src, c0, c1):
+            nc.sync.dma_start(raw[:, :, c0:c1], src.rearrange("(p t) c -> p t c", t=PACK)[:, :, c0:c1])
+
+        x_raw0, y_raw0, xm_raw0 = staged("x_raw0"), staged("y_raw0"), staged("xm_raw0")
+        x_raw1, y_raw1, xm_raw1 = staged("x_raw1"), staged("y_raw1"), staged("xm_raw1")
         planes = []
         for t in range(PACK):
+            if t == PACK - 1:
+                for c0, c1 in HALVES:
+                    load(x_raw0, xT[0], c0, c1)
             plane = keep.tile([P, T], F32, name=f"plane{t}")
             nc.sync.dma_start(plane[:], wT.rearrange("(p t) c -> p t c", t=PACK)[:, t, :])
             planes.append(plane)
-        x_raw = [load(xT[0], "x_raw0", 2)]
-        xm_raw = [load(xm[0], "xm_raw0")]
-        y_raw = [load(y[0], "y_raw0", 2)]
-        x_raw.append(load(xT[1], "x_raw1"))
-        y_raw.append(load(y[1], "y_raw1"))
-        xm_raw.append(load(xm[1], "xm_raw1"))
+        load(xm_raw0, xm[0], 0, HALF)
+        load(y_raw0, y[0], 0, N)
+        load(xm_raw0, xm[0], HALF, D)
+        load(x_raw1, xT[1], 0, R)
+        load(y_raw1, y[1], 0, N)
+        load(xm_raw1, xm[1], 0, D)
 
         out_tiles = []
-        for j in range(D // BLK):
-            o = keep.tile([P, T], F32, name=f"out{j}")
-            nc.gpsimd.memset(o[:], 0.0)
-            out_tiles.append(o)
-
-        w_pairs = keep.tile([P, 2, B * N, 2], BF16, name="w_pairs")
-
-        def gather(t, c0, c1):
-            nc.vector.tensor_copy(w_pairs[:, t // 2, c0:c1, t % 2], planes[t][:].indirect(listed(c0, c1 - c0)))
-
-        def join_pairs(engine_copy, op, b, c0, c1):
-            engine_copy(
-                op[0][:, c0:c1, :].rearrange("p c (u e) -> p c u e", e=2),
-                w_pairs[:, :, b * N + c0 : b * N + c1, :].rearrange("p u c e -> p c u e"),
-            )
+        for j in range(BLOCKS):
+            zeros = keep.tile([P, T], F32, name=f"out{j}")
+            nc.gpsimd.memset(zeros[:], 0.0)
+            out_tiles.append(zeros)
 
         kb_listed = keep.tile([P, B * N], F32, name="kb_listed")
-        nc.vector.tensor_copy(kb_listed[:], kb_row[:].indirect(offsets[:]))
-        bias = keep.tile([P, B * N // BLK], F32, name="bias")
+        nc.vector.tensor_copy(kb_listed[:], kb_table[:].indirect(offsets[:]))
+        bias = keep.tile([P, B * BLOCKS], F32, name="bias")
         for b in range(B):
-            bank = psum.tile([P, N // BLK, BLK], F32, name="bank", tag="turned")
-            for j in range(N // BLK):
+            bank = psum.tile([P, BLOCKS, BLK], F32, name="kb_turned", tag=f"bank{b}")
+            for j in range(BLOCKS):
                 c0 = b * N + j * BLK
                 nc.tensor.transpose(bank[:, j, :], kb_listed[:, c0 : c0 + BLK], ident[:])
-            nc.scalar.copy(bias[:, b * 4 : (b + 1) * 4], bank[:, :, KB_ROW])
+            nc.scalar.copy(bias[:, b * BLOCKS : (b + 1) * BLOCKS], bank[:, :, KB_ROW])
 
-        def operand(name):
+        def operand(name, pad=0):
             grouped = keep.tile([P, N, PACK], BF16, name=name + "_grouped", align_bytes=64)
-            codes = keep.tile([P, N], U32, name=name + "_codes", align_bytes=64)
-            scales = keep.tile([P, N], U8, name=name + "_scales", align_bytes=64)
-            return grouped, codes, scales
+            codes = keep.tile([P, pad + N], U32, name=name + "_codes", align_bytes=64)
+            scales = keep.tile([P, pad + N], U8, name=name + "_scales", align_bytes=64)
+            return grouped, codes, scales, pad
+
+        def block(j):
+            return slice(j * BLK, (j + 1) * BLK)
 
         def by_lines(ap, order):
-            return ap.rearrange(order + " -> p c t i", i=4)
+            return ap.rearrange(order + " -> p c t i", i=LINE)
 
-        def interleave(engine_copy, op, raw, c0, c1):
-            engine_copy(by_lines(op[0][:, c0:c1, :], "p (c i) t"), by_lines(raw[:, :, c0:c1], "p t (c i)"))
+        def cast(op, raw, c0, c1):
+            nc.scalar.copy(by_lines(op[0][:, c0:c1, :], "p (c i) t"), by_lines(raw[:, :, c0:c1], "p t (c i)"))
+
+        def cast_blocks(op, raw, blocks):
+            for j in blocks:
+                cast(op, raw, j * BLK, (j + 1) * BLK)
 
         def quantize(op, c0, c1, fmt):
+            grouped, codes, scales, pad = op
             nc.vector.quantize_mx(
-                out=op[1][:, c0:c1].bitcast(fmt),
-                scales=op[2][:, c0:c1],
-                in_=op[0][:, c0:c1, :].rearrange("p c t -> p (c t)"),
+                out=codes[:, pad + c0 : pad + c1].bitcast(fmt),
+                scales=scales[:, pad + c0 : pad + c1],
+                in_=grouped[:, c0:c1, :].rearrange("p c t -> p (c t)"),
             )
 
-        def product(bank, lhs, c0, lhs_fmt, rhs, rhs_fmt):
+        def product(bank_number, lhs, j, rhs, rhs_fmt, first):
+            bank = psum.tile([P, N], F32, name="product", tag=f"bank{bank_number}")
             nc.tensor.matmul_mx(
                 out=bank[:],
-                lhsT=lhs[1][:, c0 : c0 + BLK].bitcast(lhs_fmt),
-                lhsT_scale=lhs[2][:, c0 : c0 + BLK],
-                rhs=rhs[1][:].bitcast(rhs_fmt),
-                rhs_scale=rhs[2][:],
+                lhsT=lhs[1][:, block(j)].bitcast(E4M3),
+                lhsT_scale=lhs[2][:, block(j)],
+                rhs=rhs[1][:, first : first + N].bitcast(rhs_fmt),
+                rhs_scale=rhs[2][:, first : first + N],
                 start=True,
                 stop=True,
             )
+            return bank
 
-        H = N // 2
-        grads = []
-        for b in range(B):
-            x_op, w_op, g_op, xm_op = operand(f"x{b}"), operand(f"w{b}"), operand(f"g{b}"), operand(f"xm{b}")
-            if b == 0:
-                for t in range(PACK - 1):
-                    gather(t, 0, B * N)
-                interleave(nc.scalar.copy, x_op, x_raw[0], 0, H)
-                interleave(nc.scalar.copy, x_op, x_raw[0], H, R)
-                gather(PACK - 1, 0, H)
-                gather(PACK - 1, H, N)
-                join_pairs(nc.vector.tensor_copy, w_op, 0, 0, H)
-                join_pairs(nc.vector.tensor_copy, w_op, 0, H, N)
-                quantize(x_op, 0, H, E4M3)
-                quantize(w_op, 0, H, E4M3)
-                quantize(x_op, H, R, E4M3)
-                quantize(w_op, H, N, E4M3)
-            else:
-                for j in range(R // BLK):
-                    interleave(nc.scalar.copy, x_op, x_raw[b], j * BLK, (j + 1) * BLK)
-                join_pairs(nc.vector.tensor_copy, w_op, 1, 0, H)
-                join_pairs(nc.vector.tensor_copy, w_op, 1, H, N)
-                quantize(x_op, 0, R, E4M3)
-                quantize(w_op, 0, N, E4M3)
-            order = [0, 1, 2, 3]
-            turned = {}
-            if b == 1:
-                by_t = [psum.tile([P, N], F32, name="bank", tag="turned") for t in range(PACK)]
-            for j in order:
-                scores = psum.tile([P, R], F32, name="scores", tag="products")
-                product(scores, w_op, j * BLK, E4M3, x_op, E4M3)
-                prob = ring.tile([P, PACK, BLK], F32, name="prob")
-                nc.scalar.activation(
-                    prob[:], scores[:].rearrange("p (m t) -> p t m", t=PACK), SIGMOID,
-                    bias=bias[:, b * 4 + j : b * 4 + j + 1],
+        pairs = keep.tile([P, B + 1, N, 2], BF16, name="pairs")
+
+        def gather_high(t, b, c0, c1):
+            nc.vector.tensor_copy(pairs[:, B, c0:c1, t - 2], planes[t][:].indirect(listed(b * N + c0, b * N + c1)))
+
+        def join_pairs(copy, op, b, c0, c1):
+            copy(
+                op[0][:, c0:c1, :].rearrange("p c (u e) -> p c u e", e=2),
+                pairs[:, b : B + 1 : B - b, c0:c1, :].rearrange("p u c e -> p c u e"),
+            )
+
+        def probabilities(b, w_op, x_op, j, bank_number):
+            scores = product(bank_number, w_op, j, x_op, E4M3, 0)
+            prob = ring.tile([P, PACK, BLK], F32, name="prob")
+            nc.scalar.activation(
+                prob[:],
+                scores[:].rearrange("p (m t) -> p t m", t=PACK),
+                SIGMOID,
+                bias=bias[:, b * BLOCKS + j : b * BLOCKS + j + 1],
+            )
+            return prob
+
+        def turn(prob, bank_number):
+            bank = psum.tile([P, PACK, BLK], F32, name="turned", tag=f"bank{bank_number}")
+            for t in range(PACK):
+                nc.tensor.transpose(bank[:, t, :], prob[:, t, :], ident[:])
+            return bank
+
+        def to_sbuf(bank, c0, c1, name, slot=None):
+            values = keep.tile([P, c1 - c0], F32, name=name, tag=slot or name, align_bytes=64)
+            nc.scalar.copy(values[:], bank[:, c0:c1])
+            return values
+
+        def scatter(j, first, values):
+            nc.vector.tensor_copy(out_tiles[j][:].indirect(listed(first, first + values.shape[1])), values[:])
+
+        x0, w0, xm0, g0 = operand("x0"), operand("w0"), operand("xm0"), operand("g0", HALF)
+        nc.gpsimd.memset(g0[1][:, 0:HALF], 0)
+        nc.gpsimd.memset(g0[2][:, 0:HALF].bitcast(U32), 0)
+
+        for t in range(2):
+            nc.vector.tensor_copy(
+                pairs[:, 0:B, :, t].rearrange("p b c -> p (b c)"), planes[t][:].indirect(offsets[:])
+            )
+        gather_high(2, 0, 0, N)
+        for c0, c1 in HALVES:
+            cast(x0, x_raw0, c0, c1)
+            quantize(x0, c0, c1, E4M3)
+        for c0, c1 in HALVES:
+            gather_high(3, 0, c0, c1)
+        for c0, c1 in HALVES:
+            join_pairs(nc.vector.tensor_copy, w0, 0, c0, c1)
+        for c0, c1 in HALVES:
+            quantize(w0, c0, c1, E4M3)
+
+        x1, w1, xm1, g1 = operand("x1"), operand("w1"), operand("xm1"), operand("g1")
+        diff0 = staged("diff0")
+        weighted1 = staged("weighted1")
+        wt0_wide = weights[:, 0, :].unsqueeze(1).unsqueeze(3).to_broadcast([P, BLK // LINE, PACK, LINE])
+        turned0 = [turn(probabilities(0, w0, x0, j, BLOCKS + j), j) for j in range(BLOCKS)]
+
+        def make_g0(blocks):
+            for j in blocks:
+                nc.vector.tensor_tensor(diff0[:, :, block(j)], turned0[j][:], y_raw0[:, :, block(j)], SUB)
+            for j in blocks:
+                nc.vector.tensor_tensor(
+                    by_lines(g0[0][:, block(j), :], "p (c i) t"),
+                    by_lines(diff0[:, :, block(j)], "p t (c i)"),
+                    wt0_wide,
+                    MULT,
                 )
-                if b == 1:
-                    for t in range(PACK):
-                        nc.tensor.transpose(by_t[t][:, j * BLK : (j + 1) * BLK], prob[:, t, :], ident[:])
-                    continue
-                bank = psum.tile([P, PACK, BLK], F32, name="bank", tag="turned")
-                for t in range(PACK):
-                    nc.tensor.transpose(bank[:, t, :], prob[:, t, :], ident[:])
-                turned[j] = bank
-            if b == 1:
-                weighted = keep.tile([P, PACK, N], F32, name="weighted")
-                for t in range(PACK):
-                    nc.scalar.activation(y_raw[1][:, t, :], y_raw[1][:, t, :], COPY, scale=weight[1][:, t : t + 1])
-                for t in range(PACK):
-                    nc.scalar.activation(weighted[:, t, :], by_t[t][:], COPY, scale=weight[1][:, t : t + 1])
-                for c0 in range(0, N, H):
-                    nc.vector.tensor_tensor(
-                        by_lines(g_op[0][:, c0 : c0 + H, :], "p (c i) t"),
-                        by_lines(weighted[:, :, c0 : c0 + H], "p t (c i)"),
-                        by_lines(y_raw[1][:, :, c0 : c0 + H], "p t (c i)"),
-                        SUB,
-                    )
-                order = []
-            wide = weight[b][:].unsqueeze(1).unsqueeze(3).to_broadcast([P, BLK // 4, PACK, 4])
-            diffs = {}
-            for step in range(len(order) + 1 if order else 0):
-                if step < len(order):
-                    j = order[step]
-                    diff = ring.tile([P, PACK, BLK], F32, name="diff")
-                    nc.vector.tensor_tensor(diff[:], turned[j][:], y_raw[b][:, :, j * BLK : (j + 1) * BLK], SUB)
-                    diffs[j] = diff
-                if step > 0:
-                    j = order[step - 1]
-                    nc.vector.tensor_tensor(
-                        by_lines(g_op[0][:, j * BLK : (j + 1) * BLK, :], "p (c i) t"),
-                        by_lines(diffs[j][:], "p t (c i)"), wide, MULT,
-                    )
-            for j in range(D // BLK):
-                interleave(nc.scalar.copy, xm_op, xm_raw[b], j * BLK, (j + 1) * BLK)
-            quantize(g_op, 0, H, E5M2)
-            quantize(xm_op, 0, BLK, E4M3)
-            quantize(g_op, H, N, E5M2)
-            quantize(xm_op, BLK, H, E4M3)
-            quantize(xm_op, H, D, E4M3)
-            grad = []
-            for j in range(D // BLK):
-                bank = psum.tile([P, N], F32, name="dw", tag="products")
-                product(bank, xm_op, j * BLK, E4M3, g_op, E5M2)
-                dw = keep.tile([P, N], F32, name=f"dw{b}_{j}")
-                nc.scalar.copy(dw[:], bank[:])
-                grad.append(dw)
-            grads.append(grad)
-            if b == 0:
-                gather(PACK - 1, N, B * N)
 
-        for b in range(B):
-            for j in range(D // BLK):
-                nc.vector.tensor_copy(out_tiles[j][:].indirect(listed(b * N, N)), grads[b][j][:])
-                if b == B - 1:
-                    nc.sync.dma_start(out[j * BLK : (j + 1) * BLK, :], out_tiles[j][:])
+        make_g0((0, 1))
+        quantize(g0, 0, BLK, E5M2)
+        quantize(g0, BLK, HALF, E5M2)
+        cast_blocks(xm0, xm_raw0, (0, 1))
+        quantize(xm0, 0, HALF, E4M3)
+        early_banks = [product(BLOCKS + j, xm0, j, g0, E5M2, 0) for j in range(EARLY)]
+        make_g0((2, 3))
+        cast_blocks(x1, x_raw1, range(BLOCKS))
+        early = [to_sbuf(early_banks[j], HALF, N, f"early{j}") for j in range(EARLY)]
+        quantize(g0, HALF, N, E5M2)
+        cast_blocks(xm0, xm_raw0, (2, 3))
+        quantize(xm0, HALF, D, E4M3)
+        quantize(x1, 0, R, E4M3)
+        late_banks = [product(BLOCKS + (EARLY + j) % BLOCKS, xm0, j, g0, E5M2, HALF) for j in range(BLOCKS)]
+
+        for c0, c1 in HALVES:
+            gather_high(2, 1, c0, c1)
+            gather_high(3, 1, c0, c1)
+        for c0, c1 in HALVES:
+            join_pairs(nc.scalar.copy, w1, 1, c0, c1)
+        quantize(w1, 0, N, E4M3)
+
+        late = [(j, HALF, to_sbuf(late_banks[j], HALF, N, f"late{j}")) for j in range(EARLY)]
+        late.append((2, 0, to_sbuf(late_banks[2], 0, N, "late2")))
+        late.append((3, 0, to_sbuf(late_banks[3], 0, HALF, "late3")))
+
+        weighted_y1 = keep.tile([P, PACK, N], F32, name="weighted_y1", tag="w1_grouped", align_bytes=64)
+        for t in range(PACK):
+            nc.gpsimd.tensor_scalar(weighted_y1[:, t, :], y_raw1[:, t, :], weights[:, 1, t : t + 1], 0.0, MULT, ADD)
+
+        def make_g1(j, prob):
+            bank = turn(prob, (6, 7, 4)[j % 3])
+            for t in range(PACK):
+                nc.scalar.activation(weighted1[:, t, block(j)], bank[:, t, :], COPY, scale=weights[:, 1, t : t + 1])
+            nc.gpsimd.tensor_tensor(
+                by_lines(g1[0][:, block(j), :], "p (c i) t"),
+                by_lines(weighted1[:, :, block(j)], "p t (c i)"),
+                by_lines(weighted_y1[:, :, block(j)], "p t (c i)"),
+                SUB,
+            )
+
+        probs1 = [probabilities(1, w1, x1, j, j) for j in range(BLOCKS - 1)]
+        make_g1(0, probs1[0])
+        probs1.append(probabilities(1, w1, x1, BLOCKS - 1, BLOCKS - 1))
+        for j in range(1, BLOCKS):
+            make_g1(j, probs1[j])
+        late.append((3, HALF, to_sbuf(late_banks[3], HALF, N, "late3_rest", slot="weighted1")))
+
+        cast_blocks(xm1, xm_raw1, range(BLOCKS))
+        for c0, c1 in HALVES:
+            quantize(g1, c0, c1, E5M2)
+            quantize(xm1, c0, c1, E4M3)
+        last = [to_sbuf(product(j, xm1, j, g1, E5M2, 0), 0, N, f"last{j}") for j in range(BLOCKS)]
+
+        for j in range(EARLY):
+            scatter(j, 0, early[j])
+        for j, first, values in late:
+            scatter(j, first, values)
+        for j in range(BLOCKS):
+            scatter(j, N, last[j])
+            nc.sync.dma_start(out[block(j), :], out_tiles[j][:])

@@ -8,6 +8,7 @@ FLOPS = 2 * 2 * B * N * D * R
 
 F32 = mybir.dt.float32
 BF16 = mybir.dt.bfloat16
+I32 = mybir.dt.int32
 U32 = mybir.dt.uint32
 U16 = mybir.dt.uint16
 U8 = mybir.dt.uint8
@@ -28,14 +29,12 @@ HALVES = ((0, HALF), (HALF, N))
 LANES = 16
 LINE = 4
 KB_ROW = 96
-EARLY = 2
 
 
 def tile_attend_gnce_w_kb_kernel(tc, xT, wT, y, wt, kb, xm, offs, out):
     nc = tc.nc
     with ExitStack() as ctx:
         keep = ctx.enter_context(tc.tile_pool(name="keep", bufs=1))
-        ring = ctx.enter_context(tc.tile_pool(name="ring", bufs=BLOCKS))
         psum = ctx.enter_context(tc.psum_pool(name="psum", bufs=1))
 
         offsets = keep.tile([P, B * N // LANES], U16, name="offsets")
@@ -44,18 +43,21 @@ def tile_attend_gnce_w_kb_kernel(tc, xT, wT, y, wt, kb, xm, offs, out):
         def listed(first, last):
             return offsets[:, first // LANES : last // LANES]
 
+        warm = keep.tile([P, 2], F32, name="warm")
+        nc.vector.memset(warm[:, 0:1], 0.0)
+        nc.scalar.activation(warm[:, 1:2], warm[:, 0:1], SIGMOID)
+
         kb_table = keep.tile([P, T], F32, name="kb_table")
-        nc.gpsimd.memset(kb_table[0:KB_ROW, :], 0.0)
+        nc.vector.memset(kb_table[0:KB_ROW, 0 : T // 2 - 1], 0.0)
+        nc.vector.memset(kb_table[0:KB_ROW, T // 2 - 1 : T], 0.0)
         nc.scalar.dma_start(kb_table[KB_ROW:P, :], kb[KB_ROW:P, :])
-        weights = keep.tile([P, B, PACK], F32, name="weights")
-        nc.scalar.dma_start(weights[:], wt.rearrange("b (p t) o -> p b (t o)", t=PACK))
         ident = keep.tile([P, P], F32, name="ident")
         make_identity(nc, ident[:])
 
         def staged(name):
             return keep.tile([P, PACK, N], F32, name=name, align_bytes=64)
 
-        def load(raw, src, c0, c1):
+        def load(raw, src, c0=0, c1=N):
             nc.sync.dma_start(raw[:, :, c0:c1], src.rearrange("(p t) c -> p t c", t=PACK)[:, :, c0:c1])
 
         x_raw0, y_raw0, xm_raw0 = staged("x_raw0"), staged("y_raw0"), staged("xm_raw0")
@@ -63,17 +65,18 @@ def tile_attend_gnce_w_kb_kernel(tc, xT, wT, y, wt, kb, xm, offs, out):
         planes = []
         for t in range(PACK):
             if t == PACK - 1:
-                for c0, c1 in HALVES:
-                    load(x_raw0, xT[0], c0, c1)
+                load(x_raw0, xT[0])
             plane = keep.tile([P, T], F32, name=f"plane{t}")
             nc.sync.dma_start(plane[:], wT.rearrange("(p t) c -> p t c", t=PACK)[:, t, :])
             planes.append(plane)
         load(xm_raw0, xm[0], 0, HALF)
-        load(y_raw0, y[0], 0, N)
+        load(y_raw0, y[0])
+        weights = keep.tile([P, B, PACK], F32, name="weights")
+        nc.sync.dma_start(weights[:], wt.rearrange("b (p t) o -> p b (t o)", t=PACK))
+        load(x_raw1, xT[1])
         load(xm_raw0, xm[0], HALF, D)
-        load(x_raw1, xT[1], 0, R)
-        load(y_raw1, y[1], 0, N)
-        load(xm_raw1, xm[1], 0, D)
+        load(y_raw1, y[1])
+        load(xm_raw1, xm[1])
 
         out_tiles = []
         for j in range(BLOCKS):
@@ -91,8 +94,8 @@ def tile_attend_gnce_w_kb_kernel(tc, xT, wT, y, wt, kb, xm, offs, out):
                 nc.tensor.transpose(bank[:, j, :], kb_listed[:, c0 : c0 + BLK], ident[:])
             nc.scalar.copy(bias[:, b * BLOCKS : (b + 1) * BLOCKS], bank[:, :, KB_ROW])
 
-        def operand(name, pad=0):
-            grouped = keep.tile([P, N, PACK], BF16, name=name + "_grouped", align_bytes=64)
+        def operand(name, pad=0, slot=None):
+            grouped = keep.tile([P, N, PACK], BF16, name=name + "_grouped", tag=slot or name, align_bytes=64)
             codes = keep.tile([P, pad + N], U32, name=name + "_codes", align_bytes=64)
             scales = keep.tile([P, pad + N], U8, name=name + "_scales", align_bytes=64)
             return grouped, codes, scales, pad
@@ -103,12 +106,12 @@ def tile_attend_gnce_w_kb_kernel(tc, xT, wT, y, wt, kb, xm, offs, out):
         def by_lines(ap, order):
             return ap.rearrange(order + " -> p c t i", i=LINE)
 
-        def cast(op, raw, c0, c1):
-            nc.scalar.copy(by_lines(op[0][:, c0:c1, :], "p (c i) t"), by_lines(raw[:, :, c0:c1], "p t (c i)"))
+        def cast(copy, op, raw, c0, c1):
+            copy(by_lines(op[0][:, c0:c1, :], "p (c i) t"), by_lines(raw[:, :, c0:c1], "p t (c i)"))
 
-        def cast_blocks(op, raw, blocks):
+        def cast_blocks(op, raw, blocks=range(BLOCKS)):
             for j in blocks:
-                cast(op, raw, j * BLK, (j + 1) * BLK)
+                cast(nc.scalar.copy, op, raw, j * BLK, (j + 1) * BLK)
 
         def quantize(op, c0, c1, fmt):
             grouped, codes, scales, pad = op
@@ -131,20 +134,19 @@ def tile_attend_gnce_w_kb_kernel(tc, xT, wT, y, wt, kb, xm, offs, out):
             )
             return bank
 
-        pairs = keep.tile([P, B + 1, N, 2], BF16, name="pairs")
+        waiting = keep.tile([P, 5 * N], BF16, name="waiting", align_bytes=64)
+        planes1 = waiting[:, 0 : PACK * N].rearrange("p (t c) -> p t c", t=PACK)
+        pairs = waiting[:, 3 * N : 5 * N]
 
-        def gather_high(t, b, c0, c1):
-            nc.vector.tensor_copy(pairs[:, B, c0:c1, t - 2], planes[t][:].indirect(listed(b * N + c0, b * N + c1)))
+        def gather(dst, t, first, last):
+            nc.vector.tensor_copy(dst, planes[t][:].indirect(listed(first, last)))
 
-        def join_pairs(copy, op, b, c0, c1):
-            copy(
-                op[0][:, c0:c1, :].rearrange("p c (u e) -> p c u e", e=2),
-                pairs[:, b : B + 1 : B - b, c0:c1, :].rearrange("p u c e -> p c u e"),
-            )
+        def gather_pairs(t):
+            gather(pairs.rearrange("p (u c e) -> p u c e", u=2, e=2)[:, t // 2, :, t % 2], t, HALF, N)
 
         def probabilities(b, w_op, x_op, j, bank_number):
             scores = product(bank_number, w_op, j, x_op, E4M3, 0)
-            prob = ring.tile([P, PACK, BLK], F32, name="prob")
+            prob = keep.tile([P, PACK, BLK], F32, name=f"prob{j}", align_bytes=64)
             nc.scalar.activation(
                 prob[:],
                 scores[:].rearrange("p (m t) -> p t m", t=PACK),
@@ -159,38 +161,48 @@ def tile_attend_gnce_w_kb_kernel(tc, xT, wT, y, wt, kb, xm, offs, out):
                 nc.tensor.transpose(bank[:, t, :], prob[:, t, :], ident[:])
             return bank
 
-        def to_sbuf(bank, c0, c1, name, slot=None):
-            values = keep.tile([P, c1 - c0], F32, name=name, tag=slot or name, align_bytes=64)
-            nc.scalar.copy(values[:], bank[:, c0:c1])
-            return values
+        def values(name, count, slot=None):
+            return keep.tile([P, count], F32, name=name, tag=slot or name, align_bytes=64)
 
-        def scatter(j, first, values):
-            nc.vector.tensor_copy(out_tiles[j][:].indirect(listed(first, first + values.shape[1])), values[:])
+        def scatter(j, first, src):
+            nc.vector.tensor_copy(out_tiles[j][:].indirect(listed(first, first + src.shape[1])), src)
 
-        x0, w0, xm0, g0 = operand("x0"), operand("w0"), operand("xm0"), operand("g0", HALF)
+        x0, w0, g0 = operand("x0"), operand("w0"), operand("g0", HALF)
         nc.gpsimd.memset(g0[1][:, 0:HALF], 0)
         nc.gpsimd.memset(g0[2][:, 0:HALF].bitcast(U32), 0)
 
-        for t in range(2):
-            nc.vector.tensor_copy(
-                pairs[:, 0:B, :, t].rearrange("p b c -> p (b c)"), planes[t][:].indirect(offsets[:])
-            )
-        gather_high(2, 0, 0, N)
+        for t in range(PACK - 1):
+            gather(w0[0][:, 0:HALF, t], t, 0, HALF)
+            gather_pairs(t)
+            if t < PACK - 2:
+                gather(planes1[:, t, :], t, N, B * N)
+        gather(planes1[:, 2, 0:HALF], 2, N, N + HALF)
+        cast(nc.scalar.copy, x0, x_raw0, 0, BLK)
+        cast(nc.vector.tensor_copy, x0, x_raw0, BLK, R)
+        gather(planes1[:, 2, HALF:N], 2, N + HALF, B * N)
+        quantize(x0, 0, R, E4M3)
+        gather(w0[0][:, 0:HALF, PACK - 1], PACK - 1, 0, HALF)
+        quantize(w0, 0, HALF, E4M3)
+        gather_pairs(PACK - 1)
+        nc.vector.tensor_copy(
+            w0[0][:, HALF:N, :].rearrange("p c t -> p (c t)").bitcast(I32).rearrange("p (c u) -> p c u", u=2),
+            pairs.bitcast(I32).rearrange("p (u c) -> p c u", u=2),
+        )
+        quantize(w0, HALF, N, E4M3)
         for c0, c1 in HALVES:
-            cast(x0, x_raw0, c0, c1)
-            quantize(x0, c0, c1, E4M3)
-        for c0, c1 in HALVES:
-            gather_high(3, 0, c0, c1)
-        for c0, c1 in HALVES:
-            join_pairs(nc.vector.tensor_copy, w0, 0, c0, c1)
-        for c0, c1 in HALVES:
-            quantize(w0, c0, c1, E4M3)
+            gather(planes1[:, PACK - 1, c0:c1], PACK - 1, N + c0, N + c1)
+        w1 = operand("w1")
+        cast(nc.vector.tensor_copy, w1, planes1, 0, HALF)
+        xm0 = operand("xm0")
+        cast_blocks(xm0, xm_raw0, (0, 1))
+        quantize(xm0, 0, HALF, E4M3)
 
-        x1, w1, xm1, g1 = operand("x1"), operand("w1"), operand("xm1"), operand("g1")
+        g1 = operand("g1")
         diff0 = staged("diff0")
         weighted1 = staged("weighted1")
         wt0_wide = weights[:, 0, :].unsqueeze(1).unsqueeze(3).to_broadcast([P, BLK // LINE, PACK, LINE])
-        turned0 = [turn(probabilities(0, w0, x0, j, BLOCKS + j), j) for j in range(BLOCKS)]
+        turned0 = [turn(probabilities(0, w0, x0, j, j + 4), j) for j in range(2)]
+        cast(nc.scalar.copy, w1, planes1, HALF, N)
 
         def make_g0(blocks):
             for j in blocks:
@@ -204,37 +216,29 @@ def tile_attend_gnce_w_kb_kernel(tc, xT, wT, y, wt, kb, xm, offs, out):
                 )
 
         make_g0((0, 1))
-        quantize(g0, 0, BLK, E5M2)
-        quantize(g0, BLK, HALF, E5M2)
-        cast_blocks(xm0, xm_raw0, (0, 1))
-        quantize(xm0, 0, HALF, E4M3)
-        early_banks = [product(BLOCKS + j, xm0, j, g0, E5M2, 0) for j in range(EARLY)]
-        make_g0((2, 3))
-        cast_blocks(x1, x_raw1, range(BLOCKS))
-        early = [to_sbuf(early_banks[j], HALF, N, f"early{j}") for j in range(EARLY)]
-        quantize(g0, HALF, N, E5M2)
-        cast_blocks(xm0, xm_raw0, (2, 3))
-        quantize(xm0, HALF, D, E4M3)
-        quantize(x1, 0, R, E4M3)
-        late_banks = [product(BLOCKS + (EARLY + j) % BLOCKS, xm0, j, g0, E5M2, HALF) for j in range(BLOCKS)]
-
-        for c0, c1 in HALVES:
-            gather_high(2, 1, c0, c1)
-            gather_high(3, 1, c0, c1)
-        for c0, c1 in HALVES:
-            join_pairs(nc.scalar.copy, w1, 1, c0, c1)
         quantize(w1, 0, N, E4M3)
+        quantize(g0, 0, HALF, E5M2)
+        turned0.append(turn(probabilities(0, w0, x0, 2, 5), 2))
+        turned0.append(turn(probabilities(0, w0, x0, 3, 0), 3))
+        early_bank = product(4, xm0, 0, g0, E5M2, 0)
+        x1 = operand("x1", slot="x0_codes")
+        cast_blocks(x1, x_raw1)
+        cast_blocks(xm0, xm_raw0, (2, 3))
+        make_g0((2, 3))
+        quantize(x1, 0, R, E4M3)
+        quantize(g0, HALF, N, E5M2)
+        quantize(xm0, HALF, D, E4M3)
+        early = values("early", HALF)
+        nc.scalar.copy(early[:], early_bank[:, HALF:N])
 
-        late = [(j, HALF, to_sbuf(late_banks[j], HALF, N, f"late{j}")) for j in range(EARLY)]
-        late.append((2, 0, to_sbuf(late_banks[2], 0, N, "late2")))
-        late.append((3, 0, to_sbuf(late_banks[3], 0, HALF, "late3")))
-
-        weighted_y1 = keep.tile([P, PACK, N], F32, name="weighted_y1", tag="w1_grouped", align_bytes=64)
+        weighted_y1 = keep.tile([P, PACK, N], F32, name="weighted_y1", tag="g0", align_bytes=64)
         for t in range(PACK):
             nc.gpsimd.tensor_scalar(weighted_y1[:, t, :], y_raw1[:, t, :], weights[:, 1, t : t + 1], 0.0, MULT, ADD)
 
+        banks1 = (6, 7, 0, 1)
+
         def make_g1(j, prob):
-            bank = turn(prob, (6, 7, 4)[j % 3])
+            bank = turn(prob, banks1[j])
             for t in range(PACK):
                 nc.scalar.activation(weighted1[:, t, block(j)], bank[:, t, :], COPY, scale=weights[:, 1, t : t + 1])
             nc.gpsimd.tensor_tensor(
@@ -244,23 +248,39 @@ def tile_attend_gnce_w_kb_kernel(tc, xT, wT, y, wt, kb, xm, offs, out):
                 SUB,
             )
 
-        probs1 = [probabilities(1, w1, x1, j, j) for j in range(BLOCKS - 1)]
+        def late_piece(j, first, last, slot=None):
+            piece = values(f"late{j}_{first}", last - first, slot)
+            nc.scalar.copy(piece[:], late_banks[j][:, first:last])
+            return j, first, piece[:]
+
+        probs1 = [probabilities(1, w1, x1, j, banks1[j]) for j in range(2)]
+        late_banks = [product((5, 2, 3, 4)[j], xm0, j, g0, E5M2, HALF) for j in range(BLOCKS)]
+        late_pieces = [late_piece(0, HALF, N)]
         make_g1(0, probs1[0])
-        probs1.append(probabilities(1, w1, x1, BLOCKS - 1, BLOCKS - 1))
-        for j in range(1, BLOCKS):
-            make_g1(j, probs1[j])
-        late.append((3, HALF, to_sbuf(late_banks[3], HALF, N, "late3_rest", slot="weighted1")))
+        probs1.append(probabilities(1, w1, x1, 2, banks1[2]))
+        late_pieces.append(late_piece(1, 0, N))
+        make_g1(1, probs1[1])
+        probs1.append(probabilities(1, w1, x1, 3, banks1[3]))
+        late_pieces.append(late_piece(2, 0, N))
+        late_pieces.append(late_piece(3, 0, HALF))
+        make_g1(2, probs1[2])
+        make_g1(3, probs1[3])
+        late_pieces.append(late_piece(3, HALF, N, slot="weighted1"))
 
-        cast_blocks(xm1, xm_raw1, range(BLOCKS))
+        xm1 = operand("xm1", slot=f"prob{BLOCKS - 1}")
+        cast_blocks(xm1, xm_raw1)
+        quantize(g1, 0, N, E5M2)
         for c0, c1 in HALVES:
-            quantize(g1, c0, c1, E5M2)
             quantize(xm1, c0, c1, E4M3)
-        last = [to_sbuf(product(j, xm1, j, g1, E5M2, 0), 0, N, f"last{j}") for j in range(BLOCKS)]
-
-        for j in range(EARLY):
-            scatter(j, 0, early[j])
-        for j, first, values in late:
-            scatter(j, first, values)
+        last = []
         for j in range(BLOCKS):
-            scatter(j, N, last[j])
+            bank = product((5, 2, 3, 6)[j], xm1, j, g1, E5M2, 0)
+            last.append(values(f"last{j}", N))
+            nc.scalar.copy(last[j][:], bank[:])
+
+        scatter(0, 0, early[:])
+        for j, first, src in late_pieces:
+            scatter(j, first, src)
+        for j in range(BLOCKS):
+            scatter(j, N, last[j][:])
             nc.sync.dma_start(out[block(j), :], out_tiles[j][:])

@@ -8,7 +8,6 @@ FLOPS = 2 * 2 * B * N * D * R
 
 F32 = mybir.dt.float32
 BF16 = mybir.dt.bfloat16
-I32 = mybir.dt.int32
 U32 = mybir.dt.uint32
 U16 = mybir.dt.uint16
 U8 = mybir.dt.uint8
@@ -26,6 +25,7 @@ BLK = 128
 BLOCKS = 4
 HALF = 256
 HALVES = ((0, HALF), (HALF, N))
+REST = B * N - HALF
 LANES = 16
 LINE = 4
 KB_ROW = 96
@@ -69,12 +69,12 @@ def tile_attend_gnce_w_kb_kernel(tc, xT, wT, y, wt, kb, xm, offs, out):
             plane = keep.tile([P, T], F32, name=f"plane{t}")
             nc.sync.dma_start(plane[:], wT.rearrange("(p t) c -> p t c", t=PACK)[:, t, :])
             planes.append(plane)
-        load(xm_raw0, xm[0], 0, HALF)
+        load(xm_raw0, xm[0], 0, BLK)
         load(y_raw0, y[0])
         weights = keep.tile([P, B, PACK], F32, name="weights")
         nc.sync.dma_start(weights[:], wt.rearrange("b (p t) o -> p b (t o)", t=PACK))
         load(x_raw1, xT[1])
-        load(xm_raw0, xm[0], HALF, D)
+        load(xm_raw0, xm[0], BLK, D)
         load(y_raw1, y[1])
         load(xm_raw1, xm[1])
 
@@ -94,8 +94,9 @@ def tile_attend_gnce_w_kb_kernel(tc, xT, wT, y, wt, kb, xm, offs, out):
                 nc.tensor.transpose(bank[:, j, :], kb_listed[:, c0 : c0 + BLK], ident[:])
             nc.scalar.copy(bias[:, b * BLOCKS : (b + 1) * BLOCKS], bank[:, :, KB_ROW])
 
-        def operand(name, pad=0, slot=None):
-            grouped = keep.tile([P, N, PACK], BF16, name=name + "_grouped", tag=slot or name, align_bytes=64)
+        def operand(name, pad=0, slot=None, grouped=None):
+            if grouped is None:
+                grouped = keep.tile([P, N, PACK], BF16, name=name + "_grouped", tag=slot or name, align_bytes=64)
             codes = keep.tile([P, pad + N], U32, name=name + "_codes", align_bytes=64)
             scales = keep.tile([P, pad + N], U8, name=name + "_scales", align_bytes=64)
             return grouped, codes, scales, pad
@@ -134,25 +135,31 @@ def tile_attend_gnce_w_kb_kernel(tc, xT, wT, y, wt, kb, xm, offs, out):
             )
             return bank
 
-        waiting = keep.tile([P, 5 * N], BF16, name="waiting", align_bytes=64)
-        planes1 = waiting[:, 0 : PACK * N].rearrange("p (t c) -> p t c", t=PACK)
-        pairs = waiting[:, 3 * N : 5 * N]
+        columns = keep.tile([P, PACK * REST - N + PACK * N], BF16, name="columns", align_bytes=64)
+        waiting = columns[:, 0 : PACK * REST].rearrange("p (t c) -> p t c", t=PACK)
+        w0_values = columns[:, PACK * REST - N :].rearrange("p (c t) -> p c t", t=PACK)
 
         def gather(dst, t, first, last):
             nc.vector.tensor_copy(dst, planes[t][:].indirect(listed(first, last)))
 
-        def gather_pairs(t):
-            gather(pairs.rearrange("p (u c e) -> p u c e", u=2, e=2)[:, t // 2, :, t % 2], t, HALF, N)
+        def gather_waiting(t, first, last):
+            gather(waiting[:, t, first - HALF : last - HALF], t, first, last)
 
-        def probabilities(b, w_op, x_op, j, bank_number):
+        def join(copy, op, first, last):
+            dst = op[0][:, first % N : first % N + last - first, :]
+            copy(by_lines(dst, "p (c i) t"), by_lines(waiting[:, :, first - HALF : last - HALF], "p t (c i)"))
+
+        def probabilities(b, w_op, x_op, j, bank_number, parts=1):
             scores = product(bank_number, w_op, j, x_op, E4M3, 0)
             prob = keep.tile([P, PACK, BLK], F32, name=f"prob{j}", align_bytes=64)
-            nc.scalar.activation(
-                prob[:],
-                scores[:].rearrange("p (m t) -> p t m", t=PACK),
-                SIGMOID,
-                bias=bias[:, b * BLOCKS + j : b * BLOCKS + j + 1],
-            )
+            step = PACK // parts
+            for t in range(0, PACK, step):
+                nc.scalar.activation(
+                    prob[:, t : t + step, :],
+                    scores[:].rearrange("p (m t) -> p t m", t=PACK)[:, t : t + step, :],
+                    SIGMOID,
+                    bias=bias[:, b * BLOCKS + j : b * BLOCKS + j + 1],
+                )
             return prob
 
         def turn(prob, bank_number):
@@ -167,46 +174,42 @@ def tile_attend_gnce_w_kb_kernel(tc, xT, wT, y, wt, kb, xm, offs, out):
         def scatter(j, first, src):
             nc.vector.tensor_copy(out_tiles[j][:].indirect(listed(first, first + src.shape[1])), src)
 
-        x0, w0, g0 = operand("x0"), operand("w0"), operand("g0", HALF)
+        x0, w0, g0 = operand("x0"), operand("w0", grouped=w0_values), operand("g0", HALF)
         nc.gpsimd.memset(g0[1][:, 0:HALF], 0)
         nc.gpsimd.memset(g0[2][:, 0:HALF].bitcast(U32), 0)
 
         for t in range(PACK - 1):
-            gather(w0[0][:, 0:HALF, t], t, 0, HALF)
-            gather_pairs(t)
-            if t < PACK - 2:
-                gather(planes1[:, t, :], t, N, B * N)
-        gather(planes1[:, 2, 0:HALF], 2, N, N + HALF)
+            gather(w0_values[:, 0:HALF, t], t, 0, HALF)
+            gather_waiting(t, HALF, B * N if t < PACK - 2 else REST)
         cast(nc.scalar.copy, x0, x_raw0, 0, BLK)
         cast(nc.vector.tensor_copy, x0, x_raw0, BLK, R)
-        gather(planes1[:, 2, HALF:N], 2, N + HALF, B * N)
+        gather_waiting(PACK - 2, REST, B * N)
         quantize(x0, 0, R, E4M3)
-        gather(w0[0][:, 0:HALF, PACK - 1], PACK - 1, 0, HALF)
+        gather(w0_values[:, 0:HALF, PACK - 1], PACK - 1, 0, HALF)
         quantize(w0, 0, HALF, E4M3)
-        gather_pairs(PACK - 1)
-        nc.vector.tensor_copy(
-            w0[0][:, HALF:N, :].rearrange("p c t -> p (c t)").bitcast(I32).rearrange("p (c u) -> p c u", u=2),
-            pairs.bitcast(I32).rearrange("p (u c) -> p c u", u=2),
-        )
+        gather_waiting(PACK - 1, HALF, N)
+        join(nc.vector.tensor_copy, w0, HALF, N)
         quantize(w0, HALF, N, E4M3)
-        for c0, c1 in HALVES:
-            gather(planes1[:, PACK - 1, c0:c1], PACK - 1, N + c0, N + c1)
-        w1 = operand("w1")
-        cast(nc.vector.tensor_copy, w1, planes1, 0, HALF)
+        gather_waiting(PACK - 1, N, REST)
+        gather_waiting(PACK - 1, REST, B * N)
         xm0 = operand("xm0")
-        cast_blocks(xm0, xm_raw0, (0, 1))
-        quantize(xm0, 0, HALF, E4M3)
+        cast_blocks(xm0, xm_raw0, (0,))
+        quantize(xm0, 0, BLK, E4M3)
 
         g1 = operand("g1")
         diff0 = staged("diff0")
         weighted1 = staged("weighted1")
         wt0_wide = weights[:, 0, :].unsqueeze(1).unsqueeze(3).to_broadcast([P, BLK // LINE, PACK, LINE])
-        turned0 = [turn(probabilities(0, w0, x0, j, j + 4), j) for j in range(2)]
-        cast(nc.scalar.copy, w1, planes1, HALF, N)
+        turned0 = [turn(probabilities(0, w0, x0, 0, 4, PACK), 0), turn(probabilities(0, w0, x0, 1, 5), 1)]
+        w1 = operand("w1")
+        for c0, c1 in HALVES:
+            join(nc.scalar.copy, w1, N + c0, N + c1)
 
-        def make_g0(blocks):
+        def differences(blocks):
             for j in blocks:
                 nc.vector.tensor_tensor(diff0[:, :, block(j)], turned0[j][:], y_raw0[:, :, block(j)], SUB)
+
+        def weigh(blocks):
             for j in blocks:
                 nc.vector.tensor_tensor(
                     by_lines(g0[0][:, block(j), :], "p (c i) t"),
@@ -215,7 +218,8 @@ def tile_attend_gnce_w_kb_kernel(tc, xT, wT, y, wt, kb, xm, offs, out):
                     MULT,
                 )
 
-        make_g0((0, 1))
+        differences((0, 1))
+        weigh((0, 1))
         quantize(w1, 0, N, E4M3)
         quantize(g0, 0, HALF, E5M2)
         turned0.append(turn(probabilities(0, w0, x0, 2, 5), 2))
@@ -223,13 +227,15 @@ def tile_attend_gnce_w_kb_kernel(tc, xT, wT, y, wt, kb, xm, offs, out):
         early_bank = product(4, xm0, 0, g0, E5M2, 0)
         x1 = operand("x1", slot="x0_codes")
         cast_blocks(x1, x_raw1)
-        cast_blocks(xm0, xm_raw0, (2, 3))
-        make_g0((2, 3))
+        differences((2, 3))
+        weigh((2, 3))
         quantize(x1, 0, R, E4M3)
         quantize(g0, HALF, N, E5M2)
-        quantize(xm0, HALF, D, E4M3)
-        early = values("early", HALF)
+        early = values("early", HALF, slot="diff0")
         nc.scalar.copy(early[:], early_bank[:, HALF:N])
+        cast_blocks(xm0, xm_raw0, (1, 2, 3))
+        quantize(xm0, BLK, HALF, E4M3)
+        quantize(xm0, HALF, D, E4M3)
 
         weighted_y1 = keep.tile([P, PACK, N], F32, name="weighted_y1", tag="g0", align_bytes=64)
         for t in range(PACK):

@@ -69,12 +69,12 @@ def tile_attend_gnce_w_kb_kernel(tc, xT, wT, y, wt, kb, xm, offs, out):
             plane = keep.tile([P, T], F32, name=f"plane{t}")
             nc.sync.dma_start(plane[:], wT.rearrange("(p t) c -> p t c", t=PACK)[:, t, :])
             planes.append(plane)
-        load(xm_raw0, xm[0], 0, BLK)
+        load(xm_raw0, xm[0], 0, HALF)
         load(y_raw0, y[0])
         weights = keep.tile([P, B, PACK], F32, name="weights")
         nc.sync.dma_start(weights[:], wt.rearrange("b (p t) o -> p b (t o)", t=PACK))
         load(x_raw1, xT[1])
-        load(xm_raw0, xm[0], BLK, D)
+        load(xm_raw0, xm[0], HALF, D)
         load(y_raw1, y[1])
         load(xm_raw1, xm[1])
 
@@ -126,8 +126,8 @@ def tile_attend_gnce_w_kb_kernel(tc, xT, wT, y, wt, kb, xm, offs, out):
             bank = psum.tile([P, N], F32, name="product", tag=f"bank{bank_number}")
             nc.tensor.matmul_mx(
                 out=bank[:],
-                lhsT=lhs[1][:, block(j)].bitcast(E4M3),
-                lhsT_scale=lhs[2][:, block(j)],
+                lhsT=lhs[1][:, lhs[3] + j * BLK : lhs[3] + (j + 1) * BLK].bitcast(E4M3),
+                lhsT_scale=lhs[2][:, lhs[3] + j * BLK : lhs[3] + (j + 1) * BLK],
                 rhs=rhs[1][:, first : first + N].bitcast(rhs_fmt),
                 rhs_scale=rhs[2][:, first : first + N],
                 start=True,
@@ -162,10 +162,10 @@ def tile_attend_gnce_w_kb_kernel(tc, xT, wT, y, wt, kb, xm, offs, out):
                 )
             return prob
 
-        def turn(prob, bank_number):
-            bank = psum.tile([P, PACK, BLK], F32, name="turned", tag=f"bank{bank_number}")
-            for t in range(PACK):
-                nc.tensor.transpose(bank[:, t, :], prob[:, t, :], ident[:])
+        def turn(prob, bank_number, first=0, last=PACK):
+            bank = psum.tile([P, last - first, BLK], F32, name="turned", tag=f"bank{bank_number}")
+            for t in range(first, last):
+                nc.tensor.transpose(bank[:, t - first, :], prob[:, t, :], ident[:])
             return bank
 
         def values(name, count, slot=None):
@@ -186,21 +186,24 @@ def tile_attend_gnce_w_kb_kernel(tc, xT, wT, y, wt, kb, xm, offs, out):
         gather_waiting(PACK - 2, REST, B * N)
         quantize(x0, 0, R, E4M3)
         gather(w0_values[:, 0:HALF, PACK - 1], PACK - 1, 0, HALF)
-        quantize(w0, 0, HALF, E4M3)
+        quantize(w0, 0, BLK, E4M3)
+        quantize(w0, BLK, HALF, E4M3)
         gather_waiting(PACK - 1, HALF, N)
         join(nc.vector.tensor_copy, w0, HALF, N)
         quantize(w0, HALF, N, E4M3)
         gather_waiting(PACK - 1, N, REST)
-        gather_waiting(PACK - 1, REST, B * N)
         xm0 = operand("xm0")
-        cast_blocks(xm0, xm_raw0, (0,))
-        quantize(xm0, 0, BLK, E4M3)
+        cast(nc.vector.tensor_copy, xm0, xm_raw0, 0, HALF)
+        gather_waiting(PACK - 1, REST, B * N)
+        quantize(xm0, 0, HALF, E4M3)
 
         g1 = operand("g1")
         diff0 = staged("diff0")
         weighted1 = staged("weighted1")
         wt0_wide = weights[:, 0, :].unsqueeze(1).unsqueeze(3).to_broadcast([P, BLK // LINE, PACK, LINE])
-        turned0 = [turn(probabilities(0, w0, x0, 0, 4, PACK), 0), turn(probabilities(0, w0, x0, 1, 5), 1)]
+        prob = probabilities(0, w0, x0, 0, 4, PACK)
+        first_parts = [(0, turn(prob, 6, 0, 2)), (2, turn(prob, 0, 2, PACK))]
+        turned0 = [None, turn(probabilities(0, w0, x0, 1, 5), 1)]
         w1 = operand("w1")
         for c0, c1 in HALVES:
             join(nc.scalar.copy, w1, N + c0, N + c1)
@@ -218,7 +221,9 @@ def tile_attend_gnce_w_kb_kernel(tc, xT, wT, y, wt, kb, xm, offs, out):
                     MULT,
                 )
 
-        differences((0, 1))
+        for t, bank in first_parts:
+            nc.vector.tensor_tensor(diff0[:, t : t + 2, block(0)], bank[:], y_raw0[:, t : t + 2, block(0)], SUB)
+        differences((1,))
         weigh((0, 1))
         quantize(w1, 0, N, E4M3)
         quantize(g0, 0, HALF, E5M2)
@@ -233,9 +238,19 @@ def tile_attend_gnce_w_kb_kernel(tc, xT, wT, y, wt, kb, xm, offs, out):
         quantize(g0, HALF, N, E5M2)
         early = values("early", HALF, slot="diff0")
         nc.scalar.copy(early[:], early_bank[:, HALF:N])
-        cast_blocks(xm0, xm_raw0, (1, 2, 3))
-        quantize(xm0, BLK, HALF, E4M3)
-        quantize(xm0, HALF, D, E4M3)
+        late_banks = [product((5, 2)[j], xm0, j, g0, E5M2, HALF) for j in range(2)]
+        late0 = values("late0", HALF)
+        nc.scalar.copy(late0[:], late_banks[0][:, HALF:N])
+        cast_blocks(xm0, xm_raw0, (2, 3))
+        scatter(0, 0, early[:])
+        scatter(0, HALF, late0[:])
+        xm0_rest = (
+            xm0[0],
+            keep.tile([P, HALF], U32, name="xm0_rest_codes", tag="diff0", align_bytes=64),
+            keep.tile([P, HALF], U8, name="xm0_rest_scales", align_bytes=64),
+            -HALF,
+        )
+        quantize(xm0_rest, HALF, D, E4M3)
 
         weighted_y1 = keep.tile([P, PACK, N], F32, name="weighted_y1", tag="g0", align_bytes=64)
         for t in range(PACK):
@@ -260,13 +275,13 @@ def tile_attend_gnce_w_kb_kernel(tc, xT, wT, y, wt, kb, xm, offs, out):
             return j, first, piece[:]
 
         probs1 = [probabilities(1, w1, x1, j, banks1[j]) for j in range(2)]
-        late_banks = [product((5, 2, 3, 4)[j], xm0, j, g0, E5M2, HALF) for j in range(BLOCKS)]
-        late_pieces = [late_piece(0, HALF, N)]
+        late_pieces = []
         make_g1(0, probs1[0])
         probs1.append(probabilities(1, w1, x1, 2, banks1[2]))
         late_pieces.append(late_piece(1, 0, N))
         make_g1(1, probs1[1])
         probs1.append(probabilities(1, w1, x1, 3, banks1[3]))
+        late_banks.extend(product(j + 1, xm0_rest, j, g0, E5M2, HALF) for j in (2, 3))
         late_pieces.append(late_piece(2, 0, N))
         late_pieces.append(late_piece(3, 0, HALF))
         make_g1(2, probs1[2])
@@ -284,7 +299,6 @@ def tile_attend_gnce_w_kb_kernel(tc, xT, wT, y, wt, kb, xm, offs, out):
             last.append(values(f"last{j}", N))
             nc.scalar.copy(last[j][:], bank[:])
 
-        scatter(0, 0, early[:])
         for j, first, src in late_pieces:
             scatter(j, first, src)
         for j in range(BLOCKS):

@@ -43,10 +43,6 @@ def tile_attend_gnce_w_kb_kernel(tc, xT, wT, y, wt, kb, xm, offs, out):
         def listed(first, last):
             return offsets[:, first // LANES : last // LANES]
 
-        warm = keep.tile([P, 2], F32, name="warm")
-        nc.vector.memset(warm[:, 0:1], 0.0)
-        nc.scalar.activation(warm[:, 1:2], warm[:, 0:1], SIGMOID)
-
         kb_table = keep.tile([P, T], F32, name="kb_table")
         nc.vector.memset(kb_table[0:KB_ROW, 0 : T // 2 - 1], 0.0)
         nc.vector.memset(kb_table[0:KB_ROW, T // 2 - 1 : T], 0.0)
@@ -181,8 +177,8 @@ def tile_attend_gnce_w_kb_kernel(tc, xT, wT, y, wt, kb, xm, offs, out):
         for t in range(PACK - 1):
             gather(w0_values[:, 0:HALF, t], t, 0, HALF)
             gather_waiting(t, HALF, B * N if t < PACK - 2 else REST)
-        cast(nc.scalar.copy, x0, x_raw0, 0, BLK)
-        cast(nc.vector.tensor_copy, x0, x_raw0, BLK, R)
+        cast_blocks(x0, x_raw0, (0, 1))
+        cast(nc.vector.tensor_copy, x0, x_raw0, HALF, R)
         gather_waiting(PACK - 2, REST, B * N)
         quantize(x0, 0, R, E4M3)
         gather(w0_values[:, 0:HALF, PACK - 1], PACK - 1, 0, HALF)

@@ -28,7 +28,7 @@ HALVES = ((0, HALF), (HALF, N))
 REST = B * N - HALF
 LANES = 16
 LINE = 4
-KB_ROW = 96
+KB_ROW = P - 1
 
 
 def tile_attend_gnce_w_kb_kernel(tc, xT, wT, y, wt, kb, xm, offs, out):

@@ -24,7 +24,6 @@ PACK = 4
 BLK = 128
 BLOCKS = 4
 HALF = 256
-HALVES = ((0, HALF), (HALF, N))
 REST = B * N - HALF
 LANES = 16
 LINE = 4
@@ -36,6 +35,9 @@ def tile_attend_gnce_w_kb_kernel(tc, xT, wT, y, wt, kb, xm, offs, out):
     with ExitStack() as ctx:
         keep = ctx.enter_context(tc.tile_pool(name="keep", bufs=1))
         psum = ctx.enter_context(tc.psum_pool(name="psum", bufs=1))
+
+        def tile(name, shape, dtype, slot=None):
+            return keep.tile([P] + shape, dtype, name=name, tag=slot or name, align_bytes=64)
 
         offsets = keep.tile([P, B * N // LANES], U16, name="offsets")
         nc.sync.dma_start(offsets[:], offs)
@@ -50,29 +52,27 @@ def tile_attend_gnce_w_kb_kernel(tc, xT, wT, y, wt, kb, xm, offs, out):
         ident = keep.tile([P, P], F32, name="ident")
         make_identity(nc, ident[:])
 
-        def staged(name):
-            return keep.tile([P, PACK, N], F32, name=name, align_bytes=64)
+        def load(name, src, c0=0, c1=N):
+            raw = tile(name, [PACK, c1 - c0], F32)
+            nc.sync.dma_start(raw[:], src.rearrange("(p t) c -> p t c", t=PACK)[:, :, c0:c1])
+            return raw
 
-        def load(raw, src, c0=0, c1=N):
-            nc.sync.dma_start(raw[:, :, c0:c1], src.rearrange("(p t) c -> p t c", t=PACK)[:, :, c0:c1])
-
-        x_raw0, y_raw0, xm_raw0 = staged("x_raw0"), staged("y_raw0"), staged("xm_raw0")
-        x_raw1, y_raw1, xm_raw1 = staged("x_raw1"), staged("y_raw1"), staged("xm_raw1")
         planes = []
         for t in range(PACK):
             if t == PACK - 1:
-                load(x_raw0, xT[0])
+                x_raw0 = load("x_raw0", xT[0])
             plane = keep.tile([P, T], F32, name=f"plane{t}")
             nc.sync.dma_start(plane[:], wT.rearrange("(p t) c -> p t c", t=PACK)[:, t, :])
             planes.append(plane)
-        load(xm_raw0, xm[0], 0, HALF)
-        load(y_raw0, y[0])
+        xm_raw0 = [load("xm_raw0a", xm[0], 0, HALF)]
+        y_raw0 = [load("y_raw0a", y[0], 0, HALF)]
         weights = keep.tile([P, B, PACK], F32, name="weights")
         nc.sync.dma_start(weights[:], wt.rearrange("b (p t) o -> p b (t o)", t=PACK))
-        load(x_raw1, xT[1])
-        load(xm_raw0, xm[0], HALF, D)
-        load(y_raw1, y[1])
-        load(xm_raw1, xm[1])
+        y_raw0.append(load("y_raw0b", y[0], HALF, N))
+        x_raw1 = load("x_raw1", xT[1])
+        xm_raw0.append(load("xm_raw0b", xm[0], HALF, D))
+        y_raw1 = load("y_raw1", y[1])
+        xm_raw1 = load("xm_raw1", xm[1])
 
         out_tiles = []
         for j in range(BLOCKS):
@@ -90,64 +90,48 @@ def tile_attend_gnce_w_kb_kernel(tc, xT, wT, y, wt, kb, xm, offs, out):
                 nc.tensor.transpose(bank[:, j, :], kb_listed[:, c0 : c0 + BLK], ident[:])
             nc.scalar.copy(bias[:, b * BLOCKS : (b + 1) * BLOCKS], bank[:, :, KB_ROW])
 
-        def operand(name, pad=0, slot=None, grouped=None):
-            if grouped is None:
-                grouped = keep.tile([P, N, PACK], BF16, name=name + "_grouped", tag=slot or name, align_bytes=64)
-            codes = keep.tile([P, pad + N], U32, name=name + "_codes", align_bytes=64)
-            scales = keep.tile([P, pad + N], U8, name=name + "_scales", align_bytes=64)
-            return grouped, codes, scales, pad
+        def block(j, count=1):
+            return slice(j * BLK, (j + count) * BLK)
 
-        def block(j):
-            return slice(j * BLK, (j + 1) * BLK)
+        def packed(name, width, slot=None):
+            return tile(name + "_codes", [width], U32, slot), tile(name + "_scales", [width], U8)
 
         def by_lines(ap, order):
             return ap.rearrange(order + " -> p c t i", i=LINE)
 
-        def cast(copy, op, raw, c0, c1):
-            copy(by_lines(op[0][:, c0:c1, :], "p (c i) t"), by_lines(raw[:, :, c0:c1], "p t (c i)"))
+        def weave(copy, dst, src):
+            copy(by_lines(dst, "p (c i) t"), by_lines(src, "p t (c i)"))
 
-        def cast_blocks(op, raw, blocks=range(BLOCKS)):
-            for j in blocks:
-                cast(nc.scalar.copy, op, raw, j * BLK, (j + 1) * BLK)
+        def weave_blocks(dst, src):
+            for j in range(src.shape[2] // BLK):
+                weave(nc.scalar.copy, dst[:, block(j), :], src[:, :, block(j)])
 
-        def quantize(op, c0, c1, fmt):
-            grouped, codes, scales, pad = op
+        def quantize(op, first, values, fmt):
+            cols = slice(first, first + values.shape[1])
             nc.vector.quantize_mx(
-                out=codes[:, pad + c0 : pad + c1].bitcast(fmt),
-                scales=scales[:, pad + c0 : pad + c1],
-                in_=grouped[:, c0:c1, :].rearrange("p c t -> p (c t)"),
+                out=op[0][:, cols].bitcast(fmt),
+                scales=op[1][:, cols],
+                in_=values.rearrange("p c t -> p (c t)"),
             )
 
-        def product(bank_number, lhs, j, rhs, rhs_fmt, first):
+        def product(bank_number, lhs, j, rhs, rhs_fmt, first=0):
             bank = psum.tile([P, N], F32, name="product", tag=f"bank{bank_number}")
             nc.tensor.matmul_mx(
                 out=bank[:],
-                lhsT=lhs[1][:, lhs[3] + j * BLK : lhs[3] + (j + 1) * BLK].bitcast(E4M3),
-                lhsT_scale=lhs[2][:, lhs[3] + j * BLK : lhs[3] + (j + 1) * BLK],
-                rhs=rhs[1][:, first : first + N].bitcast(rhs_fmt),
-                rhs_scale=rhs[2][:, first : first + N],
+                lhsT=lhs[0][:, block(j)].bitcast(E4M3),
+                lhsT_scale=lhs[1][:, block(j)],
+                rhs=rhs[0][:, first : first + N].bitcast(rhs_fmt),
+                rhs_scale=rhs[1][:, first : first + N],
                 start=True,
                 stop=True,
             )
             return bank
 
-        columns = keep.tile([P, PACK * REST - N + PACK * N], BF16, name="columns", align_bytes=64)
-        waiting = columns[:, 0 : PACK * REST].rearrange("p (t c) -> p t c", t=PACK)
-        w0_values = columns[:, PACK * REST - N :].rearrange("p (c t) -> p c t", t=PACK)
-
         def gather(dst, t, first, last):
             nc.vector.tensor_copy(dst, planes[t][:].indirect(listed(first, last)))
 
-        def gather_waiting(t, first, last):
-            gather(waiting[:, t, first - HALF : last - HALF], t, first, last)
-
-        def join(copy, op, first, last):
-            dst = op[0][:, first % N : first % N + last - first, :]
-            copy(by_lines(dst, "p (c i) t"), by_lines(waiting[:, :, first - HALF : last - HALF], "p t (c i)"))
-
-        def probabilities(b, w_op, x_op, j, bank_number, parts=1):
-            scores = product(bank_number, w_op, j, x_op, E4M3, 0)
-            prob = keep.tile([P, PACK, BLK], F32, name=f"prob{j}", align_bytes=64)
+        def probabilities(b, w_op, x_op, j, bank_number, prob, parts=1):
+            scores = product(bank_number, w_op, j, x_op, E4M3)
             step = PACK // parts
             for t in range(0, PACK, step):
                 nc.scalar.activation(
@@ -158,145 +142,150 @@ def tile_attend_gnce_w_kb_kernel(tc, xT, wT, y, wt, kb, xm, offs, out):
                 )
             return prob
 
+        def prob_tile(j):
+            return tile(f"prob{j}", [PACK, BLK], F32)[:]
+
         def turn(prob, bank_number, first=0, last=PACK):
             bank = psum.tile([P, last - first, BLK], F32, name="turned", tag=f"bank{bank_number}")
             for t in range(first, last):
                 nc.tensor.transpose(bank[:, t - first, :], prob[:, t, :], ident[:])
             return bank
 
-        def values(name, count, slot=None):
-            return keep.tile([P, count], F32, name=name, tag=slot or name, align_bytes=64)
+        def piece(name, bank, first, last, slot=None):
+            values = tile(name, [last - first], F32, slot)
+            nc.scalar.copy(values[:], bank[:, first:last])
+            return values
 
-        def scatter(j, first, src):
-            nc.vector.tensor_copy(out_tiles[j][:].indirect(listed(first, first + src.shape[1])), src)
+        def scatter(j, first, values):
+            nc.vector.tensor_copy(out_tiles[j][:].indirect(listed(first, first + values.shape[1])), values[:])
 
-        x0, w0, g0 = operand("x0"), operand("w0", grouped=w0_values), operand("g0", HALF)
-        nc.gpsimd.memset(g0[1][:, 0:HALF], 0)
-        nc.gpsimd.memset(g0[2][:, 0:HALF].bitcast(U32), 0)
+        columns = tile("columns", [PACK * REST - N + PACK * N], BF16)
+        waiting = columns[:, 0 : PACK * REST].rearrange("p (t c) -> p t c", t=PACK)
+        w0_values = columns[:, PACK * REST - N :].rearrange("p (c t) -> p c t", t=PACK)
+
+        def gather_waiting(t, first, last):
+            gather(waiting[:, t, first - HALF : last - HALF], t, first, last)
+
+        x0, w0 = packed("x0", R), packed("w0", N)
+        g_ops = [packed(f"g{b}", HALF + N) for b in range(B)]
+        for codes, scales in g_ops:
+            nc.gpsimd.memset(codes[:, 0:HALF], 0)
+            nc.gpsimd.memset(scales[:, 0:HALF].bitcast(U32), 0)
+        g0, g1 = g_ops
 
         for t in range(PACK - 1):
             gather(w0_values[:, 0:HALF, t], t, 0, HALF)
             gather_waiting(t, HALF, B * N if t < PACK - 2 else REST)
-        cast_blocks(x0, x_raw0, (0, 1))
-        cast(nc.vector.tensor_copy, x0, x_raw0, HALF, R)
+        x0_values = tile("x0_values", [R, PACK], BF16)
+        weave_blocks(x0_values[:, 0:HALF, :], x_raw0[:, :, 0:HALF])
+        weave(nc.vector.tensor_copy, x0_values[:, HALF:R, :], x_raw0[:, :, HALF:R])
         gather_waiting(PACK - 2, REST, B * N)
-        quantize(x0, 0, R, E4M3)
+        quantize(x0, 0, x0_values[:], E4M3)
         gather(w0_values[:, 0:HALF, PACK - 1], PACK - 1, 0, HALF)
-        quantize(w0, 0, BLK, E4M3)
-        quantize(w0, BLK, HALF, E4M3)
+        for j in range(2):
+            quantize(w0, j * BLK, w0_values[:, block(j), :], E4M3)
         gather_waiting(PACK - 1, HALF, N)
-        join(nc.vector.tensor_copy, w0, HALF, N)
-        quantize(w0, HALF, N, E4M3)
+        weave(nc.vector.tensor_copy, w0_values[:, HALF:N, :], waiting[:, :, 0:HALF])
+        quantize(w0, HALF, w0_values[:, HALF:N, :], E4M3)
         gather_waiting(PACK - 1, N, REST)
-        xm0 = operand("xm0")
-        cast(nc.vector.tensor_copy, xm0, xm_raw0, 0, HALF)
         gather_waiting(PACK - 1, REST, B * N)
-        quantize(xm0, 0, HALF, E4M3)
 
-        g1 = operand("g1")
-        diff0 = staged("diff0")
-        weighted1 = staged("weighted1")
-        wt0_wide = weights[:, 0, :].unsqueeze(1).unsqueeze(3).to_broadcast([P, BLK // LINE, PACK, LINE])
-        prob = probabilities(0, w0, x0, 0, 4, PACK)
+        g0_values = tile("g0_values", [HALF, PACK], BF16)
+        wt0_by_lines = weights[:, 0, :].unsqueeze(1).unsqueeze(3).to_broadcast([P, BLK // LINE, PACK, LINE])
+        wt0_woven = weights[:, 0, :].unsqueeze(1).to_broadcast([P, BLK, PACK])
+
+        prob = probabilities(0, w0, x0, 0, 4, prob_tile(0), PACK)
         first_parts = [(0, turn(prob, 6, 0, 2)), (2, turn(prob, 0, 2, PACK))]
-        turned0 = [None, turn(probabilities(0, w0, x0, 1, 5), 1)]
-        w1 = operand("w1")
-        for c0, c1 in HALVES:
-            join(nc.scalar.copy, w1, N + c0, N + c1)
-
-        def differences(blocks):
-            for j in blocks:
-                nc.vector.tensor_tensor(diff0[:, :, block(j)], turned0[j][:], y_raw0[:, :, block(j)], SUB)
-
-        def weigh(blocks):
-            for j in blocks:
-                nc.vector.tensor_tensor(
-                    by_lines(g0[0][:, block(j), :], "p (c i) t"),
-                    by_lines(diff0[:, :, block(j)], "p t (c i)"),
-                    wt0_wide,
-                    MULT,
-                )
-
+        turned = turn(probabilities(0, w0, x0, 1, 5, prob_tile(1)), 1)
+        diff01 = tile("diff01", [2, PACK, BLK], F32)
         for t, bank in first_parts:
-            nc.vector.tensor_tensor(diff0[:, t : t + 2, block(0)], bank[:], y_raw0[:, t : t + 2, block(0)], SUB)
-        differences((1,))
-        weigh((0, 1))
-        quantize(w1, 0, N, E4M3)
-        quantize(g0, 0, HALF, E5M2)
-        turned0.append(turn(probabilities(0, w0, x0, 2, 5), 2))
-        turned0.append(turn(probabilities(0, w0, x0, 3, 0), 3))
-        early_bank = product(4, xm0, 0, g0, E5M2, 0)
-        x1 = operand("x1", slot="x0_codes")
-        cast_blocks(x1, x_raw1)
-        differences((2, 3))
-        weigh((2, 3))
-        quantize(x1, 0, R, E4M3)
-        quantize(g0, HALF, N, E5M2)
-        early = values("early", HALF, slot="diff0")
-        nc.scalar.copy(early[:], early_bank[:, HALF:N])
-        late_banks = [product((5, 2)[j], xm0, j, g0, E5M2, HALF) for j in range(2)]
-        late0 = values("late0", HALF)
-        nc.scalar.copy(late0[:], late_banks[0][:, HALF:N])
-        cast_blocks(xm0, xm_raw0, (2, 3))
-        scatter(0, 0, early[:])
-        scatter(0, HALF, late0[:])
-        xm0_rest = (
-            xm0[0],
-            keep.tile([P, HALF], U32, name="xm0_rest_codes", tag="diff0", align_bytes=64),
-            keep.tile([P, HALF], U8, name="xm0_rest_scales", align_bytes=64),
-            -HALF,
-        )
-        quantize(xm0_rest, HALF, D, E4M3)
+            nc.vector.tensor_tensor(diff01[:, 0, t : t + 2, :], bank[:], y_raw0[0][:, t : t + 2, block(0)], SUB)
+        nc.vector.tensor_tensor(diff01[:, 1], turned[:], y_raw0[0][:, :, block(1)], SUB)
+        for j in range(2):
+            nc.vector.tensor_tensor(
+                by_lines(g0_values[:, block(j), :], "p (c i) t"), by_lines(diff01[:, j], "p t (c i)"), wt0_by_lines, MULT
+            )
+        turned23 = [turn(probabilities(0, w0, x0, j, (5, 0)[j - 2], prob_tile(j)), j) for j in (2, 3)]
+        xm0a_values = tile("xm0a_values", [HALF, PACK], BF16)
+        weave_blocks(xm0a_values[:], xm_raw0[0][:])
+        xm0a = packed("xm0a", HALF)
+        quantize(xm0a, 0, xm0a_values[:], E4M3)
+        quantize(g0, HALF, g0_values[:], E5M2)
+        diff23 = tile("diff23", [HALF, PACK], F32, "diff01")
+        for j in range(2):
+            nc.vector.tensor_tensor(
+                diff23[:, block(j), :].rearrange("p (c i) t -> p c t i", i=2),
+                turned23[j][:].rearrange("p t (c i) -> p c t i", i=2),
+                y_raw0[1][:, :, block(j)].rearrange("p t (c i) -> p c t i", i=2),
+                SUB,
+            )
+            nc.gpsimd.tensor_tensor(g0_values[:, block(j), :], diff23[:, block(j), :], wt0_woven, MULT)
+        for j, bank_number in enumerate((4, 7)):
+            scatter(j, 0, piece(f"early{j}", product(bank_number, xm0a, j, g0, E5M2), HALF, N))
 
-        weighted_y1 = keep.tile([P, PACK, N], F32, name="weighted_y1", tag="g0", align_bytes=64)
+        w1_values = tile("w1_values", [N, PACK], BF16, "prob3")
+        weave_blocks(w1_values[:], waiting[:, :, HALF:REST])
+        x1_values = tile("x1_values", [R, PACK], BF16, "x0_codes")
+        weave_blocks(x1_values[:], x_raw1[:])
+        xm0b_values = tile("xm0b_values", [HALF, PACK], BF16)
+        weave_blocks(xm0b_values[:], xm_raw0[1][:])
+        quantize(g0, N, g0_values[:], E5M2)
+        w1 = packed("w1", N, "diff01")
+        quantize(w1, 0, w1_values[:], E4M3)
+        x1 = packed("x1", R, "g0_values")
+        quantize(x1, 0, x1_values[:], E4M3)
+        xm0b = packed("xm0b", HALF)
+        quantize(xm0b, 0, xm0b_values[:], E4M3)
+        late_banks = [product((5, 2)[j], xm0a, j, g0, E5M2, HALF) for j in range(2)]
+        scatter(0, HALF, piece("late0", late_banks[0], HALF, N, "x0_codes"))
+        scatter(1, HALF, piece("late1", late_banks[1], HALF, N))
+
+        weighted_y1 = tile("weighted_y1", [PACK, N], F32, "xm0b_values")
         for t in range(PACK):
             nc.gpsimd.tensor_scalar(weighted_y1[:, t, :], y_raw1[:, t, :], weights[:, 1, t : t + 1], 0.0, MULT, ADD)
-
-        banks1 = (6, 7, 0, 1)
+        g1_values = tile("g1_values", [HALF, PACK], BF16)
+        weighted1 = [tile(f"weighted1{h}", [2, PACK, BLK], F32) for h in range(2)]
+        banks1 = (6, 7, 6, 7)
 
         def make_g1(j, prob):
             bank = turn(prob, banks1[j])
+            weighted = weighted1[j // 2][:, j % 2]
             for t in range(PACK):
-                nc.scalar.activation(weighted1[:, t, block(j)], bank[:, t, :], COPY, scale=weights[:, 1, t : t + 1])
+                nc.scalar.activation(weighted[:, t, :], bank[:, t, :], COPY, scale=weights[:, 1, t : t + 1])
             nc.gpsimd.tensor_tensor(
-                by_lines(g1[0][:, block(j), :], "p (c i) t"),
-                by_lines(weighted1[:, :, block(j)], "p t (c i)"),
+                by_lines(g1_values[:, block(j % 2), :], "p (c i) t"),
+                by_lines(weighted, "p t (c i)"),
                 by_lines(weighted_y1[:, :, block(j)], "p t (c i)"),
                 SUB,
             )
 
-        def late_piece(j, first, last, slot=None):
-            piece = values(f"late{j}_{first}", last - first, slot)
-            nc.scalar.copy(piece[:], late_banks[j][:, first:last])
-            return j, first, piece[:]
+        probs1 = [probabilities(1, w1, x1, j, banks1[j], prob_tile(j)) for j in range(2)]
+        late_banks.extend(product((4, 3)[j], xm0b, j, g0, E5M2, HALF) for j in range(2))
+        scatter(2, 0, piece("late2", late_banks[2], 0, N))
+        for j in range(2):
+            make_g1(j, probs1[j])
+        probs1.extend(probabilities(1, w1, x1, j, banks1[j], prob_tile(j)) for j in (2, 3))
+        xm1a_values = tile("xm1a_values", [HALF, PACK], BF16)
+        weave_blocks(xm1a_values[:], xm_raw1[:, :, 0:HALF])
+        xm1a = packed("xm1a", HALF)
+        quantize(xm1a, 0, xm1a_values[:], E4M3)
+        quantize(g1, HALF, g1_values[:], E5M2)
+        scatter(3, 0, piece("late3", late_banks[3], 0, N, "weighted10"))
+        for j in (2, 3):
+            make_g1(j, probs1[j])
+        scatter(0, N, piece("last0a", product(5, xm1a, 0, g1, E5M2), HALF, N))
+        xm1b_values = tile("xm1b_values", [HALF, PACK], BF16, "prob3")
+        weave_blocks(xm1b_values[:], xm_raw1[:, :, HALF:D])
+        xm1b = packed("xm1b", HALF)
+        quantize(g1, N, g1_values[:], E5M2)
+        quantize(xm1b, 0, xm1b_values[:], E4M3)
+        scatter(1, N, piece("last1a", product(2, xm1a, 1, g1, E5M2), HALF, N, "weighted11"))
 
-        probs1 = [probabilities(1, w1, x1, j, banks1[j]) for j in range(2)]
-        late_pieces = []
-        make_g1(0, probs1[0])
-        probs1.append(probabilities(1, w1, x1, 2, banks1[2]))
-        late_pieces.append(late_piece(1, 0, N))
-        make_g1(1, probs1[1])
-        probs1.append(probabilities(1, w1, x1, 3, banks1[3]))
-        late_banks.extend(product(j + 1, xm0_rest, j, g0, E5M2, HALF) for j in (2, 3))
-        late_pieces.append(late_piece(2, 0, N))
-        late_pieces.append(late_piece(3, 0, HALF))
-        make_g1(2, probs1[2])
-        make_g1(3, probs1[3])
-        late_pieces.append(late_piece(3, HALF, N, slot="weighted1"))
-
-        xm1 = operand("xm1", slot=f"prob{BLOCKS - 1}")
-        cast_blocks(xm1, xm_raw1)
-        quantize(g1, 0, N, E5M2)
-        for c0, c1 in HALVES:
-            quantize(xm1, c0, c1, E4M3)
-        last = []
-        for j in range(BLOCKS):
-            bank = product((5, 2, 3, 6)[j], xm1, j, g1, E5M2, 0)
-            last.append(values(f"last{j}", N))
-            nc.scalar.copy(last[j][:], bank[:])
-
-        for j, first, src in late_pieces:
-            scatter(j, first, src)
-        for j in range(BLOCKS):
-            scatter(j, N, last[j][:])
+        def finish(j, first, values):
+            scatter(j, N + first, values)
             nc.sync.dma_start(out[block(j), :], out_tiles[j][:])
+
+        finish(0, HALF, piece("last0b", product(4, xm1a, 0, g1, E5M2, HALF), HALF, N))
+        finish(1, HALF, piece("last1b", product(3, xm1a, 1, g1, E5M2, HALF), HALF, N))
+        finish(2, 0, piece("last2", product(0, xm1b, 0, g1, E5M2, HALF), 0, N))
+        finish(3, 0, piece("last3", product(1, xm1b, 1, g1, E5M2, HALF), 0, N))

@@ -49,6 +49,8 @@ def tile_attend_gnce_w_kb_kernel(tc, xT, wT, y, wt, kb, xm, offs, out):
         nc.vector.memset(kb_table[0:KB_ROW, 0 : T // 2 - 1], 0.0)
         nc.vector.memset(kb_table[0:KB_ROW, T // 2 - 1 : T], 0.0)
         nc.scalar.dma_start(kb_table[KB_ROW:P, :], kb[KB_ROW:P, :])
+        weights = keep.tile([P, B, PACK], F32, name="weights")
+        nc.scalar.dma_start(weights[:], wt.rearrange("b (p t) o -> p b (t o)", t=PACK))
         ident = keep.tile([P, P], F32, name="ident")
         make_identity(nc, ident[:])
 
@@ -66,8 +68,6 @@ def tile_attend_gnce_w_kb_kernel(tc, xT, wT, y, wt, kb, xm, offs, out):
             planes.append(plane)
         xm_raw0 = [load("xm_raw0a", xm[0], 0, HALF)]
         y_raw0 = [load("y_raw0a", y[0], 0, HALF)]
-        weights = keep.tile([P, B, PACK], F32, name="weights")
-        nc.sync.dma_start(weights[:], wt.rearrange("b (p t) o -> p b (t o)", t=PACK))
         y_raw0.append(load("y_raw0b", y[0], HALF, N))
         x_raw1 = load("x_raw1", xT[1])
         xm_raw0.append(load("xm_raw0b", xm[0], HALF, D))
@@ -227,58 +227,61 @@ def tile_attend_gnce_w_kb_kernel(tc, xT, wT, y, wt, kb, xm, offs, out):
         weave_blocks(w1_values[:], waiting[:, :, HALF:REST])
         x1_values = tile("x1_values", [R, PACK], BF16, "x0_codes")
         weave_blocks(x1_values[:], x_raw1[:])
-        xm0b_values = tile("xm0b_values", [HALF, PACK], BF16)
-        weave_blocks(xm0b_values[:], xm_raw0[1][:])
+        weighted_y1_row = tile("weighted_y1", [PACK * N], F32)
+        weighted_y1 = weighted_y1_row[:].rearrange("p (h t c) -> p h t c", h=2, t=PACK)
+        xm0b_values = weighted_y1_row[:, HALF + BLK : REST + BLK].bitcast(BF16).rearrange("p (c t) -> p c t", t=PACK)
+        weave_blocks(xm0b_values, xm_raw0[1][:])
         quantize(g0, N, g0_values[:], E5M2)
         w1 = packed("w1", N, "diff01")
         quantize(w1, 0, w1_values[:], E4M3)
         x1 = packed("x1", R, "g0_values")
         quantize(x1, 0, x1_values[:], E4M3)
         xm0b = packed("xm0b", HALF)
-        quantize(xm0b, 0, xm0b_values[:], E4M3)
+        quantize(xm0b, 0, xm0b_values, E4M3)
         late_banks = [product((5, 2)[j], xm0a, j, g0, E5M2, HALF) for j in range(2)]
         scatter(0, HALF, piece("late0", late_banks[0], HALF, N, "x0_codes"))
         scatter(1, HALF, piece("late1", late_banks[1], HALF, N))
 
-        weighted_y1 = tile("weighted_y1", [PACK, N], F32, "xm0b_values")
         for t in range(PACK):
-            nc.gpsimd.tensor_scalar(weighted_y1[:, t, :], y_raw1[:, t, :], weights[:, 1, t : t + 1], 0.0, MULT, ADD)
+            labels = y_raw1[:, t, :].rearrange("p (h c) -> p h c", h=2)
+            nc.gpsimd.tensor_scalar(weighted_y1[:, :, t, :], labels, weights[:, 1, t : t + 1], 0.0, MULT, ADD)
         g1_values = tile("g1_values", [HALF, PACK], BF16)
         weighted1 = [tile(f"weighted1{h}", [2, PACK, BLK], F32) for h in range(2)]
-        banks1 = (6, 7, 6, 7)
+        banks1 = (6, 7, 0, 7)
 
         def make_g1(j, prob):
-            bank = turn(prob, banks1[j])
+            bank = turn(prob, (0, 7, 6, 7)[j])
             weighted = weighted1[j // 2][:, j % 2]
             for t in range(PACK):
                 nc.scalar.activation(weighted[:, t, :], bank[:, t, :], COPY, scale=weights[:, 1, t : t + 1])
-            nc.gpsimd.tensor_tensor(
+            (nc.vector if j == BLOCKS - 1 else nc.gpsimd).tensor_tensor(
                 by_lines(g1_values[:, block(j % 2), :], "p (c i) t"),
                 by_lines(weighted, "p t (c i)"),
-                by_lines(weighted_y1[:, :, block(j)], "p t (c i)"),
+                by_lines(weighted_y1[:, j // 2, :, block(j % 2)], "p t (c i)"),
                 SUB,
             )
 
-        probs1 = [probabilities(1, w1, x1, j, banks1[j], prob_tile(j)) for j in range(2)]
+        probs1 = [probabilities(1, w1, x1, j, banks1[j], prob_tile(j), (PACK, 1)[j]) for j in range(2)]
+        make_g1(0, probs1[0])
         late_banks.extend(product((4, 3)[j], xm0b, j, g0, E5M2, HALF) for j in range(2))
         scatter(2, 0, piece("late2", late_banks[2], 0, N))
-        for j in range(2):
-            make_g1(j, probs1[j])
+        make_g1(1, probs1[1])
         probs1.extend(probabilities(1, w1, x1, j, banks1[j], prob_tile(j)) for j in (2, 3))
+        scatter(3, 0, piece("late3a", late_banks[3], 0, HALF))
         xm1a_values = tile("xm1a_values", [HALF, PACK], BF16)
         weave_blocks(xm1a_values[:], xm_raw1[:, :, 0:HALF])
         xm1a = packed("xm1a", HALF)
         quantize(xm1a, 0, xm1a_values[:], E4M3)
         quantize(g1, HALF, g1_values[:], E5M2)
-        scatter(3, 0, piece("late3", late_banks[3], 0, N, "weighted10"))
+        scatter(3, HALF, piece("late3b", late_banks[3], HALF, N, "weighted10"))
         for j in (2, 3):
             make_g1(j, probs1[j])
         scatter(0, N, piece("last0a", product(5, xm1a, 0, g1, E5M2), HALF, N))
         xm1b_values = tile("xm1b_values", [HALF, PACK], BF16, "prob3")
         weave_blocks(xm1b_values[:], xm_raw1[:, :, HALF:D])
         xm1b = packed("xm1b", HALF)
-        quantize(g1, N, g1_values[:], E5M2)
         quantize(xm1b, 0, xm1b_values[:], E4M3)
+        quantize(g1, N, g1_values[:], E5M2)
         scatter(1, N, piece("last1a", product(2, xm1a, 1, g1, E5M2), HALF, N, "weighted11"))
 
         def finish(j, first, values):

@@ -223,28 +223,28 @@ def tile_attend_gnce_w_kb_kernel(tc, xT, wT, y, wt, kb, xm, offs, out):
         for j, bank_number in enumerate((4, 7)):
             scatter(j, 0, piece(f"early{j}", product(bank_number, xm0a, j, g0, E5M2), HALF, N))
 
-        w1_values = tile("w1_values", [N, PACK], BF16, "prob3")
+        w1_values = tile("w1_values", [N, PACK], BF16, "prob2")
         weave_blocks(w1_values[:], waiting[:, :, HALF:REST])
-        x1_values = tile("x1_values", [R, PACK], BF16, "x0_codes")
-        weave_blocks(x1_values[:], x_raw1[:])
-        weighted_y1_row = tile("weighted_y1", [PACK * N], F32)
-        weighted_y1 = weighted_y1_row[:].rearrange("p (h t c) -> p h t c", h=2, t=PACK)
-        xm0b_values = weighted_y1_row[:, HALF + BLK : REST + BLK].bitcast(BF16).rearrange("p (c t) -> p c t", t=PACK)
-        weave_blocks(xm0b_values, xm_raw0[1][:])
+        x1_values = [tile("x1a_values", [HALF, PACK], BF16, "x0_codes"), tile("x1b_values", [HALF, PACK], BF16)]
+        for h in range(2):
+            weave_blocks(x1_values[h][:], x_raw1[:, :, block(2 * h, 2)])
+        xm0b_values = tile("xm0b_values", [HALF, PACK], BF16)
+        weave_blocks(xm0b_values[:], xm_raw0[1][:])
         quantize(g0, N, g0_values[:], E5M2)
         w1 = packed("w1", N, "diff01")
         quantize(w1, 0, w1_values[:], E4M3)
         x1 = packed("x1", R, "g0_values")
-        quantize(x1, 0, x1_values[:], E4M3)
+        for h in range(2):
+            quantize(x1, h * HALF, x1_values[h][:], E4M3)
         xm0b = packed("xm0b", HALF)
-        quantize(xm0b, 0, xm0b_values, E4M3)
+        quantize(xm0b, 0, xm0b_values[:], E4M3)
         late_banks = [product((5, 2)[j], xm0a, j, g0, E5M2, HALF) for j in range(2)]
         scatter(0, HALF, piece("late0", late_banks[0], HALF, N, "x0_codes"))
         scatter(1, HALF, piece("late1", late_banks[1], HALF, N))
 
+        weighted_y1 = tile("weighted_y1", [PACK, N], F32, "xm0b_values")
         for t in range(PACK):
-            labels = y_raw1[:, t, :].rearrange("p (h c) -> p h c", h=2)
-            nc.gpsimd.tensor_scalar(weighted_y1[:, :, t, :], labels, weights[:, 1, t : t + 1], 0.0, MULT, ADD)
+            nc.gpsimd.tensor_scalar(weighted_y1[:, t, :], y_raw1[:, t, :], weights[:, 1, t : t + 1], 0.0, MULT, ADD)
         g1_values = tile("g1_values", [HALF, PACK], BF16)
         weighted1 = [tile(f"weighted1{h}", [2, PACK, BLK], F32) for h in range(2)]
         banks1 = (6, 7, 0, 7)
@@ -257,7 +257,7 @@ def tile_attend_gnce_w_kb_kernel(tc, xT, wT, y, wt, kb, xm, offs, out):
             (nc.vector if j == BLOCKS - 1 else nc.gpsimd).tensor_tensor(
                 by_lines(g1_values[:, block(j % 2), :], "p (c i) t"),
                 by_lines(weighted, "p t (c i)"),
-                by_lines(weighted_y1[:, j // 2, :, block(j % 2)], "p t (c i)"),
+                by_lines(weighted_y1[:, :, block(j)], "p t (c i)"),
                 SUB,
             )
 

@@ -27,6 +27,7 @@ HALF = 256
 REST = B * N - HALF
 LANES = 16
 LINE = 4
+PAIR = 2
 KB_ROW = P - 1
 
 
@@ -36,8 +37,8 @@ def tile_attend_gnce_w_kb_kernel(tc, xT, wT, y, wt, kb, xm, offs, out):
         keep = ctx.enter_context(tc.tile_pool(name="keep", bufs=1))
         psum = ctx.enter_context(tc.psum_pool(name="psum", bufs=1))
 
-        def tile(name, shape, dtype, slot=None):
-            return keep.tile([P] + shape, dtype, name=name, tag=slot or name, align_bytes=64)
+        def tile(name, shape, dtype, place=None):
+            return keep.tile([P] + shape, dtype, name=name, tag=place or name, align_bytes=64)
 
         offsets = keep.tile([P, B * N // LANES], U16, name="offsets")
         nc.sync.dma_start(offsets[:], offs)
@@ -49,8 +50,6 @@ def tile_attend_gnce_w_kb_kernel(tc, xT, wT, y, wt, kb, xm, offs, out):
         nc.vector.memset(kb_table[0:KB_ROW, 0 : T // 2 - 1], 0.0)
         nc.vector.memset(kb_table[0:KB_ROW, T // 2 - 1 : T], 0.0)
         nc.scalar.dma_start(kb_table[KB_ROW:P, :], kb[KB_ROW:P, :])
-        weights = keep.tile([P, B, PACK], F32, name="weights")
-        nc.scalar.dma_start(weights[:], wt.rearrange("b (p t) o -> p b (t o)", t=PACK))
         ident = keep.tile([P, P], F32, name="ident")
         make_identity(nc, ident[:])
 
@@ -68,6 +67,8 @@ def tile_attend_gnce_w_kb_kernel(tc, xT, wT, y, wt, kb, xm, offs, out):
             planes.append(plane)
         xm_raw0 = [load("xm_raw0a", xm[0], 0, HALF)]
         y_raw0 = [load("y_raw0a", y[0], 0, HALF)]
+        weights = keep.tile([P, B, PACK], F32, name="weights")
+        nc.sync.dma_start(weights[:], wt.rearrange("b (p t) o -> p b (t o)", t=PACK))
         y_raw0.append(load("y_raw0b", y[0], HALF, N))
         x_raw1 = load("x_raw1", xT[1])
         xm_raw0.append(load("xm_raw0b", xm[0], HALF, D))
@@ -93,8 +94,8 @@ def tile_attend_gnce_w_kb_kernel(tc, xT, wT, y, wt, kb, xm, offs, out):
         def block(j, count=1):
             return slice(j * BLK, (j + count) * BLK)
 
-        def packed(name, width, slot=None):
-            return tile(name + "_codes", [width], U32, slot), tile(name + "_scales", [width], U8)
+        def packed(name, width, place=None):
+            return tile(name + "_codes", [width], U32, place), tile(name + "_scales", [width], U8)
 
         def by_lines(ap, order):
             return ap.rearrange(order + " -> p c t i", i=LINE)
@@ -151,13 +152,13 @@ def tile_attend_gnce_w_kb_kernel(tc, xT, wT, y, wt, kb, xm, offs, out):
                 nc.tensor.transpose(bank[:, t - first, :], prob[:, t, :], ident[:])
             return bank
 
-        def piece(name, bank, first, last, slot=None):
-            values = tile(name, [last - first], F32, slot)
-            nc.scalar.copy(values[:], bank[:, first:last])
-            return values
+        def piece(name, bank, first, last, place=None):
+            sums = tile(name, [last - first], F32, place)
+            nc.scalar.copy(sums[:], bank[:, first:last])
+            return sums
 
-        def scatter(j, first, values):
-            nc.vector.tensor_copy(out_tiles[j][:].indirect(listed(first, first + values.shape[1])), values[:])
+        def scatter(j, first, sums):
+            nc.vector.tensor_copy(out_tiles[j][:].indirect(listed(first, first + sums.shape[1])), sums[:])
 
         columns = tile("columns", [PACK * REST - N + PACK * N], BF16)
         waiting = columns[:, 0 : PACK * REST].rearrange("p (t c) -> p t c", t=PACK)
@@ -214,9 +215,9 @@ def tile_attend_gnce_w_kb_kernel(tc, xT, wT, y, wt, kb, xm, offs, out):
         diff23 = tile("diff23", [HALF, PACK], F32, "diff01")
         for j in range(2):
             nc.vector.tensor_tensor(
-                diff23[:, block(j), :].rearrange("p (c i) t -> p c t i", i=2),
-                turned23[j][:].rearrange("p t (c i) -> p c t i", i=2),
-                y_raw0[1][:, :, block(j)].rearrange("p t (c i) -> p c t i", i=2),
+                diff23[:, block(j), :].rearrange("p (c i) t -> p c t i", i=PAIR),
+                turned23[j][:].rearrange("p t (c i) -> p c t i", i=PAIR),
+                y_raw0[1][:, :, block(j)].rearrange("p t (c i) -> p c t i", i=PAIR),
                 SUB,
             )
             nc.gpsimd.tensor_tensor(g0_values[:, block(j), :], diff23[:, block(j), :], wt0_woven, MULT)
@@ -247,10 +248,10 @@ def tile_attend_gnce_w_kb_kernel(tc, xT, wT, y, wt, kb, xm, offs, out):
             nc.gpsimd.tensor_scalar(weighted_y1[:, t, :], y_raw1[:, t, :], weights[:, 1, t : t + 1], 0.0, MULT, ADD)
         g1_values = tile("g1_values", [HALF, PACK], BF16)
         weighted1 = [tile(f"weighted1{h}", [2, PACK, BLK], F32) for h in range(2)]
-        banks1 = (6, 7, 0, 7)
+        score_banks1, turn_banks1 = (6, 7, 0, 7), (0, 7, 6, 7)
 
         def make_g1(j, prob):
-            bank = turn(prob, (0, 7, 6, 7)[j])
+            bank = turn(prob, turn_banks1[j])
             weighted = weighted1[j // 2][:, j % 2]
             for t in range(PACK):
                 nc.scalar.activation(weighted[:, t, :], bank[:, t, :], COPY, scale=weights[:, 1, t : t + 1])
@@ -261,12 +262,12 @@ def tile_attend_gnce_w_kb_kernel(tc, xT, wT, y, wt, kb, xm, offs, out):
                 SUB,
             )
 
-        probs1 = [probabilities(1, w1, x1, j, banks1[j], prob_tile(j), (PACK, 1)[j]) for j in range(2)]
+        probs1 = [probabilities(1, w1, x1, j, score_banks1[j], prob_tile(j), (PACK, 1)[j]) for j in range(2)]
         make_g1(0, probs1[0])
         late_banks.extend(product((4, 3)[j], xm0b, j, g0, E5M2, HALF) for j in range(2))
         scatter(2, 0, piece("late2", late_banks[2], 0, N))
         make_g1(1, probs1[1])
-        probs1.extend(probabilities(1, w1, x1, j, banks1[j], prob_tile(j)) for j in (2, 3))
+        probs1.extend(probabilities(1, w1, x1, j, score_banks1[j], prob_tile(j)) for j in (2, 3))
         scatter(3, 0, piece("late3a", late_banks[3], 0, HALF))
         xm1a_values = tile("xm1a_values", [HALF, PACK], BF16)
         weave_blocks(xm1a_values[:], xm_raw1[:, :, 0:HALF])
@@ -284,9 +285,13 @@ def tile_attend_gnce_w_kb_kernel(tc, xT, wT, y, wt, kb, xm, offs, out):
         quantize(g1, N, g1_values[:], E5M2)
         scatter(1, N, piece("last1a", product(2, xm1a, 1, g1, E5M2), HALF, N, "weighted11"))
 
-        def finish(j, first, values):
-            scatter(j, N + first, values)
-            nc.sync.dma_start(out[block(j), :], out_tiles[j][:])
+        def finish(j, first, sums):
+            scatter(j, N + first, sums)
+            if j < BLOCKS - 1:
+                nc.sync.dma_start(out[block(j), :], out_tiles[j][:])
+            else:
+                nc.sync.dma_start(out[block(j), 0 : T // 2], out_tiles[j][:, 0 : T // 2])
+                nc.scalar.dma_start(out[block(j), T // 2 : T], out_tiles[j][:, T // 2 : T])
 
         finish(0, HALF, piece("last0b", product(4, xm1a, 0, g1, E5M2, HALF), HALF, N))
         finish(1, HALF, piece("last1b", product(3, xm1a, 1, g1, E5M2, HALF), HALF, N))

@@ -52,6 +52,8 @@ def tile_attend_gnce_w_kb_kernel(tc, xT, wT, y, wt, kb, xm, offs, out):
         nc.scalar.dma_start(kb_table[KB_ROW:P, :], kb[KB_ROW:P, :])
         ident = keep.tile([P, P], F32, name="ident")
         make_identity(nc, ident[:])
+        warm = keep.tile([P, 1], F32, name="warm")
+        nc.scalar.activation(warm[:], ident[:, 0:1], SIGMOID)
 
         def load(name, src, c0=0, c1=N):
             raw = tile(name, [PACK, c1 - c0], F32)
@@ -60,13 +62,12 @@ def tile_attend_gnce_w_kb_kernel(tc, xT, wT, y, wt, kb, xm, offs, out):
 
         planes = []
         for t in range(PACK):
-            if t == PACK - 1:
-                x_raw0 = load("x_raw0", xT[0])
             plane = keep.tile([P, T], F32, name=f"plane{t}")
             nc.sync.dma_start(plane[:], wT.rearrange("(p t) c -> p t c", t=PACK)[:, t, :])
             planes.append(plane)
-        xm_raw0 = [load("xm_raw0a", xm[0], 0, HALF)]
+        x_raw0 = load("x_raw0", xT[0])
         y_raw0 = [load("y_raw0a", y[0], 0, HALF)]
+        xm_raw0 = [load("xm_raw0a", xm[0], 0, HALF)]
         weights = keep.tile([P, B, PACK], F32, name="weights")
         nc.sync.dma_start(weights[:], wt.rearrange("b (p t) o -> p b (t o)", t=PACK))
         y_raw0.append(load("y_raw0b", y[0], HALF, N))
@@ -115,14 +116,14 @@ def tile_attend_gnce_w_kb_kernel(tc, xT, wT, y, wt, kb, xm, offs, out):
                 in_=values.rearrange("p c t -> p (c t)"),
             )
 
-        def product(bank_number, lhs, j, rhs, rhs_fmt, first=0):
-            bank = psum.tile([P, N], F32, name="product", tag=f"bank{bank_number}")
+        def product(bank_number, lhs, j, rhs, rhs_fmt, first=0, width=N):
+            bank = psum.tile([P, width], F32, name="product", tag=f"bank{bank_number}")
             nc.tensor.matmul_mx(
                 out=bank[:],
                 lhsT=lhs[0][:, block(j)].bitcast(E4M3),
                 lhsT_scale=lhs[1][:, block(j)],
-                rhs=rhs[0][:, first : first + N].bitcast(rhs_fmt),
-                rhs_scale=rhs[1][:, first : first + N],
+                rhs=rhs[0][:, first : first + width].bitcast(rhs_fmt),
+                rhs_scale=rhs[1][:, first : first + width],
                 start=True,
                 stop=True,
             )
@@ -160,12 +161,17 @@ def tile_attend_gnce_w_kb_kernel(tc, xT, wT, y, wt, kb, xm, offs, out):
         def scatter(j, first, sums):
             nc.vector.tensor_copy(out_tiles[j][:].indirect(listed(first, first + sums.shape[1])), sums[:])
 
-        columns = tile("columns", [PACK * REST - N + PACK * N], BF16)
-        waiting = columns[:, 0 : PACK * REST].rearrange("p (t c) -> p t c", t=PACK)
-        w0_values = columns[:, PACK * REST - N :].rearrange("p (c t) -> p c t", t=PACK)
+        columns = tile("columns", [2 * B * N * 2 + HALF * 2], BF16)
+        pairs = columns[:, 0 : 2 * B * N * 2].rearrange("p (h c e) -> p h c e", h=2, e=2)
+        pair_words = columns[:, 0 : 2 * B * N * 2].bitcast(U32).rearrange("p (h c) -> p c h", h=2)
+        x0b_values = columns[:, 2 * B * N * 2 - HALF * 2 :].rearrange("p (c t) -> p c t", t=PACK)
 
-        def gather_waiting(t, first, last):
-            gather(waiting[:, t, first - HALF : last - HALF], t, first, last)
+        def gather_pairs(t, first, last):
+            gather(pairs[:, t // 2, first:last, t % 2], t, first, last)
+
+        def join(values, first):
+            words = values.rearrange("p c t -> p (c t)").bitcast(U32).rearrange("p (c h) -> p c h", h=2)
+            nc.scalar.copy(words, pair_words[:, first : first + values.shape[1], :])
 
         x0, w0 = packed("x0", R), packed("w0", N)
         g_ops = [packed(f"g{b}", HALF + N) for b in range(B)]
@@ -174,41 +180,57 @@ def tile_attend_gnce_w_kb_kernel(tc, xT, wT, y, wt, kb, xm, offs, out):
             nc.gpsimd.memset(scales[:, 0:HALF].bitcast(U32), 0)
         g0, g1 = g_ops
 
-        for t in range(PACK - 1):
-            gather(w0_values[:, 0:HALF, t], t, 0, HALF)
-            gather_waiting(t, HALF, B * N if t < PACK - 2 else REST)
-        x0_values = tile("x0_values", [R, PACK], BF16)
-        weave_blocks(x0_values[:, 0:HALF, :], x_raw0[:, :, 0:HALF])
-        weave(nc.vector.tensor_copy, x0_values[:, HALF:R, :], x_raw0[:, :, HALF:R])
-        gather_waiting(PACK - 2, REST, B * N)
-        quantize(x0, 0, x0_values[:], E4M3)
-        gather(w0_values[:, 0:HALF, PACK - 1], PACK - 1, 0, HALF)
-        for j in range(2):
-            quantize(w0, j * BLK, w0_values[:, block(j), :], E4M3)
-        gather_waiting(PACK - 1, HALF, N)
-        weave(nc.vector.tensor_copy, w0_values[:, HALF:N, :], waiting[:, :, 0:HALF])
-        quantize(w0, HALF, w0_values[:, HALF:N, :], E4M3)
-        gather_waiting(PACK - 1, N, REST)
-        gather_waiting(PACK - 1, REST, B * N)
+        for t in range(2):
+            gather_pairs(t, 0, B * N)
+        gather_pairs(2, 0, REST)
+        w0_values = [tile(f"w0{h}_values", [HALF, PACK], BF16) for h in range(2)]
+        for h in range(2):
+            gather_pairs(3, h * HALF, (h + 1) * HALF)
+            join(w0_values[h][:], h * HALF)
+        gather_pairs(3, N, REST)
+        w1a_values = tile("w1a_values", [HALF, PACK], BF16)
+        join(w1a_values[:], N)
+        for h in range(2):
+            quantize(w0, h * HALF, w0_values[h][:], E4M3)
+        x0_values = [tile("x0a_values", [HALF, PACK], BF16)[:], x0b_values]
+        for h, copy in enumerate((nc.vector.tensor_copy, nc.scalar.copy)):
+            copy(
+                x0_values[h].rearrange("p (q m) t -> p m t q", q=2),
+                x_raw0[:].rearrange("p t (m q) -> p m t q", q=PACK)[:, :, :, 2 * h : 2 * h + 2],
+            )
+        for h in range(2):
+            quantize(x0, h * HALF, x0_values[h], E4M3)
+        for t in (2, 3):
+            gather_pairs(t, REST, B * N)
 
         g0_values = tile("g0_values", [HALF, PACK], BF16)
         wt0_by_lines = weights[:, 0, :].unsqueeze(1).unsqueeze(3).to_broadcast([P, BLK // LINE, PACK, LINE])
         wt0_woven = weights[:, 0, :].unsqueeze(1).to_broadcast([P, BLK, PACK])
 
-        prob = probabilities(0, w0, x0, 0, 4, prob_tile(0), PACK)
-        first_parts = [(0, turn(prob, 6, 0, 2)), (2, turn(prob, 0, 2, PACK))]
-        turned = turn(probabilities(0, w0, x0, 1, 5, prob_tile(1)), 1)
+        def sigmoid(prob, scores, b, j):
+            nc.scalar.activation(prob, scores, SIGMOID, bias=bias[:, b * BLOCKS + j : b * BLOCKS + j + 1])
+
         diff01 = tile("diff01", [2, PACK, BLK], F32)
-        for t, bank in first_parts:
-            nc.vector.tensor_tensor(diff01[:, 0, t : t + 2, :], bank[:], y_raw0[0][:, t : t + 2, block(0)], SUB)
-        nc.vector.tensor_tensor(diff01[:, 1], turned[:], y_raw0[0][:, :, block(1)], SUB)
+        for h in range(2):
+            for j in range(2):
+                scores = product(4 - 2 * h + j, w0, j, x0, E4M3, h * HALF, HALF)
+                prob = tile(f"first_prob{j}{h}", [2, BLK], F32)
+                sigmoid(prob[:].rearrange("p q m -> p (q m)"), scores[:], 0, j)
+                bank = turn(prob, 6 - 6 * h + j, 0, 2)
+                ts = slice(2 * h, 2 * h + 2)
+                nc.vector.tensor_tensor(diff01[:, j, ts, :], bank[:], y_raw0[0][:, ts, block(j)], SUB)
         for j in range(2):
             nc.vector.tensor_tensor(
                 by_lines(g0_values[:, block(j), :], "p (c i) t"), by_lines(diff01[:, j], "p t (c i)"), wt0_by_lines, MULT
             )
-        turned23 = [turn(probabilities(0, w0, x0, j, (5, 0)[j - 2], prob_tile(j)), j) for j in (2, 3)]
         xm0a_values = tile("xm0a_values", [HALF, PACK], BF16)
-        weave_blocks(xm0a_values[:], xm_raw0[0][:])
+        for j in range(2):
+            nc.gpsimd.tensor_copy(xm0a_values[:, block(j), :], xm_raw0[0][:, :, block(j)].rearrange("p t c -> p c t"))
+        turned23 = []
+        for j in (2, 3):
+            prob = prob_tile(j)
+            sigmoid(prob.rearrange("p q m -> p (q m)"), product(4 + j, w0, j, x0, E4M3)[:], 0, j)
+            turned23.append(turn(prob, 2 + j))
         xm0a = packed("xm0a", HALF)
         quantize(xm0a, 0, xm0a_values[:], E4M3)
         quantize(g0, HALF, g0_values[:], E5M2)
@@ -221,11 +243,11 @@ def tile_attend_gnce_w_kb_kernel(tc, xT, wT, y, wt, kb, xm, offs, out):
                 SUB,
             )
             nc.gpsimd.tensor_tensor(g0_values[:, block(j), :], diff23[:, block(j), :], wt0_woven, MULT)
-        for j, bank_number in enumerate((4, 7)):
+        for j, bank_number in enumerate((0, 1)):
             scatter(j, 0, piece(f"early{j}", product(bank_number, xm0a, j, g0, E5M2), HALF, N))
 
-        w1_values = tile("w1_values", [N, PACK], BF16, "prob2")
-        weave_blocks(w1_values[:], waiting[:, :, HALF:REST])
+        w1_values = [w1a_values, tile("w1b_values", [HALF, PACK], BF16, "prob2")]
+        join(w1_values[1][:], REST)
         x1_values = [tile("x1a_values", [HALF, PACK], BF16, "x0_codes"), tile("x1b_values", [HALF, PACK], BF16)]
         for h in range(2):
             weave_blocks(x1_values[h][:], x_raw1[:, :, block(2 * h, 2)])
@@ -233,7 +255,8 @@ def tile_attend_gnce_w_kb_kernel(tc, xT, wT, y, wt, kb, xm, offs, out):
         weave_blocks(xm0b_values[:], xm_raw0[1][:])
         quantize(g0, N, g0_values[:], E5M2)
         w1 = packed("w1", N, "diff01")
-        quantize(w1, 0, w1_values[:], E4M3)
+        for h in range(2):
+            quantize(w1, h * HALF, w1_values[h][:], E4M3)
         x1 = packed("x1", R, "g0_values")
         for h in range(2):
             quantize(x1, h * HALF, x1_values[h][:], E4M3)

@@ -28,6 +28,7 @@ REST = B * N - HALF
 LANES = 16
 LINE = 4
 PAIR = 2
+RUN = 64
 KB_ROW = P - 1
 
 
@@ -66,10 +67,10 @@ def tile_attend_gnce_w_kb_kernel(tc, xT, wT, y, wt, kb, xm, offs, out):
             nc.sync.dma_start(plane[:], wT.rearrange("(p t) c -> p t c", t=PACK)[:, t, :])
             planes.append(plane)
         x_raw0 = load("x_raw0", xT[0])
-        y_raw0 = [load("y_raw0a", y[0], 0, HALF)]
-        xm_raw0 = [load("xm_raw0a", xm[0], 0, HALF)]
         weights = keep.tile([P, B, PACK], F32, name="weights")
         nc.sync.dma_start(weights[:], wt.rearrange("b (p t) o -> p b (t o)", t=PACK))
+        y_raw0 = [load("y_raw0a", y[0], 0, HALF)]
+        xm_raw0 = [load("xm_raw0a", xm[0], 0, HALF)]
         y_raw0.append(load("y_raw0b", y[0], HALF, N))
         x_raw1 = load("x_raw1", xT[1])
         xm_raw0.append(load("xm_raw0b", xm[0], HALF, D))
@@ -161,10 +162,11 @@ def tile_attend_gnce_w_kb_kernel(tc, xT, wT, y, wt, kb, xm, offs, out):
         def scatter(j, first, sums):
             nc.vector.tensor_copy(out_tiles[j][:].indirect(listed(first, first + sums.shape[1])), sums[:])
 
-        columns = tile("columns", [2 * B * N * 2 + HALF * 2], BF16)
+        columns = tile("columns", [2 * B * N * 2 + PACK * HALF * 2], BF16)
         pairs = columns[:, 0 : 2 * B * N * 2].rearrange("p (h c e) -> p h c e", h=2, e=2)
         pair_words = columns[:, 0 : 2 * B * N * 2].bitcast(U32).rearrange("p (h c) -> p c h", h=2)
-        x0b_values = columns[:, 2 * B * N * 2 - HALF * 2 :].rearrange("p (c t) -> p c t", t=PACK)
+        x0b_values = columns[:, 2 * B * N * 2 - HALF * 2 : 2 * B * N * 2 + HALF * 2].rearrange("p (c t) -> p c t", t=PACK)
+        weighted_y0 = columns[:, 2 * B * N * 2 :].bitcast(F32).rearrange("p (u t i) -> p t u i", t=PACK, i=RUN)
 
         def gather_pairs(t, first, last):
             gather(pairs[:, t // 2, first:last, t % 2], t, first, last)
@@ -173,7 +175,7 @@ def tile_attend_gnce_w_kb_kernel(tc, xT, wT, y, wt, kb, xm, offs, out):
             words = values.rearrange("p c t -> p (c t)").bitcast(U32).rearrange("p (c h) -> p c h", h=2)
             nc.scalar.copy(words, pair_words[:, first : first + values.shape[1], :])
 
-        x0, w0 = packed("x0", R), packed("w0", N)
+        x0 = packed("x0", R)
         g_ops = [packed(f"g{b}", HALF + N) for b in range(B)]
         for codes, scales in g_ops:
             nc.gpsimd.memset(codes[:, 0:HALF], 0)
@@ -188,10 +190,8 @@ def tile_attend_gnce_w_kb_kernel(tc, xT, wT, y, wt, kb, xm, offs, out):
             gather_pairs(3, h * HALF, (h + 1) * HALF)
             join(w0_values[h][:], h * HALF)
         gather_pairs(3, N, REST)
-        w1a_values = tile("w1a_values", [HALF, PACK], BF16)
-        join(w1a_values[:], N)
-        for h in range(2):
-            quantize(w0, h * HALF, w0_values[h][:], E4M3)
+        w0 = [packed("w0a", HALF)]
+        quantize(w0[0], 0, w0_values[0][:], E4M3)
         x0_values = [tile("x0a_values", [HALF, PACK], BF16)[:], x0b_values]
         for h, copy in enumerate((nc.vector.tensor_copy, nc.scalar.copy)):
             copy(
@@ -200,40 +200,58 @@ def tile_attend_gnce_w_kb_kernel(tc, xT, wT, y, wt, kb, xm, offs, out):
             )
         for h in range(2):
             quantize(x0, h * HALF, x0_values[h], E4M3)
+        w1a_values = tile("w1a_values", [HALF, PACK], BF16, "x_raw0")
+        join(w1a_values[:], N)
+        w0.append(packed("w0b", HALF, "x0a_values"))
+        quantize(w0[1], 0, w0_values[1][:], E4M3)
         for t in (2, 3):
             gather_pairs(t, REST, B * N)
 
         g0_values = tile("g0_values", [HALF, PACK], BF16)
-        wt0_by_lines = weights[:, 0, :].unsqueeze(1).unsqueeze(3).to_broadcast([P, BLK // LINE, PACK, LINE])
+
+        def runs(ap):
+            return ap.rearrange("p (u i) -> p u i", i=RUN)
+
+        for t in range(PACK):
+            nc.gpsimd.tensor_scalar(weighted_y0[:, t], runs(y_raw0[0][:, t, :]), weights[:, 0, t : t + 1], 0.0, MULT, ADD)
         wt0_woven = weights[:, 0, :].unsqueeze(1).to_broadcast([P, BLK, PACK])
 
         def sigmoid(prob, scores, b, j):
             nc.scalar.activation(prob, scores, SIGMOID, bias=bias[:, b * BLOCKS + j : b * BLOCKS + j + 1])
 
-        diff01 = tile("diff01", [2, PACK, BLK], F32)
+        g_planes = tile("diff01", [2, PACK, BLK], BF16)
         for h in range(2):
             for j in range(2):
-                scores = product(4 - 2 * h + j, w0, j, x0, E4M3, h * HALF, HALF)
+                scores = product(4 - 2 * h + j, w0[0], j, x0, E4M3, h * HALF, HALF)
                 prob = tile(f"first_prob{j}{h}", [2, BLK], F32)
                 sigmoid(prob[:].rearrange("p q m -> p (q m)"), scores[:], 0, j)
                 bank = turn(prob, 6 - 6 * h + j, 0, 2)
-                ts = slice(2 * h, 2 * h + 2)
-                nc.vector.tensor_tensor(diff01[:, j, ts, :], bank[:], y_raw0[0][:, ts, block(j)], SUB)
-        for j in range(2):
-            nc.vector.tensor_tensor(
-                by_lines(g0_values[:, block(j), :], "p (c i) t"), by_lines(diff01[:, j], "p t (c i)"), wt0_by_lines, MULT
-            )
-        xm0a_values = tile("xm0a_values", [HALF, PACK], BF16)
-        for j in range(2):
-            nc.gpsimd.tensor_copy(xm0a_values[:, block(j), :], xm_raw0[0][:, :, block(j)].rearrange("p t c -> p c t"))
+                for t in (2 * h, 2 * h + 1):
+                    nc.vector.scalar_tensor_tensor(
+                        runs(g_planes[:, j, t, :]),
+                        runs(bank[:, t % 2, :]),
+                        weights[:, 0, t : t + 1],
+                        weighted_y0[:, t, 2 * j : 2 * j + 2, :],
+                        MULT,
+                        SUB,
+                    )
+                if h:
+                    weave(nc.vector.tensor_copy, g0_values[:, block(j), :], g_planes[:, j])
+        xm0a_values = tile("xm0a_values", [HALF, PACK], BF16, "first_prob10")
+        weave_blocks(xm0a_values[:], xm_raw0[0][:])
         turned23 = []
         for j in (2, 3):
             prob = prob_tile(j)
-            sigmoid(prob.rearrange("p q m -> p (q m)"), product(4 + j, w0, j, x0, E4M3)[:], 0, j)
+            sigmoid(prob.rearrange("p q m -> p (q m)"), product(4 + j, w0[1], j - 2, x0, E4M3)[:], 0, j)
             turned23.append(turn(prob, 2 + j))
         xm0a = packed("xm0a", HALF)
         quantize(xm0a, 0, xm0a_values[:], E4M3)
         quantize(g0, HALF, g0_values[:], E5M2)
+        w1b_values = tile("w1b_values", [HALF, PACK], BF16, "first_prob11")
+        join(w1b_values[:], REST)
+        w1 = packed("w1", N, "first_prob10")
+        for h, values in enumerate((w1a_values, w1b_values)):
+            quantize(w1, h * HALF, values[:], E4M3)
         diff23 = tile("diff23", [HALF, PACK], F32, "diff01")
         for j in range(2):
             nc.vector.tensor_tensor(
@@ -243,25 +261,22 @@ def tile_attend_gnce_w_kb_kernel(tc, xT, wT, y, wt, kb, xm, offs, out):
                 SUB,
             )
             nc.gpsimd.tensor_tensor(g0_values[:, block(j), :], diff23[:, block(j), :], wt0_woven, MULT)
-        for j, bank_number in enumerate((0, 1)):
-            scatter(j, 0, piece(f"early{j}", product(bank_number, xm0a, j, g0, E5M2), HALF, N))
+        early_banks = [product(j, xm0a, j, g0, E5M2) for j in range(2)]
+        scatter(0, 0, piece("early0", early_banks[0], HALF, N))
 
-        w1_values = [w1a_values, tile("w1b_values", [HALF, PACK], BF16, "prob2")]
-        join(w1_values[1][:], REST)
         x1_values = [tile("x1a_values", [HALF, PACK], BF16, "x0_codes"), tile("x1b_values", [HALF, PACK], BF16)]
         for h in range(2):
             weave_blocks(x1_values[h][:], x_raw1[:, :, block(2 * h, 2)])
         xm0b_values = tile("xm0b_values", [HALF, PACK], BF16)
         weave_blocks(xm0b_values[:], xm_raw0[1][:])
         quantize(g0, N, g0_values[:], E5M2)
-        w1 = packed("w1", N, "diff01")
-        for h in range(2):
-            quantize(w1, h * HALF, w1_values[h][:], E4M3)
-        x1 = packed("x1", R, "g0_values")
+        early1 = piece("early1", early_banks[1], HALF, N, "g0_values")
+        x1 = packed("x1", R, "diff01")
         for h in range(2):
             quantize(x1, h * HALF, x1_values[h][:], E4M3)
         xm0b = packed("xm0b", HALF)
         quantize(xm0b, 0, xm0b_values[:], E4M3)
+        scatter(1, 0, early1)
         late_banks = [product((5, 2)[j], xm0a, j, g0, E5M2, HALF) for j in range(2)]
         scatter(0, HALF, piece("late0", late_banks[0], HALF, N, "x0_codes"))
         scatter(1, HALF, piece("late1", late_banks[1], HALF, N))
@@ -278,7 +293,7 @@ def tile_attend_gnce_w_kb_kernel(tc, xT, wT, y, wt, kb, xm, offs, out):
             weighted = weighted1[j // 2][:, j % 2]
             for t in range(PACK):
                 nc.scalar.activation(weighted[:, t, :], bank[:, t, :], COPY, scale=weights[:, 1, t : t + 1])
-            (nc.vector if j == BLOCKS - 1 else nc.gpsimd).tensor_tensor(
+            nc.gpsimd.tensor_tensor(
                 by_lines(g1_values[:, block(j % 2), :], "p (c i) t"),
                 by_lines(weighted, "p t (c i)"),
                 by_lines(weighted_y1[:, :, block(j)], "p t (c i)"),
@@ -291,21 +306,20 @@ def tile_attend_gnce_w_kb_kernel(tc, xT, wT, y, wt, kb, xm, offs, out):
         scatter(2, 0, piece("late2", late_banks[2], 0, N))
         make_g1(1, probs1[1])
         probs1.extend(probabilities(1, w1, x1, j, score_banks1[j], prob_tile(j)) for j in (2, 3))
-        scatter(3, 0, piece("late3a", late_banks[3], 0, HALF))
         xm1a_values = tile("xm1a_values", [HALF, PACK], BF16)
         weave_blocks(xm1a_values[:], xm_raw1[:, :, 0:HALF])
         xm1a = packed("xm1a", HALF)
         quantize(xm1a, 0, xm1a_values[:], E4M3)
         quantize(g1, HALF, g1_values[:], E5M2)
-        scatter(3, HALF, piece("late3b", late_banks[3], HALF, N, "weighted10"))
+        scatter(3, 0, piece("late3", late_banks[3], 0, N, "weighted10"))
         for j in (2, 3):
             make_g1(j, probs1[j])
         scatter(0, N, piece("last0a", product(5, xm1a, 0, g1, E5M2), HALF, N))
         xm1b_values = tile("xm1b_values", [HALF, PACK], BF16, "prob3")
         weave_blocks(xm1b_values[:], xm_raw1[:, :, HALF:D])
-        xm1b = packed("xm1b", HALF)
-        quantize(xm1b, 0, xm1b_values[:], E4M3)
         quantize(g1, N, g1_values[:], E5M2)
+        xm1b = packed("xm1b", HALF, "xm0b_values")
+        quantize(xm1b, 0, xm1b_values[:], E4M3)
         scatter(1, N, piece("last1a", product(2, xm1a, 1, g1, E5M2), HALF, N, "weighted11"))
 
         def finish(j, first, sums):

@@ -157,10 +157,10 @@ def tile_attend_gnce_w_kb_kernel(tc, xT, wT, y, wt, kb, xm, offs, out):
         def piece(name, bank, first, last, place=None):
             sums = tile(name, [last - first], F32, place)
             nc.scalar.copy(sums[:], bank[:, first:last])
-            return sums
+            return sums[:]
 
         def scatter(j, first, sums):
-            nc.vector.tensor_copy(out_tiles[j][:].indirect(listed(first, first + sums.shape[1])), sums[:])
+            nc.vector.tensor_copy(out_tiles[j][:].indirect(listed(first, first + sums.shape[1])), sums)
 
         columns = tile("columns", [2 * B * N * 2 + PACK * HALF * 2], BF16)
         pairs = columns[:, 0 : 2 * B * N * 2].rearrange("p (h c e) -> p h c e", h=2, e=2)
@@ -242,7 +242,9 @@ def tile_attend_gnce_w_kb_kernel(tc, xT, wT, y, wt, kb, xm, offs, out):
         turned23 = []
         for j in (2, 3):
             prob = prob_tile(j)
-            sigmoid(prob.rearrange("p q m -> p (q m)"), product(4 + j, w0[1], j - 2, x0, E4M3)[:], 0, j)
+            scores = product(4 + j, w0[1], j - 2, x0, E4M3)
+            for h in range(2):
+                sigmoid(prob[:, 2 * h : 2 * h + 2, :].rearrange("p q m -> p (q m)"), scores[:, block(2 * h, 2)], 0, j)
             turned23.append(turn(prob, 2 + j))
         xm0a = packed("xm0a", HALF)
         quantize(xm0a, 0, xm0a_values[:], E4M3)
@@ -285,12 +287,11 @@ def tile_attend_gnce_w_kb_kernel(tc, xT, wT, y, wt, kb, xm, offs, out):
         for t in range(PACK):
             nc.gpsimd.tensor_scalar(weighted_y1[:, t, :], y_raw1[:, t, :], weights[:, 1, t : t + 1], 0.0, MULT, ADD)
         g1_values = tile("g1_values", [HALF, PACK], BF16)
-        weighted1 = [tile(f"weighted1{h}", [2, PACK, BLK], F32) for h in range(2)]
+        weighted01 = tile("weighted01", [2, PACK, BLK], F32)
         score_banks1, turn_banks1 = (6, 7, 0, 7), (0, 7, 6, 7)
 
-        def make_g1(j, prob):
+        def make_g1(j, prob, weighted):
             bank = turn(prob, turn_banks1[j])
-            weighted = weighted1[j // 2][:, j % 2]
             for t in range(PACK):
                 nc.scalar.activation(weighted[:, t, :], bank[:, t, :], COPY, scale=weights[:, 1, t : t + 1])
             nc.gpsimd.tensor_tensor(
@@ -301,26 +302,28 @@ def tile_attend_gnce_w_kb_kernel(tc, xT, wT, y, wt, kb, xm, offs, out):
             )
 
         probs1 = [probabilities(1, w1, x1, j, score_banks1[j], prob_tile(j), (PACK, 1)[j]) for j in range(2)]
-        make_g1(0, probs1[0])
+        make_g1(0, probs1[0], weighted01[:, 0])
         late_banks.extend(product((4, 3)[j], xm0b, j, g0, E5M2, HALF) for j in range(2))
         scatter(2, 0, piece("late2", late_banks[2], 0, N))
-        make_g1(1, probs1[1])
+        make_g1(1, probs1[1], weighted01[:, 1])
         probs1.extend(probabilities(1, w1, x1, j, score_banks1[j], prob_tile(j)) for j in (2, 3))
         xm1a_values = tile("xm1a_values", [HALF, PACK], BF16)
         weave_blocks(xm1a_values[:], xm_raw1[:, :, 0:HALF])
         xm1a = packed("xm1a", HALF)
         quantize(xm1a, 0, xm1a_values[:], E4M3)
         quantize(g1, HALF, g1_values[:], E5M2)
-        scatter(3, 0, piece("late3", late_banks[3], 0, N, "weighted10"))
-        for j in (2, 3):
-            make_g1(j, probs1[j])
+        late3_and_weighted3 = tile("late3_and_weighted3", [2, N], F32, "weighted01")
+        nc.scalar.copy(late3_and_weighted3[:, 0, :], late_banks[3][:])
+        scatter(3, 0, late3_and_weighted3[:, 0, :])
+        make_g1(2, probs1[2], tile("weighted2", [PACK, BLK], F32)[:])
+        make_g1(3, probs1[3], late3_and_weighted3[:, 1, :].rearrange("p (t c) -> p t c", t=PACK))
         scatter(0, N, piece("last0a", product(5, xm1a, 0, g1, E5M2), HALF, N))
         xm1b_values = tile("xm1b_values", [HALF, PACK], BF16, "prob3")
         weave_blocks(xm1b_values[:], xm_raw1[:, :, HALF:D])
         quantize(g1, N, g1_values[:], E5M2)
         xm1b = packed("xm1b", HALF, "xm0b_values")
         quantize(xm1b, 0, xm1b_values[:], E4M3)
-        scatter(1, N, piece("last1a", product(2, xm1a, 1, g1, E5M2), HALF, N, "weighted11"))
+        scatter(1, N, piece("last1a", product(2, xm1a, 1, g1, E5M2), HALF, N, "weighted01"))
 
         def finish(j, first, sums):
             scatter(j, N + first, sums)

@@ -24,11 +24,9 @@ PACK = 4
 BLK = 128
 BLOCKS = 4
 HALF = 256
-REST = B * N - HALF
 LANES = 16
 LINE = 4
 PAIR = 2
-RUN = 64
 KB_ROW = P - 1
 
 
@@ -41,11 +39,17 @@ def tile_attend_gnce_w_kb_kernel(tc, xT, wT, y, wt, kb, xm, offs, out):
         def tile(name, shape, dtype, place=None):
             return keep.tile([P] + shape, dtype, name=name, tag=place or name, align_bytes=64)
 
+        def bank(number, shape):
+            return psum.tile([P] + shape, F32, name=f"bank{number}", tag=f"bank{number}")
+
+        def block(j, count=1):
+            return slice(j * BLK, (j + count) * BLK)
+
         offsets = keep.tile([P, B * N // LANES], U16, name="offsets")
         nc.sync.dma_start(offsets[:], offs)
 
-        def listed(first, last):
-            return offsets[:, first // LANES : last // LANES]
+        def listed(first, count):
+            return offsets[:, first // LANES : (first + count) // LANES]
 
         kb_table = keep.tile([P, T], F32, name="kb_table")
         nc.vector.memset(kb_table[0:KB_ROW, 0 : T // 2 - 1], 0.0)
@@ -67,15 +71,18 @@ def tile_attend_gnce_w_kb_kernel(tc, xT, wT, y, wt, kb, xm, offs, out):
             nc.sync.dma_start(plane[:], wT.rearrange("(p t) c -> p t c", t=PACK)[:, t, :])
             planes.append(plane)
         x_raw0 = load("x_raw0", xT[0])
-        weights = keep.tile([P, B, PACK], F32, name="weights")
-        nc.sync.dma_start(weights[:], wt.rearrange("b (p t) o -> p b (t o)", t=PACK))
-        y_raw0 = [load("y_raw0a", y[0], 0, HALF)]
-        xm_raw0 = [load("xm_raw0a", xm[0], 0, HALF)]
-        y_raw0.append(load("y_raw0b", y[0], HALF, N))
         x_raw1 = load("x_raw1", xT[1])
-        xm_raw0.append(load("xm_raw0b", xm[0], HALF, D))
+        xm_raw0a = load("xm_raw0a", xm[0], 0, HALF)
+        y_raw0 = [load("y_raw0a", y[0], 0, HALF)]
+        wt_square = keep.tile([P, P], F32, name="wt_square")
+        nc.gpsimd.memset(wt_square[:, B * PACK : P], 0.0)
+        weights = wt_square[:, 0 : B * PACK].rearrange("p (b t) -> p b t", t=PACK)
+        nc.sync.dma_start(weights, wt.rearrange("b (p t) o -> p b (t o)", t=PACK))
+        xm_raw1a = load("xm_raw1a", xm[1], 0, HALF)
+        y_raw0.append(load("y_raw0b", y[0], HALF, N))
         y_raw1 = load("y_raw1", y[1])
-        xm_raw1 = load("xm_raw1", xm[1])
+        xm_raw0b = load("xm_raw0b", xm[0], HALF, D)
+        xm_raw1b = load("xm_raw1b", xm[1], HALF, D)
 
         out_tiles = []
         for j in range(BLOCKS):
@@ -87,27 +94,19 @@ def tile_attend_gnce_w_kb_kernel(tc, xT, wT, y, wt, kb, xm, offs, out):
         nc.vector.tensor_copy(kb_listed[:], kb_table[:].indirect(offsets[:]))
         bias = keep.tile([P, B * BLOCKS], F32, name="bias")
         for b in range(B):
-            bank = psum.tile([P, BLOCKS, BLK], F32, name="kb_turned", tag=f"bank{b}")
+            kb_turned = bank(b, [BLOCKS, BLK])
             for j in range(BLOCKS):
-                c0 = b * N + j * BLK
-                nc.tensor.transpose(bank[:, j, :], kb_listed[:, c0 : c0 + BLK], ident[:])
-            nc.scalar.copy(bias[:, b * BLOCKS : (b + 1) * BLOCKS], bank[:, :, KB_ROW])
-
-        def block(j, count=1):
-            return slice(j * BLK, (j + count) * BLK)
+                nc.tensor.transpose(kb_turned[:, j, :], kb_listed[:, block(b * BLOCKS + j)], ident[:])
+            nc.scalar.copy(bias[:, b * BLOCKS : (b + 1) * BLOCKS], kb_turned[:, :, KB_ROW])
 
         def packed(name, width, place=None):
             return tile(name + "_codes", [width], U32, place), tile(name + "_scales", [width], U8)
 
-        def by_lines(ap, order):
-            return ap.rearrange(order + " -> p c t i", i=LINE)
-
         def weave(copy, dst, src):
-            copy(by_lines(dst, "p (c i) t"), by_lines(src, "p t (c i)"))
+            copy(dst.rearrange("p (c i) t -> p c t i", i=LINE), src.rearrange("p t (c i) -> p c t i", i=LINE))
 
-        def weave_blocks(dst, src):
-            for j in range(src.shape[2] // BLK):
-                weave(nc.scalar.copy, dst[:, block(j), :], src[:, :, block(j)])
+        def weave_on_gpsimd(dst, src):
+            nc.gpsimd.tensor_scalar(dst, src.rearrange("p t c -> p c t"), 1.0, 0.0, MULT, ADD)
 
         def quantize(op, first, values, fmt):
             cols = slice(first, first + values.shape[1])
@@ -117,10 +116,9 @@ def tile_attend_gnce_w_kb_kernel(tc, xT, wT, y, wt, kb, xm, offs, out):
                 in_=values.rearrange("p c t -> p (c t)"),
             )
 
-        def product(bank_number, lhs, j, rhs, rhs_fmt, first=0, width=N):
-            bank = psum.tile([P, width], F32, name="product", tag=f"bank{bank_number}")
+        def product(dst, lhs, j, rhs, rhs_fmt, first, width):
             nc.tensor.matmul_mx(
-                out=bank[:],
+                out=dst,
                 lhsT=lhs[0][:, block(j)].bitcast(E4M3),
                 lhsT_scale=lhs[1][:, block(j)],
                 rhs=rhs[0][:, first : first + width].bitcast(rhs_fmt),
@@ -128,212 +126,163 @@ def tile_attend_gnce_w_kb_kernel(tc, xT, wT, y, wt, kb, xm, offs, out):
                 start=True,
                 stop=True,
             )
-            return bank
 
-        def gather(dst, t, first, last):
-            nc.vector.tensor_copy(dst, planes[t][:].indirect(listed(first, last)))
-
-        def probabilities(b, w_op, x_op, j, bank_number, prob, parts=1):
-            scores = product(bank_number, w_op, j, x_op, E4M3)
-            step = PACK // parts
-            for t in range(0, PACK, step):
-                nc.scalar.activation(
-                    prob[:, t : t + step, :],
-                    scores[:].rearrange("p (m t) -> p t m", t=PACK)[:, t : t + step, :],
-                    SIGMOID,
-                    bias=bias[:, b * BLOCKS + j : b * BLOCKS + j + 1],
-                )
+        def probabilities(b, j, w_op, x_op, number):
+            scores = bank(number, [R])
+            product(scores[:], w_op, j, x_op, E4M3, 0, R)
+            prob = tile(f"prob{b}{j}", [PACK, BLK], F32)
+            nc.scalar.activation(
+                prob[:],
+                scores[:].rearrange("p (m t) -> p t m", t=PACK),
+                SIGMOID,
+                bias=bias[:, b * BLOCKS + j : b * BLOCKS + j + 1],
+            )
             return prob
 
-        def prob_tile(j):
-            return tile(f"prob{j}", [PACK, BLK], F32)[:]
+        def turn(prob, number):
+            turned = bank(number, [PACK, BLK])
+            for t in range(PACK):
+                nc.tensor.transpose(turned[:, t, :], prob[:, t, :], ident[:])
+            return turned
 
-        def turn(prob, bank_number, first=0, last=PACK):
-            bank = psum.tile([P, last - first, BLK], F32, name="turned", tag=f"bank{bank_number}")
-            for t in range(first, last):
-                nc.tensor.transpose(bank[:, t - first, :], prob[:, t, :], ident[:])
-            return bank
-
-        def piece(name, bank, first, last, place=None):
-            sums = tile(name, [last - first], F32, place)
-            nc.scalar.copy(sums[:], bank[:, first:last])
-            return sums[:]
-
-        def scatter(j, first, sums):
-            nc.vector.tensor_copy(out_tiles[j][:].indirect(listed(first, first + sums.shape[1])), sums)
-
-        columns = tile("columns", [2 * B * N * 2 + PACK * HALF * 2], BF16)
-        pairs = columns[:, 0 : 2 * B * N * 2].rearrange("p (h c e) -> p h c e", h=2, e=2)
-        pair_words = columns[:, 0 : 2 * B * N * 2].bitcast(U32).rearrange("p (h c) -> p c h", h=2)
-        x0b_values = columns[:, 2 * B * N * 2 - HALF * 2 : 2 * B * N * 2 + HALF * 2].rearrange("p (c t) -> p c t", t=PACK)
-        weighted_y0 = columns[:, 2 * B * N * 2 :].bitcast(F32).rearrange("p (u t i) -> p t u i", t=PACK, i=RUN)
-
-        def gather_pairs(t, first, last):
-            gather(pairs[:, t // 2, first:last, t % 2], t, first, last)
-
-        def join(values, first):
-            words = values.rearrange("p c t -> p (c t)").bitcast(U32).rearrange("p (c h) -> p c h", h=2)
-            nc.scalar.copy(words, pair_words[:, first : first + values.shape[1], :])
-
-        x0 = packed("x0", R)
-        g_ops = [packed(f"g{b}", HALF + N) for b in range(B)]
-        for codes, scales in g_ops:
-            nc.gpsimd.memset(codes[:, 0:HALF], 0)
-            nc.gpsimd.memset(scales[:, 0:HALF].bitcast(U32), 0)
-        g0, g1 = g_ops
-
-        for t in range(2):
-            gather_pairs(t, 0, B * N)
-        gather_pairs(2, 0, REST)
-        w0_values = [tile(f"w0{h}_values", [HALF, PACK], BF16) for h in range(2)]
-        for h in range(2):
-            gather_pairs(3, h * HALF, (h + 1) * HALF)
-            join(w0_values[h][:], h * HALF)
-        gather_pairs(3, N, REST)
-        w0 = [packed("w0a", HALF)]
-        quantize(w0[0], 0, w0_values[0][:], E4M3)
-        x0_values = [tile("x0a_values", [HALF, PACK], BF16)[:], x0b_values]
-        for h, copy in enumerate((nc.vector.tensor_copy, nc.scalar.copy)):
-            copy(
-                x0_values[h].rearrange("p (q m) t -> p m t q", q=2),
-                x_raw0[:].rearrange("p t (m q) -> p m t q", q=PACK)[:, :, :, 2 * h : 2 * h + 2],
+        def difference(dst, turned, y_block):
+            nc.vector.tensor_tensor(
+                dst.rearrange("p (c i) t -> p c t i", i=PAIR),
+                turned[:].rearrange("p t (c i) -> p c t i", i=PAIR),
+                y_block.rearrange("p t (c i) -> p c t i", i=PAIR),
+                SUB,
             )
-        for h in range(2):
-            quantize(x0, h * HALF, x0_values[h], E4M3)
-        w1a_values = tile("w1a_values", [HALF, PACK], BF16, "x_raw0")
-        join(w1a_values[:], N)
-        w0.append(packed("w0b", HALF, "x0a_values"))
-        quantize(w0[1], 0, w0_values[1][:], E4M3)
-        for t in (2, 3):
-            gather_pairs(t, REST, B * N)
 
-        g0_values = tile("g0_values", [HALF, PACK], BF16)
+        def weigh(engine, wt_group, values, diff):
+            engine.tensor_tensor(values, diff, wt_group.unsqueeze(1).to_broadcast([P, BLK, PACK]), MULT)
 
-        def runs(ap):
-            return ap.rearrange("p (u i) -> p u i", i=RUN)
+        def scatter_v(j, first, sums):
+            nc.vector.tensor_copy(out_tiles[j][:].indirect(listed(first, sums.shape[1])), sums)
 
+        def scatter_s(j, first, sums):
+            nc.scalar.activation(out_tiles[j][:].indirect(listed(first, sums.shape[1])), sums, COPY)
+
+        w0_values = tile("w0_values", [N, PACK], BF16)
+        w1_planes = tile("w1_planes", [PACK, N], BF16)
         for t in range(PACK):
-            nc.gpsimd.tensor_scalar(weighted_y0[:, t], runs(y_raw0[0][:, t, :]), weights[:, 0, t : t + 1], 0.0, MULT, ADD)
-        wt0_woven = weights[:, 0, :].unsqueeze(1).to_broadcast([P, BLK, PACK])
+            nc.vector.tensor_copy(w0_values[:, :, t], planes[t][:].indirect(listed(0, N)))
+            nc.scalar.activation(w1_planes[:, t, :], planes[t][:].indirect(listed(N, N)), COPY)
+        w0 = packed("w0", N)
+        quantize(w0, 0, w0_values[:], E4M3)
+        x0_values = tile("x0_values", [R, PACK], BF16)
+        weave(nc.vector.tensor_copy, x0_values[:, block(0, 3), :], x_raw0[:, :, block(0, 3)])
+        weave(nc.scalar.copy, x0_values[:, block(3), :], x_raw0[:, :, block(3)])
+        x0 = packed("x0", R)
+        quantize(x0, 0, x0_values[:], E4M3)
+        w1_values = [tile("w1a_values", [BLK, PACK], BF16), tile("w1b_values", [N - BLK, PACK], BF16, "x_raw0")]
+        weave(nc.scalar.copy, w1_values[0][:], w1_planes[:, :, block(0)])
+        for j in range(BLOCKS - 1):
+            weave(nc.scalar.copy, w1_values[1][:, block(j), :], w1_planes[:, :, block(1 + j)])
 
-        def sigmoid(prob, scores, b, j):
-            nc.scalar.activation(prob, scores, SIGMOID, bias=bias[:, b * BLOCKS + j : b * BLOCKS + j + 1])
+        g0, g1 = packed("g0", N), packed("g1", N)
+        diff0 = [tile(f"diff0{h}", [HALF, PACK], F32) for h in range(2)]
+        diff1 = [tile(f"diff1{h}", [HALF, PACK], F32) for h in range(2)]
 
-        g_planes = tile("diff01", [2, PACK, BLK], BF16)
-        for h in range(2):
+        def pieces01(name, number, xm_op, g_op, first, copy):
+            both = bank(number, [2, HALF])
             for j in range(2):
-                scores = product(4 - 2 * h + j, w0[0], j, x0, E4M3, h * HALF, HALF)
-                prob = tile(f"first_prob{j}{h}", [2, BLK], F32)
-                sigmoid(prob[:].rearrange("p q m -> p (q m)"), scores[:], 0, j)
-                bank = turn(prob, 6 - 6 * h + j, 0, 2)
-                for t in (2 * h, 2 * h + 1):
-                    nc.vector.scalar_tensor_tensor(
-                        runs(g_planes[:, j, t, :]),
-                        runs(bank[:, t % 2, :]),
-                        weights[:, 0, t : t + 1],
-                        weighted_y0[:, t, 2 * j : 2 * j + 2, :],
-                        MULT,
-                        SUB,
-                    )
-                if h:
-                    weave(nc.vector.tensor_copy, g0_values[:, block(j), :], g_planes[:, j])
-        xm0a_values = tile("xm0a_values", [HALF, PACK], BF16, "first_prob10")
-        weave_blocks(xm0a_values[:], xm_raw0[0][:])
-        turned23 = []
-        for j in (2, 3):
-            prob = prob_tile(j)
-            scores = product(4 + j, w0[1], j - 2, x0, E4M3)
-            for h in range(2):
-                sigmoid(prob[:, 2 * h : 2 * h + 2, :].rearrange("p q m -> p (q m)"), scores[:, block(2 * h, 2)], 0, j)
-            turned23.append(turn(prob, 2 + j))
+                product(both[:, j, :], xm_op, j, g_op, E5M2, first, HALF)
+            sums = tile(name, [2, HALF], F32)
+            copy(sums[:], both[:])
+            return sums
+
+        def piece(name, number, xm_op, j, g_op, copy):
+            whole = bank(number, [N])
+            product(whole[:], xm_op, j, g_op, E5M2, 0, N)
+            sums = tile(name, [N], F32)
+            copy(sums[:], whole[:])
+            return sums
+
+        def cast_on_scalar(name, raw, place=None):
+            values = tile(name, [HALF, PACK], BF16, place)
+            for j in range(2):
+                weave(nc.scalar.copy, values[:, block(j), :], raw[:, :, block(j)])
+            return values
+
+        for j in range(2):
+            difference(diff0[0][:, block(j), :], turn(probabilities(0, j, w0, x0, j), BLOCKS + j), y_raw0[0][:, :, block(j)])
+        probs = [probabilities(0, j, w0, x0, j) for j in (2, 3)]
+        x1_values = tile("x1_values", [R, PACK], BF16)
+        weave(nc.vector.tensor_copy, x1_values[:], x_raw1[:])
+        w1 = packed("w1", N, "x0_values")
+        quantize(w1, 0, w1_values[0][:], E4M3)
+        quantize(w1, BLK, w1_values[1][:], E4M3)
+        x1 = packed("x1", R)
+        quantize(x1, 0, x1_values[:], E4M3)
+        xm0a_values = tile("xm0a_values", [HALF, PACK], BF16)
+        weave(nc.vector.tensor_copy, xm0a_values[:], xm_raw0a[:])
         xm0a = packed("xm0a", HALF)
         quantize(xm0a, 0, xm0a_values[:], E4M3)
-        quantize(g0, HALF, g0_values[:], E5M2)
-        w1b_values = tile("w1b_values", [HALF, PACK], BF16, "first_prob11")
-        join(w1b_values[:], REST)
-        w1 = packed("w1", N, "first_prob10")
-        for h, values in enumerate((w1a_values, w1b_values)):
-            quantize(w1, h * HALF, values[:], E4M3)
-        diff23 = tile("diff23", [HALF, PACK], F32, "diff01")
+        g0a_values = tile("g0a_values", [HALF, PACK], BF16, "g_values")
         for j in range(2):
-            nc.vector.tensor_tensor(
-                diff23[:, block(j), :].rearrange("p (c i) t -> p c t i", i=PAIR),
-                turned23[j][:].rearrange("p t (c i) -> p c t i", i=PAIR),
-                y_raw0[1][:, :, block(j)].rearrange("p t (c i) -> p c t i", i=PAIR),
-                SUB,
-            )
-            nc.gpsimd.tensor_tensor(g0_values[:, block(j), :], diff23[:, block(j), :], wt0_woven, MULT)
-        early_banks = [product(j, xm0a, j, g0, E5M2) for j in range(2)]
-        scatter(0, 0, piece("early0", early_banks[0], HALF, N))
+            weigh(nc.vector, weights[:, 0, :], g0a_values[:, block(j), :], diff0[0][:, block(j), :])
+        quantize(g0, 0, g0a_values[:], E5M2)
+        probs.extend(probabilities(1, j, w1, x1, (6, 7, 0, 1)[j]) for j in range(BLOCKS))
+        first0 = []
+        for j in range(2):
+            half = bank(4 + j, [HALF])
+            product(half[:], xm0a, j, g0, E5M2, 0, HALF)
+            first0.append(tile(f"first0{j}", [HALF], F32))
+            nc.scalar.copy(first0[j][:], half[:])
 
-        x1_values = [tile("x1a_values", [HALF, PACK], BF16, "x0_codes"), tile("x1b_values", [HALF, PACK], BF16)]
-        for h in range(2):
-            weave_blocks(x1_values[h][:], x_raw1[:, :, block(2 * h, 2)])
-        xm0b_values = tile("xm0b_values", [HALF, PACK], BF16)
-        weave_blocks(xm0b_values[:], xm_raw0[1][:])
-        quantize(g0, N, g0_values[:], E5M2)
-        early1 = piece("early1", early_banks[1], HALF, N, "g0_values")
-        x1 = packed("x1", R, "diff01")
-        for h in range(2):
-            quantize(x1, h * HALF, x1_values[h][:], E4M3)
-        xm0b = packed("xm0b", HALF)
-        quantize(xm0b, 0, xm0b_values[:], E4M3)
-        scatter(1, 0, early1)
-        late_banks = [product((5, 2)[j], xm0a, j, g0, E5M2, HALF) for j in range(2)]
-        scatter(0, HALF, piece("late0", late_banks[0], HALF, N, "x0_codes"))
-        scatter(1, HALF, piece("late1", late_banks[1], HALF, N))
+        once = bank(3, [P])
+        nc.tensor.transpose(once[:], wt_square[:], ident[:])
+        wt_rows = keep.tile([P, P], F32, name="wt_rows")
+        nc.scalar.copy(wt_rows[:], once[:])
+        twice = bank(3, [P])
+        nc.tensor.transpose(twice[:], wt_rows[:], ident[:])
 
-        weighted_y1 = tile("weighted_y1", [PACK, N], F32, "xm0b_values")
-        for t in range(PACK):
-            nc.gpsimd.tensor_scalar(weighted_y1[:, t, :], y_raw1[:, t, :], weights[:, 1, t : t + 1], 0.0, MULT, ADD)
-        g1_values = tile("g1_values", [HALF, PACK], BF16)
-        weighted01 = tile("weighted01", [2, PACK, BLK], F32)
-        score_banks1, turn_banks1 = (6, 7, 0, 7), (0, 7, 6, 7)
-
-        def make_g1(j, prob, weighted):
-            bank = turn(prob, turn_banks1[j])
-            for t in range(PACK):
-                nc.scalar.activation(weighted[:, t, :], bank[:, t, :], COPY, scale=weights[:, 1, t : t + 1])
-            nc.gpsimd.tensor_tensor(
-                by_lines(g1_values[:, block(j % 2), :], "p (c i) t"),
-                by_lines(weighted, "p t (c i)"),
-                by_lines(weighted_y1[:, :, block(j)], "p t (c i)"),
-                SUB,
-            )
-
-        probs1 = [probabilities(1, w1, x1, j, score_banks1[j], prob_tile(j), (PACK, 1)[j]) for j in range(2)]
-        make_g1(0, probs1[0], weighted01[:, 0])
-        late_banks.extend(product((4, 3)[j], xm0b, j, g0, E5M2, HALF) for j in range(2))
-        scatter(2, 0, piece("late2", late_banks[2], 0, N))
-        make_g1(1, probs1[1], weighted01[:, 1])
-        probs1.extend(probabilities(1, w1, x1, j, score_banks1[j], prob_tile(j)) for j in (2, 3))
-        xm1a_values = tile("xm1a_values", [HALF, PACK], BF16)
-        weave_blocks(xm1a_values[:], xm_raw1[:, :, 0:HALF])
-        xm1a = packed("xm1a", HALF)
+        for j in range(2):
+            difference(diff0[1][:, block(j), :], turn(probs[j], 6 + j), y_raw0[1][:, :, block(j)])
+        g0b_values = tile("g0b_values", [HALF, PACK], BF16)
+        for j in range(2):
+            weigh(nc.gpsimd, weights[:, 0, :], g0b_values[:, block(j), :], diff0[1][:, block(j), :])
+        xm1a_values = cast_on_scalar("xm1a_values", xm_raw1a, "g_values")
+        quantize(g0, HALF, g0b_values[:], E5M2)
+        xm1a = packed("xm1a", HALF, "diff01")
         quantize(xm1a, 0, xm1a_values[:], E4M3)
-        quantize(g1, HALF, g1_values[:], E5M2)
-        late3_and_weighted3 = tile("late3_and_weighted3", [2, N], F32, "weighted01")
-        nc.scalar.copy(late3_and_weighted3[:, 0, :], late_banks[3][:])
-        scatter(3, 0, late3_and_weighted3[:, 0, :])
-        make_g1(2, probs1[2], tile("weighted2", [PACK, BLK], F32)[:])
-        make_g1(3, probs1[3], late3_and_weighted3[:, 1, :].rearrange("p (t c) -> p t c", t=PACK))
-        scatter(0, N, piece("last0a", product(5, xm1a, 0, g1, E5M2), HALF, N))
-        xm1b_values = tile("xm1b_values", [HALF, PACK], BF16, "prob3")
-        weave_blocks(xm1b_values[:], xm_raw1[:, :, HALF:D])
-        quantize(g1, N, g1_values[:], E5M2)
-        xm1b = packed("xm1b", HALF, "xm0b_values")
+        scatter_v(0, 0, first0[0][:])
+        scatter_s(1, 0, first0[1][:])
+        xm0b_values = cast_on_scalar("xm0b_values", xm_raw0b)
+        second0 = pieces01("second0", 2, xm0a, g0, HALF, nc.scalar.copy)
+        scatter_s(1, HALF, second0[:, 1, :])
+        scatter_s(0, HALF, second0[:, 0, :])
+
+        for j in range(BLOCKS):
+            difference(diff1[j // 2][:, block(j % 2), :], turn(probs[2 + j], 4 + j), y_raw1[:, :, block(j)])
+        g1_values = tile("g1_values", [N, PACK], BF16, "g_values")
+        for j in range(2):
+            weigh(nc.gpsimd, weights[:, 1, :], g1_values[:, block(j), :], diff1[0][:, block(j), :])
+        for j in range(2):
+            weigh(nc.vector, twice[:, PACK : 2 * PACK], g1_values[:, block(2 + j), :], diff1[1][:, block(j), :])
+        quantize(g1, 0, g1_values[:], E5M2)
+        xm0b = packed("xm0b", HALF, "diff10")
+        quantize(xm0b, 0, xm0b_values[:], E4M3)
+        xm1b_values = tile("xm1b_values", [HALF, PACK], BF16, "xm0b_values")
+        weave_on_gpsimd(xm1b_values[:], xm_raw1b[:])
+        last0 = piece("last0", 0, xm1a, 0, g1, nc.vector.tensor_copy)
+        last1 = piece("last1", 1, xm1a, 1, g1, nc.scalar.copy)
+        late3 = piece("late3", 2, xm0b, 1, g0, nc.scalar.copy)
+        scatter_v(0, N, last0[:])
+        nc.sync.dma_start(out[block(0), :], out_tiles[0][:])
+        for h in range(2):
+            scatter_s(1, N + h * HALF, last1[:, block(2 * h, 2)])
+        nc.sync.dma_start(out[block(1), :], out_tiles[1][:])
+        xm1b = packed("xm1b", HALF)
         quantize(xm1b, 0, xm1b_values[:], E4M3)
-        scatter(1, N, piece("last1a", product(2, xm1a, 1, g1, E5M2), HALF, N, "weighted01"))
-
-        def finish(j, first, sums):
-            scatter(j, N + first, sums)
-            if j < BLOCKS - 1:
-                nc.sync.dma_start(out[block(j), :], out_tiles[j][:])
-            else:
-                nc.sync.dma_start(out[block(j), 0 : T // 2], out_tiles[j][:, 0 : T // 2])
-                nc.scalar.dma_start(out[block(j), T // 2 : T], out_tiles[j][:, T // 2 : T])
-
-        finish(0, HALF, piece("last0b", product(4, xm1a, 0, g1, E5M2, HALF), HALF, N))
-        finish(1, HALF, piece("last1b", product(3, xm1a, 1, g1, E5M2, HALF), HALF, N))
-        finish(2, 0, piece("last2", product(0, xm1b, 0, g1, E5M2, HALF), 0, N))
-        finish(3, 0, piece("last3", product(1, xm1b, 1, g1, E5M2, HALF), 0, N))
+        late2 = piece("late2", 0, xm0b, 0, g0, nc.vector.tensor_copy)
+        last3 = piece("last3", 4, xm1b, 1, g1, nc.vector.tensor_copy)
+        last2 = piece("last2", 5, xm1b, 0, g1, nc.vector.tensor_copy)
+        for h in range(2):
+            scatter_s(3, h * HALF, late3[:, block(2 * h, 2)])
+        for h in range(2):
+            scatter_s(3, N + h * HALF, last3[:, block(2 * h, 2)])
+        nc.scalar.dma_start(out[block(3), :], out_tiles[3][:])
+        scatter_v(2, 0, late2[:])
+        scatter_v(2, N, last2[:])
+        nc.sync.dma_start(out[block(2), :], out_tiles[2][:])

@@ -27,6 +27,7 @@ HALF = 256
 LANES = 16
 LINE = 4
 PAIR = 2
+WT_ROW = P - B
 KB_ROW = P - 1
 
 
@@ -55,6 +56,9 @@ def tile_attend_gnce_w_kb_kernel(tc, xT, wT, y, wt, kb, xm, offs, out):
         nc.vector.memset(kb_table[0:KB_ROW, 0 : T // 2 - 1], 0.0)
         nc.vector.memset(kb_table[0:KB_ROW, T // 2 - 1 : T], 0.0)
         nc.scalar.dma_start(kb_table[KB_ROW:P, :], kb[KB_ROW:P, :])
+        wt_table = keep.tile([P, R], F32, name="wt_table")
+        nc.gpsimd.memset(wt_table[0:WT_ROW, :], 0.0)
+        nc.scalar.dma_start(wt_table[WT_ROW:P, :], wt.rearrange("b r o -> b (r o)"))
         ident = keep.tile([P, P], F32, name="ident")
         make_identity(nc, ident[:])
         warm = keep.tile([P, 1], F32, name="warm")
@@ -77,7 +81,6 @@ def tile_attend_gnce_w_kb_kernel(tc, xT, wT, y, wt, kb, xm, offs, out):
         wt_square = keep.tile([P, P], F32, name="wt_square")
         nc.gpsimd.memset(wt_square[:, B * PACK : P], 0.0)
         weights = wt_square[:, 0 : B * PACK].rearrange("p (b t) -> p b t", t=PACK)
-        nc.sync.dma_start(weights, wt.rearrange("b (p t) o -> p b (t o)", t=PACK))
         xm_raw1a = load("xm_raw1a", xm[1], 0, HALF)
         y_raw0.append(load("y_raw0b", y[0], HALF, N))
         y_raw1 = load("y_raw1", y[1])
@@ -98,6 +101,17 @@ def tile_attend_gnce_w_kb_kernel(tc, xT, wT, y, wt, kb, xm, offs, out):
             for j in range(BLOCKS):
                 nc.tensor.transpose(kb_turned[:, j, :], kb_listed[:, block(b * BLOCKS + j)], ident[:])
             nc.scalar.copy(bias[:, b * BLOCKS : (b + 1) * BLOCKS], kb_turned[:, :, KB_ROW])
+
+        dealt = bank(2, [PACK, P])
+        for k in range(PACK):
+            nc.tensor.transpose(dealt[:, k, :], wt_table[:, k::PACK], ident[:])
+        nc.scalar.activation(weights, dealt[:, :, WT_ROW:P].rearrange("p t b -> p b t"), COPY, scale=-1.0)
+        once = bank(3, [P])
+        nc.tensor.transpose(once[:], wt_square[:], ident[:])
+        wt_rows = keep.tile([P, P], F32, name="wt_rows")
+        nc.scalar.copy(wt_rows[:], once[:])
+        twice = bank(3, [P])
+        nc.tensor.transpose(twice[:], wt_rows[:], ident[:])
 
         def packed(name, width, place=None):
             return tile(name + "_codes", [width], U32, place), tile(name + "_scales", [width], U8)
@@ -147,14 +161,19 @@ def tile_attend_gnce_w_kb_kernel(tc, xT, wT, y, wt, kb, xm, offs, out):
 
         def difference(dst, turned, y_block):
             nc.vector.tensor_tensor(
-                dst.rearrange("p (c i) t -> p c t i", i=PAIR),
-                turned[:].rearrange("p t (c i) -> p c t i", i=PAIR),
+                dst.rearrange("p c t -> p (c t)").rearrange("p (c t i) -> p c t i", t=PACK, i=PAIR),
                 y_block.rearrange("p t (c i) -> p c t i", i=PAIR),
+                turned[:].rearrange("p t (c i) -> p c t i", i=PAIR),
                 SUB,
             )
 
         def weigh(engine, wt_group, values, diff):
-            engine.tensor_tensor(values, diff, wt_group.unsqueeze(1).to_broadcast([P, BLK, PACK]), MULT)
+            engine.tensor_tensor(
+                values.rearrange("p (c i) t -> p c i t", i=PAIR),
+                diff.rearrange("p c t -> p (c t)").rearrange("p (c t i) -> p c i t", t=PACK, i=PAIR),
+                wt_group.unsqueeze(1).unsqueeze(1).to_broadcast([P, values.shape[1] // PAIR, PAIR, PACK]),
+                MULT,
+            )
 
         def scatter_v(j, first, sums):
             nc.vector.tensor_copy(out_tiles[j][:].indirect(listed(first, sums.shape[1])), sums)
@@ -206,7 +225,7 @@ def tile_attend_gnce_w_kb_kernel(tc, xT, wT, y, wt, kb, xm, offs, out):
 
         for j in range(2):
             difference(diff0[0][:, block(j), :], turn(probabilities(0, j, w0, x0, j), BLOCKS + j), y_raw0[0][:, :, block(j)])
-        probs = [probabilities(0, j, w0, x0, j) for j in (2, 3)]
+        probs = [probabilities(0, j, w0, x0, (2, 7)[j - 2]) for j in (2, 3)]
         x1_values = tile("x1_values", [R, PACK], BF16)
         weave(nc.vector.tensor_copy, x1_values[:], x_raw1[:])
         w1 = packed("w1", N, "x0_values")
@@ -219,23 +238,15 @@ def tile_attend_gnce_w_kb_kernel(tc, xT, wT, y, wt, kb, xm, offs, out):
         xm0a = packed("xm0a", HALF)
         quantize(xm0a, 0, xm0a_values[:], E4M3)
         g0a_values = tile("g0a_values", [HALF, PACK], BF16, "g_values")
-        for j in range(2):
-            weigh(nc.vector, weights[:, 0, :], g0a_values[:, block(j), :], diff0[0][:, block(j), :])
+        weigh(nc.vector, twice[:, 0:PACK], g0a_values[:], diff0[0][:])
         quantize(g0, 0, g0a_values[:], E5M2)
-        probs.extend(probabilities(1, j, w1, x1, (6, 7, 0, 1)[j]) for j in range(BLOCKS))
+        probs.extend(probabilities(1, j, w1, x1, (6, 7, 1, 2)[j]) for j in range(BLOCKS))
         first0 = []
         for j in range(2):
             half = bank(4 + j, [HALF])
             product(half[:], xm0a, j, g0, E5M2, 0, HALF)
             first0.append(tile(f"first0{j}", [HALF], F32))
             nc.scalar.copy(first0[j][:], half[:])
-
-        once = bank(3, [P])
-        nc.tensor.transpose(once[:], wt_square[:], ident[:])
-        wt_rows = keep.tile([P, P], F32, name="wt_rows")
-        nc.scalar.copy(wt_rows[:], once[:])
-        twice = bank(3, [P])
-        nc.tensor.transpose(twice[:], wt_rows[:], ident[:])
 
         for j in range(2):
             difference(diff0[1][:, block(j), :], turn(probs[j], 6 + j), y_raw0[1][:, :, block(j)])
@@ -258,8 +269,7 @@ def tile_attend_gnce_w_kb_kernel(tc, xT, wT, y, wt, kb, xm, offs, out):
         g1_values = tile("g1_values", [N, PACK], BF16, "g_values")
         for j in range(2):
             weigh(nc.gpsimd, weights[:, 1, :], g1_values[:, block(j), :], diff1[0][:, block(j), :])
-        for j in range(2):
-            weigh(nc.vector, twice[:, PACK : 2 * PACK], g1_values[:, block(2 + j), :], diff1[1][:, block(j), :])
+        weigh(nc.vector, twice[:, PACK : 2 * PACK], g1_values[:, block(2, 2), :], diff1[1][:])
         quantize(g1, 0, g1_values[:], E5M2)
         xm0b = packed("xm0b", HALF, "diff10")
         quantize(xm0b, 0, xm0b_values[:], E4M3)

@@ -28,6 +28,7 @@ LANES = 16
 LINE = 4
 PAIR = 2
 WT_ROW = P - B
+RUN = 32
 KB_ROW = P - 1
 
 
@@ -52,6 +53,10 @@ def tile_attend_gnce_w_kb_kernel(tc, xT, wT, y, wt, kb, xm, offs, out):
         def listed(first, count):
             return offsets[:, first // LANES : (first + count) // LANES]
 
+        warm = keep.tile([P, 2], F32, name="warm")
+        nc.gpsimd.memset(warm[:, 0:1], 0.0)
+        ident = keep.tile([P, P], F32, name="ident")
+        make_identity(nc, ident[:])
         kb_table = keep.tile([P, T], F32, name="kb_table")
         nc.vector.memset(kb_table[0:KB_ROW, 0 : T // 2 - 1], 0.0)
         nc.vector.memset(kb_table[0:KB_ROW, T // 2 - 1 : T], 0.0)
@@ -59,10 +64,7 @@ def tile_attend_gnce_w_kb_kernel(tc, xT, wT, y, wt, kb, xm, offs, out):
         wt_table = keep.tile([P, R], F32, name="wt_table")
         nc.gpsimd.memset(wt_table[0:WT_ROW, :], 0.0)
         nc.scalar.dma_start(wt_table[WT_ROW:P, :], wt.rearrange("b r o -> b (r o)"))
-        ident = keep.tile([P, P], F32, name="ident")
-        make_identity(nc, ident[:])
-        warm = keep.tile([P, 1], F32, name="warm")
-        nc.scalar.activation(warm[:], ident[:, 0:1], SIGMOID)
+        nc.scalar.activation(warm[:, 1:2], warm[:, 0:1], SIGMOID)
 
         def load(name, src, c0=0, c1=N):
             raw = tile(name, [PACK, c1 - c0], F32)
@@ -93,6 +95,19 @@ def tile_attend_gnce_w_kb_kernel(tc, xT, wT, y, wt, kb, xm, offs, out):
             nc.gpsimd.memset(zeros[:], 0.0)
             out_tiles.append(zeros)
 
+        dealt = bank(2, [PACK, P])
+        for k in range(PACK):
+            nc.tensor.transpose(dealt[:, k, :], wt_table[:, k::PACK], ident[:])
+        nc.scalar.activation(weights, dealt[:, :, WT_ROW:P].rearrange("p t b -> p b t"), COPY, scale=-1.0)
+        spread = tile("spread", [B, RUN, PACK], F32)
+        nc.scalar.copy(spread[:], weights.unsqueeze(2).to_broadcast([P, B, RUN, PACK]))
+        once = bank(3, [P])
+        nc.tensor.transpose(once[:], wt_square[:], ident[:])
+        wt_rows = keep.tile([P, P], F32, name="wt_rows")
+        nc.scalar.copy(wt_rows[:], once[:])
+        twice = bank(3, [P])
+        nc.tensor.transpose(twice[:], wt_rows[:], ident[:])
+
         kb_listed = keep.tile([P, B * N], F32, name="kb_listed")
         nc.vector.tensor_copy(kb_listed[:], kb_table[:].indirect(offsets[:]))
         bias = keep.tile([P, B * BLOCKS], F32, name="bias")
@@ -101,17 +116,6 @@ def tile_attend_gnce_w_kb_kernel(tc, xT, wT, y, wt, kb, xm, offs, out):
             for j in range(BLOCKS):
                 nc.tensor.transpose(kb_turned[:, j, :], kb_listed[:, block(b * BLOCKS + j)], ident[:])
             nc.scalar.copy(bias[:, b * BLOCKS : (b + 1) * BLOCKS], kb_turned[:, :, KB_ROW])
-
-        dealt = bank(2, [PACK, P])
-        for k in range(PACK):
-            nc.tensor.transpose(dealt[:, k, :], wt_table[:, k::PACK], ident[:])
-        nc.scalar.activation(weights, dealt[:, :, WT_ROW:P].rearrange("p t b -> p b t"), COPY, scale=-1.0)
-        once = bank(3, [P])
-        nc.tensor.transpose(once[:], wt_square[:], ident[:])
-        wt_rows = keep.tile([P, P], F32, name="wt_rows")
-        nc.scalar.copy(wt_rows[:], once[:])
-        twice = bank(3, [P])
-        nc.tensor.transpose(twice[:], wt_rows[:], ident[:])
 
         def packed(name, width, place=None):
             return tile(name + "_codes", [width], U32, place), tile(name + "_scales", [width], U8)
@@ -159,21 +163,37 @@ def tile_attend_gnce_w_kb_kernel(tc, xT, wT, y, wt, kb, xm, offs, out):
                 nc.tensor.transpose(turned[:, t, :], prob[:, t, :], ident[:])
             return turned
 
+        def paired(diff, order):
+            return diff.rearrange("p c t -> p (c t)").rearrange(f"p (c t i) -> p {order}", t=PACK, i=PAIR)
+
+        def woven(diff):
+            return diff.rearrange("p (c i) t -> p c t i", i=PAIR)
+
         def difference(dst, turned, y_block):
             nc.vector.tensor_tensor(
-                dst.rearrange("p c t -> p (c t)").rearrange("p (c t i) -> p c t i", t=PACK, i=PAIR),
+                dst,
                 y_block.rearrange("p t (c i) -> p c t i", i=PAIR),
                 turned[:].rearrange("p t (c i) -> p c t i", i=PAIR),
                 SUB,
             )
 
-        def weigh(engine, wt_group, values, diff):
-            engine.tensor_tensor(
+        def weigh_on_vector(b, values, diff):
+            nc.vector.tensor_tensor(
                 values.rearrange("p (c i) t -> p c i t", i=PAIR),
-                diff.rearrange("p c t -> p (c t)").rearrange("p (c t i) -> p c i t", t=PACK, i=PAIR),
-                wt_group.unsqueeze(1).unsqueeze(1).to_broadcast([P, values.shape[1] // PAIR, PAIR, PACK]),
+                paired(diff, "c i t"),
+                twice[:, b * PACK : (b + 1) * PACK]
+                .unsqueeze(1)
+                .unsqueeze(1)
+                .to_broadcast([P, values.shape[1] // PAIR, PAIR, PACK]),
                 MULT,
             )
+
+        def weigh_on_gpsimd(b, values, diff):
+            def rows(ap):
+                return ap.rearrange("p (r c) t -> p r (c t)", c=RUN)
+
+            weight = rows(spread[:, b, :, :]).to_broadcast([P, BLK // RUN, RUN * PACK])
+            nc.gpsimd.tensor_tensor(rows(values), rows(diff), weight, MULT)
 
         def scatter_v(j, first, sums):
             nc.vector.tensor_copy(out_tiles[j][:].indirect(listed(first, sums.shape[1])), sums)
@@ -224,7 +244,7 @@ def tile_attend_gnce_w_kb_kernel(tc, xT, wT, y, wt, kb, xm, offs, out):
             return values
 
         for j in range(2):
-            difference(diff0[0][:, block(j), :], turn(probabilities(0, j, w0, x0, j), BLOCKS + j), y_raw0[0][:, :, block(j)])
+            difference(paired(diff0[0][:, block(j), :], "c t i"), turn(probabilities(0, j, w0, x0, j), BLOCKS + j), y_raw0[0][:, :, block(j)])
         probs = [probabilities(0, j, w0, x0, (2, 7)[j - 2]) for j in (2, 3)]
         x1_values = tile("x1_values", [R, PACK], BF16)
         weave(nc.vector.tensor_copy, x1_values[:], x_raw1[:])
@@ -238,7 +258,7 @@ def tile_attend_gnce_w_kb_kernel(tc, xT, wT, y, wt, kb, xm, offs, out):
         xm0a = packed("xm0a", HALF)
         quantize(xm0a, 0, xm0a_values[:], E4M3)
         g0a_values = tile("g0a_values", [HALF, PACK], BF16, "g_values")
-        weigh(nc.vector, twice[:, 0:PACK], g0a_values[:], diff0[0][:])
+        weigh_on_vector(0, g0a_values[:], diff0[0][:])
         quantize(g0, 0, g0a_values[:], E5M2)
         probs.extend(probabilities(1, j, w1, x1, (6, 7, 1, 2)[j]) for j in range(BLOCKS))
         first0 = []
@@ -249,10 +269,10 @@ def tile_attend_gnce_w_kb_kernel(tc, xT, wT, y, wt, kb, xm, offs, out):
             nc.scalar.copy(first0[j][:], half[:])
 
         for j in range(2):
-            difference(diff0[1][:, block(j), :], turn(probs[j], 6 + j), y_raw0[1][:, :, block(j)])
+            difference(woven(diff0[1][:, block(j), :]), turn(probs[j], 6 + j), y_raw0[1][:, :, block(j)])
         g0b_values = tile("g0b_values", [HALF, PACK], BF16)
         for j in range(2):
-            weigh(nc.gpsimd, weights[:, 0, :], g0b_values[:, block(j), :], diff0[1][:, block(j), :])
+            weigh_on_gpsimd(0, g0b_values[:, block(j), :], diff0[1][:, block(j), :])
         xm1a_values = cast_on_scalar("xm1a_values", xm_raw1a, "g_values")
         quantize(g0, HALF, g0b_values[:], E5M2)
         xm1a = packed("xm1a", HALF, "diff01")
@@ -265,11 +285,12 @@ def tile_attend_gnce_w_kb_kernel(tc, xT, wT, y, wt, kb, xm, offs, out):
         scatter_s(0, HALF, second0[:, 0, :])
 
         for j in range(BLOCKS):
-            difference(diff1[j // 2][:, block(j % 2), :], turn(probs[2 + j], 4 + j), y_raw1[:, :, block(j)])
+            dst = diff1[j // 2][:, block(j % 2), :]
+            difference(woven(dst) if j < 2 else paired(dst, "c t i"), turn(probs[2 + j], 4 + j), y_raw1[:, :, block(j)])
         g1_values = tile("g1_values", [N, PACK], BF16, "g_values")
         for j in range(2):
-            weigh(nc.gpsimd, weights[:, 1, :], g1_values[:, block(j), :], diff1[0][:, block(j), :])
-        weigh(nc.vector, twice[:, PACK : 2 * PACK], g1_values[:, block(2, 2), :], diff1[1][:])
+            weigh_on_gpsimd(1, g1_values[:, block(j), :], diff1[0][:, block(j), :])
+        weigh_on_vector(1, g1_values[:, block(2, 2), :], diff1[1][:])
         quantize(g1, 0, g1_values[:], E5M2)
         xm0b = packed("xm0b", HALF, "diff10")
         quantize(xm0b, 0, xm0b_values[:], E4M3)

@@ -266,7 +266,7 @@ def tile_attend_gnce_w_kb_kernel(tc, xT, wT, y, wt, kb, xm, offs, out):
             half = bank(4 + j, [HALF])
             product(half[:], xm0a, j, g0, E5M2, 0, HALF)
             first0.append(tile(f"first0{j}", [HALF], F32))
-            nc.scalar.copy(first0[j][:], half[:])
+            (nc.vector.tensor_copy, nc.scalar.copy)[j](first0[j][:], half[:])
 
         for j in range(2):
             difference(woven(diff0[1][:, block(j), :]), turn(probs[j], 6 + j), y_raw0[1][:, :, block(j)])
@@ -296,24 +296,24 @@ def tile_attend_gnce_w_kb_kernel(tc, xT, wT, y, wt, kb, xm, offs, out):
         quantize(xm0b, 0, xm0b_values[:], E4M3)
         xm1b_values = tile("xm1b_values", [HALF, PACK], BF16, "xm0b_values")
         weave_on_gpsimd(xm1b_values[:], xm_raw1b[:])
-        last0 = piece("last0", 0, xm1a, 0, g1, nc.vector.tensor_copy)
-        last1 = piece("last1", 1, xm1a, 1, g1, nc.scalar.copy)
         late3 = piece("late3", 2, xm0b, 1, g0, nc.scalar.copy)
+        for h in range(2):
+            scatter_s(3, h * HALF, late3[:, block(2 * h, 2)])
+        late2 = piece("late2", 3, xm0b, 0, g0, nc.vector.tensor_copy)
+        last0 = piece("last0", 0, xm1a, 0, g1, nc.vector.tensor_copy)
+        last1 = piece("last1", 1, xm1a, 1, g1, nc.vector.tensor_copy)
+        xm1b = packed("xm1b", HALF)
+        quantize(xm1b, 0, xm1b_values[:], E4M3)
         scatter_v(0, N, last0[:])
         nc.sync.dma_start(out[block(0), :], out_tiles[0][:])
         for h in range(2):
             scatter_s(1, N + h * HALF, last1[:, block(2 * h, 2)])
         nc.sync.dma_start(out[block(1), :], out_tiles[1][:])
-        xm1b = packed("xm1b", HALF)
-        quantize(xm1b, 0, xm1b_values[:], E4M3)
-        late2 = piece("late2", 0, xm0b, 0, g0, nc.vector.tensor_copy)
         last3 = piece("last3", 4, xm1b, 1, g1, nc.vector.tensor_copy)
         last2 = piece("last2", 5, xm1b, 0, g1, nc.vector.tensor_copy)
         for h in range(2):
-            scatter_s(3, h * HALF, late3[:, block(2 * h, 2)])
-        for h in range(2):
             scatter_s(3, N + h * HALF, last3[:, block(2 * h, 2)])
         nc.scalar.dma_start(out[block(3), :], out_tiles[3][:])
-        scatter_v(2, 0, late2[:])
         scatter_v(2, N, last2[:])
+        scatter_v(2, 0, late2[:])
         nc.sync.dma_start(out[block(2), :], out_tiles[2][:])

@@ -134,6 +134,11 @@ def tile_attend_gnce_w_kb_kernel(tc, xT, wT, y, wt, kb, xm, offs, out):
                 in_=values.rearrange("p c t -> p (c t)"),
             )
 
+        def quantize_halves(op, first, values, fmt):
+            width = values.shape[1] // 2
+            for h in range(2):
+                quantize(op, first + h * width, values[:, h * width : (h + 1) * width, :], fmt)
+
         def product(dst, lhs, j, rhs, rhs_fmt, first, width):
             nc.tensor.matmul_mx(
                 out=dst,
@@ -204,15 +209,18 @@ def tile_attend_gnce_w_kb_kernel(tc, xT, wT, y, wt, kb, xm, offs, out):
         w0_values = tile("w0_values", [N, PACK], BF16)
         w1_planes = tile("w1_planes", [PACK, N], BF16)
         for t in range(PACK):
-            nc.vector.tensor_copy(w0_values[:, :, t], planes[t][:].indirect(listed(0, N)))
+            width = N if t < PACK - 1 else HALF
+            for first in range(0, N, width):
+                nc.vector.tensor_copy(w0_values[:, first : first + width, t], planes[t][:].indirect(listed(first, width)))
             nc.scalar.activation(w1_planes[:, t, :], planes[t][:].indirect(listed(N, N)), COPY)
         w0 = packed("w0", N)
-        quantize(w0, 0, w0_values[:], E4M3)
+        quantize_halves(w0, 0, w0_values[:], E4M3)
         x0_values = tile("x0_values", [R, PACK], BF16)
-        weave(nc.vector.tensor_copy, x0_values[:, block(0, 3), :], x_raw0[:, :, block(0, 3)])
+        for cols in (block(0, 2), block(2)):
+            weave(nc.vector.tensor_copy, x0_values[:, cols, :], x_raw0[:, :, cols])
         weave(nc.scalar.copy, x0_values[:, block(3), :], x_raw0[:, :, block(3)])
         x0 = packed("x0", R)
-        quantize(x0, 0, x0_values[:], E4M3)
+        quantize_halves(x0, 0, x0_values[:], E4M3)
         w1_values = [tile("w1a_values", [BLK, PACK], BF16), tile("w1b_values", [N - BLK, PACK], BF16, "x_raw0")]
         weave(nc.scalar.copy, w1_values[0][:], w1_planes[:, :, block(0)])
         for j in range(BLOCKS - 1):
@@ -247,19 +255,21 @@ def tile_attend_gnce_w_kb_kernel(tc, xT, wT, y, wt, kb, xm, offs, out):
             difference(paired(diff0[0][:, block(j), :], "c t i"), turn(probabilities(0, j, w0, x0, j), BLOCKS + j), y_raw0[0][:, :, block(j)])
         probs = [probabilities(0, j, w0, x0, (2, 7)[j - 2]) for j in (2, 3)]
         x1_values = tile("x1_values", [R, PACK], BF16)
-        weave(nc.vector.tensor_copy, x1_values[:], x_raw1[:])
+        for h in range(2):
+            weave(nc.vector.tensor_copy, x1_values[:, block(2 * h, 2), :], x_raw1[:, :, block(2 * h, 2)])
         w1 = packed("w1", N, "x0_values")
         quantize(w1, 0, w1_values[0][:], E4M3)
         quantize(w1, BLK, w1_values[1][:], E4M3)
         x1 = packed("x1", R)
-        quantize(x1, 0, x1_values[:], E4M3)
+        quantize_halves(x1, 0, x1_values[:], E4M3)
         xm0a_values = tile("xm0a_values", [HALF, PACK], BF16)
         weave(nc.vector.tensor_copy, xm0a_values[:], xm_raw0a[:])
         xm0a = packed("xm0a", HALF)
         quantize(xm0a, 0, xm0a_values[:], E4M3)
         g0a_values = tile("g0a_values", [HALF, PACK], BF16, "g_values")
-        weigh_on_vector(0, g0a_values[:], diff0[0][:])
-        quantize(g0, 0, g0a_values[:], E5M2)
+        for j in range(2):
+            weigh_on_vector(0, g0a_values[:, block(j), :], diff0[0][:, block(j), :])
+        quantize_halves(g0, 0, g0a_values[:], E5M2)
         probs.extend(probabilities(1, j, w1, x1, (6, 7, 1, 2)[j]) for j in range(BLOCKS))
         first0 = []
         for j in range(2):

@@ -83,8 +83,8 @@ def tile_attend_gnce_w_kb_kernel(tc, xT, wT, y, wt, kb, xm, offs, out):
         wt_square = keep.tile([P, P], F32, name="wt_square")
         nc.gpsimd.memset(wt_square[:, B * PACK : P], 0.0)
         weights = wt_square[:, 0 : B * PACK].rearrange("p (b t) -> p b t", t=PACK)
-        xm_raw1a = load("xm_raw1a", xm[1], 0, HALF)
         y_raw0.append(load("y_raw0b", y[0], HALF, N))
+        xm_raw1a = load("xm_raw1a", xm[1], 0, HALF)
         y_raw1 = load("y_raw1", y[1])
         xm_raw0b = load("xm_raw0b", xm[0], HALF, D)
         xm_raw1b = load("xm_raw1b", xm[1], HALF, D)
@@ -235,14 +235,16 @@ def tile_attend_gnce_w_kb_kernel(tc, xT, wT, y, wt, kb, xm, offs, out):
             for j in range(2):
                 product(both[:, j, :], xm_op, j, g_op, E5M2, first, HALF)
             sums = tile(name, [2, HALF], F32)
-            copy(sums[:], both[:])
+            for j in (1, 0):
+                copy(sums[:, j, :], both[:, j, :])
             return sums
 
-        def piece(name, number, xm_op, j, g_op, copy):
+        def piece(name, number, xm_op, j, g_op, copy, parts=1):
             whole = bank(number, [N])
             product(whole[:], xm_op, j, g_op, E5M2, 0, N)
             sums = tile(name, [N], F32)
-            copy(sums[:], whole[:])
+            for first in range(0, N, N // parts):
+                copy(sums[:, first : first + N // parts], whole[:, first : first + N // parts])
             return sums
 
         def cast_on_scalar(name, raw, place=None):
@@ -271,18 +273,18 @@ def tile_attend_gnce_w_kb_kernel(tc, xT, wT, y, wt, kb, xm, offs, out):
             weigh_on_vector(0, g0a_values[:, block(j), :], diff0[0][:, block(j), :])
         quantize_halves(g0, 0, g0a_values[:], E5M2)
         probs.extend(probabilities(1, j, w1, x1, (6, 7, 1, 2)[j]) for j in range(BLOCKS))
-        first0 = []
+        first_banks = [bank(4 + j, [HALF]) for j in range(2)]
         for j in range(2):
-            half = bank(4 + j, [HALF])
-            product(half[:], xm0a, j, g0, E5M2, 0, HALF)
-            first0.append(tile(f"first0{j}", [HALF], F32))
-            (nc.vector.tensor_copy, nc.scalar.copy)[j](first0[j][:], half[:])
+            product(first_banks[j][:], xm0a, j, g0, E5M2, 0, HALF)
 
         for j in range(2):
             difference(woven(diff0[1][:, block(j), :]), turn(probs[j], 6 + j), y_raw0[1][:, :, block(j)])
         g0b_values = tile("g0b_values", [HALF, PACK], BF16)
         for j in range(2):
             weigh_on_gpsimd(0, g0b_values[:, block(j), :], diff0[1][:, block(j), :])
+        first0 = [tile(f"first0{j}", [HALF], F32) for j in range(2)]
+        for j in range(2):
+            nc.vector.tensor_copy(first0[j][:], first_banks[j][:])
         xm1a_values = cast_on_scalar("xm1a_values", xm_raw1a, "g_values")
         quantize(g0, HALF, g0b_values[:], E5M2)
         xm1a = packed("xm1a", HALF, "diff01")
@@ -300,27 +302,32 @@ def tile_attend_gnce_w_kb_kernel(tc, xT, wT, y, wt, kb, xm, offs, out):
         g1_values = tile("g1_values", [N, PACK], BF16, "g_values")
         for j in range(2):
             weigh_on_gpsimd(1, g1_values[:, block(j), :], diff1[0][:, block(j), :])
-        weigh_on_vector(1, g1_values[:, block(2, 2), :], diff1[1][:])
-        quantize(g1, 0, g1_values[:], E5M2)
+        for j in range(2):
+            weigh_on_vector(1, g1_values[:, block(2 + j), :], diff1[1][:, block(j), :])
+        quantize_halves(g1, 0, g1_values[:], E5M2)
         xm0b = packed("xm0b", HALF, "diff10")
         quantize(xm0b, 0, xm0b_values[:], E4M3)
         xm1b_values = tile("xm1b_values", [HALF, PACK], BF16, "xm0b_values")
         weave_on_gpsimd(xm1b_values[:], xm_raw1b[:])
-        late3 = piece("late3", 2, xm0b, 1, g0, nc.scalar.copy)
+        late3 = piece("late3", 2, xm0b, 1, g0, nc.scalar.copy, 2)
         for h in range(2):
             scatter_s(3, h * HALF, late3[:, block(2 * h, 2)])
         late2 = piece("late2", 3, xm0b, 0, g0, nc.vector.tensor_copy)
         last0 = piece("last0", 0, xm1a, 0, g1, nc.vector.tensor_copy)
-        last1 = piece("last1", 1, xm1a, 1, g1, nc.vector.tensor_copy)
+        last1_bank = bank(1, [N])
+        product(last1_bank[:], xm1a, 1, g1, E5M2, 0, N)
+        last1 = tile("last1", [N], F32)
+        nc.vector.tensor_copy(last1[:, 0:HALF], last1_bank[:, 0:HALF])
         xm1b = packed("xm1b", HALF)
         quantize(xm1b, 0, xm1b_values[:], E4M3)
         scatter_v(0, N, last0[:])
         nc.sync.dma_start(out[block(0), :], out_tiles[0][:])
+        nc.vector.tensor_copy(last1[:, HALF:N], last1_bank[:, HALF:N])
         for h in range(2):
             scatter_s(1, N + h * HALF, last1[:, block(2 * h, 2)])
         nc.sync.dma_start(out[block(1), :], out_tiles[1][:])
-        last3 = piece("last3", 4, xm1b, 1, g1, nc.vector.tensor_copy)
         last2 = piece("last2", 5, xm1b, 0, g1, nc.vector.tensor_copy)
+        last3 = piece("last3", 4, xm1b, 1, g1, nc.vector.tensor_copy)
         for h in range(2):
             scatter_s(3, N + h * HALF, last3[:, block(2 * h, 2)])
         nc.scalar.dma_start(out[block(3), :], out_tiles[3][:])

from contextlib import ExitStack

import concourse.mybir as mybir
from concourse.masks import make_identity

B, N, T, D, R = 2, 512, 2048, 512, 512
FLOPS = 2 * 2 * B * N * D * R

F32 = mybir.dt.float32
BF16 = mybir.dt.bfloat16
U32 = mybir.dt.uint32
U16 = mybir.dt.uint16
U8 = mybir.dt.uint8
E4M3 = mybir.dt.float8_e4m3fn_x4
E5M2 = mybir.dt.float8_e5m2_x4
SIGMOID = mybir.ActivationFunctionType.Sigmoid
COPY = mybir.ActivationFunctionType.Copy
MULT = mybir.AluOpType.mult
ADD = mybir.AluOpType.add
SUB = mybir.AluOpType.subtract

P = 128
PACK = 4
BLK = 128
BLOCKS = 4
HALF = 256
LANES = 16
LINE = 4
PAIR = 2
WT_ROW = P - B
RUN = 32
KB_ROW = P - 1


def tile_attend_gnce_w_kb_kernel(tc, xT, wT, y, wt, kb, xm, offs, out):
    nc = tc.nc
    with ExitStack() as ctx:
        keep = ctx.enter_context(tc.tile_pool(name="keep", bufs=1))
        psum = ctx.enter_context(tc.psum_pool(name="psum", bufs=1))

        def tile(name, shape, dtype, place=None):
            return keep.tile([P] + shape, dtype, name=name, tag=place or name, align_bytes=64)

        def bank(number, shape):
            return psum.tile([P] + shape, F32, name=f"bank{number}", tag=f"bank{number}")

        def block(j, count=1):
            return slice(j * BLK, (j + count) * BLK)

        offsets = keep.tile([P, B * N // LANES], U16, name="offsets")
        nc.sync.dma_start(offsets[:], offs)

        def listed(first, count):
            return offsets[:, first // LANES : (first + count) // LANES]

        warm = keep.tile([P, 2], F32, name="warm")
        nc.gpsimd.memset(warm[:, 0:1], 0.0)
        ident = keep.tile([P, P], F32, name="ident")
        make_identity(nc, ident[:])
        kb_table = keep.tile([P, T], F32, name="kb_table")
        nc.vector.memset(kb_table[0:KB_ROW, 0 : T // 2 - 1], 0.0)
        nc.vector.memset(kb_table[0:KB_ROW, T // 2 - 1 : T], 0.0)
        nc.scalar.dma_start(kb_table[KB_ROW:P, :], kb[KB_ROW:P, :])
        wt_table = keep.tile([P, R], F32, name="wt_table")
        nc.gpsimd.memset(wt_table[0:WT_ROW, :], 0.0)
        nc.scalar.dma_start(wt_table[WT_ROW:P, :], wt.rearrange("b r o -> b (r o)"))
        nc.scalar.activation(warm[:, 1:2], warm[:, 0:1], SIGMOID)

        def load(name, src, c0=0, c1=N):
            raw = tile(name, [PACK, c1 - c0], F32)
            nc.sync.dma_start(raw[:], src.rearrange("(p t) c -> p t c", t=PACK)[:, :, c0:c1])
            return raw

        planes = []
        for t in range(PACK):
            plane = keep.tile([P, T], F32, name=f"plane{t}")
            nc.sync.dma_start(plane[:], wT.rearrange("(p t) c -> p t c", t=PACK)[:, t, :])
            planes.append(plane)
        x_raw0 = load("x_raw0", xT[0])
        x_raw1 = load("x_raw1", xT[1])
        xm_raw0a = load("xm_raw0a", xm[0], 0, HALF)
        y_raw0 = [load("y_raw0a", y[0], 0, HALF)]
        wt_square = keep.tile([P, P], F32, name="wt_square")
        nc.gpsimd.memset(wt_square[:, B * PACK : P], 0.0)
        weights = wt_square[:, 0 : B * PACK].rearrange("p (b t) -> p b t", t=PACK)
        y_raw0.append(load("y_raw0b", y[0], HALF, N))
        xm_raw1a = load("xm_raw1a", xm[1], 0, HALF)
        y_raw1 = load("y_raw1", y[1])
        xm_raw0b = load("xm_raw0b", xm[0], HALF, D)
        xm_raw1b = load("xm_raw1b", xm[1], HALF, D)

        out_tiles = []
        for j in range(BLOCKS):
            zeros = keep.tile([P, T], F32, name=f"out{j}")
            nc.gpsimd.memset(zeros[:], 0.0)
            out_tiles.append(zeros)

        dealt = bank(2, [PACK, P])
        for k in range(PACK):
            nc.tensor.transpose(dealt[:, k, :], wt_table[:, k::PACK], ident[:])
        nc.scalar.activation(weights, dealt[:, :, WT_ROW:P].rearrange("p t b -> p b t"), COPY, scale=-1.0)
        spread = tile("spread", [B, RUN, PACK], F32)
        nc.scalar.copy(spread[:], weights.unsqueeze(2).to_broadcast([P, B, RUN, PACK]))
        once = bank(3, [P])
        nc.tensor.transpose(once[:], wt_square[:], ident[:])
        wt_rows = keep.tile([P, P], F32, name="wt_rows")
        nc.scalar.copy(wt_rows[:], once[:])
        twice = bank(3, [P])
        nc.tensor.transpose(twice[:], wt_rows[:], ident[:])

        kb_listed = keep.tile([P, B * N], F32, name="kb_listed")
        nc.vector.tensor_copy(kb_listed[:], kb_table[:].indirect(offsets[:]))
        bias = keep.tile([P, B * BLOCKS], F32, name="bias")
        for b in range(B):
            kb_turned = bank(b, [BLOCKS, BLK])
            for j in range(BLOCKS):
                nc.tensor.transpose(kb_turned[:, j, :], kb_listed[:, block(b * BLOCKS + j)], ident[:])
            nc.scalar.copy(bias[:, b * BLOCKS : (b + 1) * BLOCKS], kb_turned[:, :, KB_ROW])

        def packed(name, width, place=None):
            return tile(name + "_codes", [width], U32, place), tile(name + "_scales", [width], U8)

        def weave(copy, dst, src):
            copy(dst.rearrange("p (c i) t -> p c t i", i=LINE), src.rearrange("p t (c i) -> p c t i", i=LINE))

        def weave_on_gpsimd(dst, src):
            nc.gpsimd.tensor_scalar(dst, src.rearrange("p t c -> p c t"), 1.0, 0.0, MULT, ADD)

        def quantize(op, first, values, fmt):
            cols = slice(first, first + values.shape[1])
            nc.vector.quantize_mx(
                out=op[0][:, cols].bitcast(fmt),
                scales=op[1][:, cols],
                in_=values.rearrange("p c t -> p (c t)"),
            )

        def quantize_halves(op, first, values, fmt):
            width = values.shape[1] // 2
            for h in range(2):
                quantize(op, first + h * width, values[:, h * width : (h + 1) * width, :], fmt)

        def product(dst, lhs, j, rhs, rhs_fmt, first, width):
            nc.tensor.matmul_mx(
                out=dst,
                lhsT=lhs[0][:, block(j)].bitcast(E4M3),
                lhsT_scale=lhs[1][:, block(j)],
                rhs=rhs[0][:, first : first + width].bitcast(rhs_fmt),
                rhs_scale=rhs[1][:, first : first + width],
                start=True,
                stop=True,
            )

        def probabilities(b, j, w_op, x_op, number):
            scores = bank(number, [R])
            product(scores[:], w_op, j, x_op, E4M3, 0, R)
            prob = tile(f"prob{b}{j}", [PACK, BLK], F32)
            nc.scalar.activation(
                prob[:],
                scores[:].rearrange("p (m t) -> p t m", t=PACK),
                SIGMOID,
                bias=bias[:, b * BLOCKS + j : b * BLOCKS + j + 1],
            )
            return prob

        def turn(prob, number):
            turned = bank(number, [PACK, BLK])
            for t in range(PACK):
                nc.tensor.transpose(turned[:, t, :], prob[:, t, :], ident[:])
            return turned

        def paired(diff, order):
            return diff.rearrange("p c t -> p (c t)").rearrange(f"p (c t i) -> p {order}", t=PACK, i=PAIR)

        def woven(diff):
            return diff.rearrange("p (c i) t -> p c t i", i=PAIR)

        def difference(dst, turned, y_block):
            nc.vector.tensor_tensor(
                dst,
                y_block.rearrange("p t (c i) -> p c t i", i=PAIR),
                turned[:].rearrange("p t (c i) -> p c t i", i=PAIR),
                SUB,
            )

        def weigh_on_vector(b, values, diff):
            nc.vector.tensor_tensor(
                values.rearrange("p (c i) t -> p c i t", i=PAIR),
                paired(diff, "c i t"),
                twice[:, b * PACK : (b + 1) * PACK]
                .unsqueeze(1)
                .unsqueeze(1)
                .to_broadcast([P, values.shape[1] // PAIR, PAIR, PACK]),
                MULT,
            )

        def weigh_on_gpsimd(b, values, diff):
            def rows(ap):
                return ap.rearrange("p (r c) t -> p r (c t)", c=RUN)

            weight = rows(spread[:, b, :, :]).to_broadcast([P, BLK // RUN, RUN * PACK])
            nc.gpsimd.tensor_tensor(rows(values), rows(diff), weight, MULT)

        def scatter_v(j, first, sums):
            nc.vector.tensor_copy(out_tiles[j][:].indirect(listed(first, sums.shape[1])), sums)

        def scatter_s(j, first, sums):
            nc.scalar.activation(out_tiles[j][:].indirect(listed(first, sums.shape[1])), sums, COPY)

        w0_values = tile("w0_values", [N, PACK], BF16)
        w1_planes = tile("w1_planes", [PACK, N], BF16)
        for t in range(PACK):
            width = N if t < PACK - 1 else HALF
            for first in range(0, N, width):
                nc.vector.tensor_copy(w0_values[:, first : first + width, t], planes[t][:].indirect(listed(first, width)))
            nc.scalar.activation(w1_planes[:, t, :], planes[t][:].indirect(listed(N, N)), COPY)
        w0 = packed("w0", N)
        quantize_halves(w0, 0, w0_values[:], E4M3)
        x0_values = tile("x0_values", [R, PACK], BF16)
        for cols in (block(0, 2), block(2)):
            weave(nc.vector.tensor_copy, x0_values[:, cols, :], x_raw0[:, :, cols])
        weave(nc.scalar.copy, x0_values[:, block(3), :], x_raw0[:, :, block(3)])
        x0 = packed("x0", R)
        quantize_halves(x0, 0, x0_values[:], E4M3)
        w1_values = [tile("w1a_values", [BLK, PACK], BF16), tile("w1b_values", [N - BLK, PACK], BF16, "x_raw0")]
        weave(nc.scalar.copy, w1_values[0][:], w1_planes[:, :, block(0)])
        for j in range(BLOCKS - 1):
            weave(nc.scalar.copy, w1_values[1][:, block(j), :], w1_planes[:, :, block(1 + j)])

        g0, g1 = packed("g0", N), packed("g1", N)
        diff0 = [tile(f"diff0{h}", [HALF, PACK], F32) for h in range(2)]
        diff1 = [tile(f"diff1{h}", [HALF, PACK], F32) for h in range(2)]

        def pieces01(name, number, xm_op, g_op, first, copy):
            both = bank(number, [2, HALF])
            for j in range(2):
                product(both[:, j, :], xm_op, j, g_op, E5M2, first, HALF)
            sums = tile(name, [2, HALF], F32)
            for j in (1, 0):
                copy(sums[:, j, :], both[:, j, :])
            return sums

        def piece(name, number, xm_op, j, g_op, copy, parts=1):
            whole = bank(number, [N])
            product(whole[:], xm_op, j, g_op, E5M2, 0, N)
            sums = tile(name, [N], F32)
            for first in range(0, N, N // parts):
                copy(sums[:, first : first + N // parts], whole[:, first : first + N // parts])
            return sums

        def cast_on_scalar(name, raw, place=None):
            values = tile(name, [HALF, PACK], BF16, place)
            for j in range(2):
                weave(nc.scalar.copy, values[:, block(j), :], raw[:, :, block(j)])
            return values

        for j in range(2):
            difference(paired(diff0[0][:, block(j), :], "c t i"), turn(probabilities(0, j, w0, x0, j), BLOCKS + j), y_raw0[0][:, :, block(j)])
        probs = [probabilities(0, j, w0, x0, (2, 7)[j - 2]) for j in (2, 3)]
        x1_values = tile("x1_values", [R, PACK], BF16)
        for h in range(2):
            weave(nc.vector.tensor_copy, x1_values[:, block(2 * h, 2), :], x_raw1[:, :, block(2 * h, 2)])
        w1 = packed("w1", N, "x0_values")
        quantize(w1, 0, w1_values[0][:], E4M3)
        quantize(w1, BLK, w1_values[1][:], E4M3)
        x1 = packed("x1", R)
        quantize_halves(x1, 0, x1_values[:], E4M3)
        xm0a_values = tile("xm0a_values", [HALF, PACK], BF16)
        weave(nc.vector.tensor_copy, xm0a_values[:], xm_raw0a[:])
        xm0a = packed("xm0a", HALF)
        quantize(xm0a, 0, xm0a_values[:], E4M3)
        g0a_values = tile("g0a_values", [HALF, PACK], BF16, "g_values")
        for j in range(2):
            weigh_on_vector(0, g0a_values[:, block(j), :], diff0[0][:, block(j), :])
        quantize_halves(g0, 0, g0a_values[:], E5M2)
        probs.extend(probabilities(1, j, w1, x1, (6, 7, 1, 2)[j]) for j in range(BLOCKS))
        first_banks = [bank(4 + j, [HALF]) for j in range(2)]
        for j in range(2):
            product(first_banks[j][:], xm0a, j, g0, E5M2, 0, HALF)

        for j in range(2):
            difference(woven(diff0[1][:, block(j), :]), turn(probs[j], 6 + j), y_raw0[1][:, :, block(j)])
        g0b_values = tile("g0b_values", [HALF, PACK], BF16)
        for j in range(2):
            weigh_on_gpsimd(0, g0b_values[:, block(j), :], diff0[1][:, block(j), :])
        first0 = [tile(f"first0{j}", [HALF], F32) for j in range(2)]
        for j in range(2):
            nc.vector.tensor_copy(first0[j][:], first_banks[j][:])
        xm1a_values = cast_on_scalar("xm1a_values", xm_raw1a, "g_values")
        quantize(g0, HALF, g0b_values[:], E5M2)
        xm1a = packed("xm1a", HALF, "diff01")
        quantize(xm1a, 0, xm1a_values[:], E4M3)
        scatter_v(0, 0, first0[0][:])
        scatter_s(1, 0, first0[1][:])
        xm0b_values = cast_on_scalar("xm0b_values", xm_raw0b)
        second0 = pieces01("second0", 2, xm0a, g0, HALF, nc.scalar.copy)
        scatter_s(1, HALF, second0[:, 1, :])
        scatter_s(0, HALF, second0[:, 0, :])

        for j in range(BLOCKS):
            dst = diff1[j // 2][:, block(j % 2), :]
            difference(woven(dst) if j < 2 else paired(dst, "c t i"), turn(probs[2 + j], 4 + j), y_raw1[:, :, block(j)])
        g1_values = tile("g1_values", [N, PACK], BF16, "g_values")
        for j in range(2):
            weigh_on_gpsimd(1, g1_values[:, block(j), :], diff1[0][:, block(j), :])
        for j in range(2):
            weigh_on_vector(1, g1_values[:, block(2 + j), :], diff1[1][:, block(j), :])
        quantize_halves(g1, 0, g1_values[:], E5M2)
        xm0b = packed("xm0b", HALF, "diff10")
        quantize(xm0b, 0, xm0b_values[:], E4M3)
        xm1b_values = tile("xm1b_values", [HALF, PACK], BF16, "xm0b_values")
        weave_on_gpsimd(xm1b_values[:], xm_raw1b[:])
        late3 = piece("late3", 2, xm0b, 1, g0, nc.scalar.copy, 2)
        for h in range(2):
            scatter_s(3, h * HALF, late3[:, block(2 * h, 2)])
        late2 = piece("late2", 3, xm0b, 0, g0, nc.vector.tensor_copy)
        last0 = piece("last0", 0, xm1a, 0, g1, nc.vector.tensor_copy)
        last1_bank = bank(1, [N])
        product(last1_bank[:], xm1a, 1, g1, E5M2, 0, N)
        last1 = tile("last1", [N], F32)
        nc.vector.tensor_copy(last1[:, 0:HALF], last1_bank[:, 0:HALF])
        xm1b = packed("xm1b", HALF)
        quantize(xm1b, 0, xm1b_values[:], E4M3)
        scatter_v(0, N, last0[:])
        nc.sync.dma_start(out[block(0), :], out_tiles[0][:])
        nc.vector.tensor_copy(last1[:, HALF:N], last1_bank[:, HALF:N])
        for h in range(2):
            scatter_s(1, N + h * HALF, last1[:, block(2 * h, 2)])
        nc.sync.dma_start(out[block(1), :], out_tiles[1][:])
        last2 = piece("last2", 5, xm1b, 0, g1, nc.vector.tensor_copy)
        last3 = piece("last3", 4, xm1b, 1, g1, nc.vector.tensor_copy)
        for h in range(2):
            scatter_s(3, N + h * HALF, last3[:, block(2 * h, 2)])
        nc.scalar.dma_start(out[block(3), :], out_tiles[3][:])
        scatter_v(2, N, last2[:])
        scatter_v(2, 0, late2[:])
        nc.sync.dma_start(out[block(2), :], out_tiles[2][:])
